import numpy as np, ml_dtypes
CORES = [51,54,179,182]
N = 4
BF = ml_dtypes.bfloat16
L, W, E, D, RO, EPS = 128, 1792, 2048, 256, 5, 5
def pack(S, EF, OT, Q, K, P, G, M):
    bf = lambda a: np.ascontiguousarray(a.reshape(N, 128, -1)).astype(np.float32).astype(BF)
    li = lambda a: np.ascontiguousarray(a.transpose(0, 1, 3, 2, 4)).reshape(N, 128, 3 * L).astype(np.int32)
    return {"st0": bf(S), "ef": bf(EF), "ot": bf(OT), "qn": li(Q), "qk": li(K), "tu": np.ascontiguousarray(P.reshape(N, 8, 3 * L)).astype(np.int32), "gl": bf(G), "rm": bf(M)}
def with15(v, last):
    return np.concatenate([v, np.broadcast_to(last, v.shape[:2] + (1, v.shape[3]))], axis=2).astype(np.int64)
def base(rng):
    cen = rng.integers(8, 56, (N, 8, 15, 1))
    def near(n):
        return np.clip(np.rint(cen + rng.standard_normal((N, 8, 15, n), dtype=np.float32) * rng.choice(np.array([1.5, 3.0, 6.0, 16.0]), (N, 8, 1, n))), 0, 63)
    S = with15(near(W), rng.random((N, 8, 1, W)) < rng.choice(np.array([0.1, 0.3, 0.5, 0.85]), (N, 8, 1, 1))); S[:, :, 15, W - 1] = 1
    EF = with15(np.rint((2 * rng.random((N, 8, 15, E)) - 1) * rng.integers(1, 9, (N, 8, 1, E))), 0)
    OT = rng.integers(0, 256, (N, 8, 16, D)); Q = rng.integers(0, W, (N, 8, 3, 16, L)); K = rng.integers(0, 946, (N, 8, 3, 16, L))
    kind = rng.integers(0, 3, (N, 8, 1, 1, L)); K = np.where(kind == 1, np.maximum(K, 300), np.where(kind == 2, K - K % 64, K))
    P = rng.integers(-3, 4, (N, 8, 3, L)); G = with15(near(L), 0); M = with15(rng.random((N, 8, 15, 1)) < 0.5, 0)
    for q in range(N):
        for g in range(8):
            Q[q, g, :, :, 5::16] = rng.choice(np.flatnonzero(S[q, g, 15]), (3, 16, L // 16))
    return S, EF, OT, Q, K, P, G, M
def setup_inputs(rng):
    return pack(*base(rng))
def setup_inputs_spread(rng):
    def un(hi, shape, eshape):
        return np.minimum(((hi + 1) * rng.random(shape) ** np.exp2(rng.integers(-2, 4, eshape))).astype(np.int64), hi)
    S = with15(un(63, (N, 8, 15, W), (N, 8, 1, W)), rng.random((N, 8, 1, W)) < rng.random((N, 8, 1, 1)))
    EF = with15(un(8, (N, 8, 15, E), (N, 8, 1, E)) * (2 * rng.integers(0, 2, (N, 8, 15, E)) - 1), 0)
    OT = un(255, (N, 8, 16, D), (N, 8, 1, D)); Q = un(W - 1, (N, 8, 3, 16, L), (N, 8, 3, 1, L)); K = un(945, (N, 8, 3, 16, L), (N, 8, 3, 1, L))
    P = rng.integers(-6, 7, (N, 8, 3, L)); G = with15(un(63, (N, 8, 15, L), (N, 8, 1, L)), 0)
    M = with15(rng.random((N, 8, 15, 1)) < rng.random((N, 8, 1, 1)), 0)
    return pack(S, EF, OT, Q, K, P, G, M)
def setup_inputs_ends(rng):
    def bits(n):
        r = rng.integers(0, 4, (N, 8, 1, n))
        return np.where(r == 0, 0, np.where(r == 1, 1, rng.integers(0, 2, (N, 8, 15, n))))
    S = with15(63 * bits(W), rng.integers(0, 2, (N, 8, 1, W))); EF = with15(16 * bits(E) - 8, 0); G = with15(63 * bits(L), 0)
    OT = 255 * rng.integers(0, 2, (N, 8, 16, D)); K = 945 * rng.integers(0, 2, (N, 8, 3, 16, L)); P = 12 * rng.integers(0, 2, (N, 8, 3, L)) - 6
    Q = np.where(rng.random((N, 8, 3, 16, L)) < 0.8, (W - 1) * rng.integers(0, 2, (N, 8, 3, 16, L)), rng.integers(0, W, (N, 8, 3, 16, L)))
    M = with15(rng.integers(0, 2, (N, 8, 15, 1)), 0)
    q, g = N - 1, 7
    S[q, g, :15, W - 1] = 63; S[q, g, :15, 0] = 0; S[q, g, 15, W - 1] = 0; S[q, g, 15, 0] = 0; EF[q, g, :15, E - 1] = 8; EF[q, g, :15, 0] = -8
    Q[q, g, :, :, L - 4:] = 0; Q[q, g, :, 15, L - 1] = W - 1; Q[q, g, :, 14, L - 2] = W - 1
    K[q, g, :, :, L - 2:] = 945; K[q, g, :, 15, L - 1] = 0; K[q, g, :, 14:, L - 2] = 0; K[q, g, :, :, L - 3] = 0; K[q, g, :, :, L - 4] = 945
    G[q, g, :15, L - 1] = 0; G[q, g, :15, L - 2] = 63; G[q, g, :15, L - 3] = 0; G[q, g, :15, L - 4] = 63
    P[q, g, :, L - 4:] = -6; P[q, g, 0, L - 2] = 6
    M[q, g, :15, 0] = 1; OT[q, g, :, 15120 % D] = 255
    return pack(S, EF, OT, Q, K, P, G, M)
def setup_inputs_corners(rng):
    S, EF, OT, Q, K, P, G, M = base(rng); i = np.arange(L); n8 = L // 8
    EF[:, 1::2] = np.take_along_axis(EF[:, 1::2], rng.integers(0, 4, (N, 4, 1, E)), 3)
    for q in range(N):
        for g in range(8):
            mode = (q + g) % 4; B = Q[q, g]; C = K[q, g]; c = (0, W - 1, L, int(rng.integers(0, W)))[int(rng.integers(0, 4))]
            S[q, g, 15] = 0 if mode == 0 else 1 if mode < 3 else (rng.random(W) < 0.5)
            B[:, :, 0::8] = rng.integers(0, W, (3, 1, n8)); B[:, :, 1::8] = L * rng.integers(0, 2 * RO, (3, 16, n8)) + i[1::8]
            B[:, :, 2::8] = (W - 1) * rng.integers(0, 2, (3, 16, n8)); B[:, :, 6::8] = L * rng.integers(0, 2 * RO, (3, 16, n8)) + i[6::8] + 1
            C[:, :, 3::8] = C[:, :1, 3::8].copy(); C[:, :, 4::8] = 945 * rng.integers(0, 2, (3, 16, n8)); C[:, :15, 5::8] = 945
            if mode == 2:
                S[q, g, 15, c] = 0; sl = rng.choice(np.array([0, 7, 15]), (3, L)); o = i[rng.random(L) < 0.5]
                for l in range(3): B[l, sl[l, o], o] = c
            m = (g // 2 + q) % 4
            if m < 3: M[q, g, :15, 0] = 0 if m != 1 else 1
            if m == 2: M[q, g, int(rng.integers(0, 15)), 0] = 1
            P[q, g, :, 0::4] = P[q, g, :1, 0::4].copy(); P[q, g, :, 1::4] = 12 * rng.integers(0, 2, (3, L // 4)) - 6; P[q, g, 2, 2::4] = P[q, g, 1, 2::4]
            G[q, g, :15, 3::8] = S[q, g][:15, B[0, 0, 3::8]]
    return pack(S, EF, OT, Q, K, P, G, M)
def setup_inputs_crowd(rng):
    S, EF, OT, Q, K, P, G, M = base(rng); i = np.arange(L); first = int(rng.integers(0, 8)); flip = int(rng.integers(0, 2))
    o = [int(g) for g in rng.permutation(8) if g not in (first, 7 - first)]
    for m, g in enumerate((first, o[0], 7 - first, o[1], o[2], o[3])):
        if m > 3: c = int(rng.integers(L, W - 2))
        elif m // 2 == flip: c = int(rng.integers(L, RO * L - 2))
        else: c = int(rng.integers(2 * RO * L, W - 2))
        z = L - 1 if m == 1 else int(rng.integers(0, L))
        S[:, g, 15, c:c + 3] = 0; P[:, g, 0] = -6; P[:, g, 1:] = 6
        if m < 4:
            EF[:, g, :15] = rng.integers(1, 9, (N, 15, E)); G[:, g, :15] = 63
            if m < 2: Q[:, g, 0] = c
            else:
                sl = rng.integers(0, 16, L); K[:, g, 0] = 945; K[:, g, 0, sl, i] = 0; Q[:, g, 0, sl, i] = c
            if m % 2 == 1:
                Q[:, g, 0, :, z] = c + 1; G[:, g, :15, z] = 0
        else:
            Q[:, g, 0] = c + rng.integers(0, 3, (N, 16, L))
            if m == 5:
                EF[:, g, :15] = rng.integers(1, 9, (N, 15, E)); G[:, g, :15] = 0; P[:, g, 0, ::2] = 6
    return pack(S, EF, OT, Q, K, P, G, M)
def check_inputs(d):
    bad = []
    for k, lo, hi in (("st0", 0, 63), ("ef", -8, 8), ("ot", 0, 255), ("qn", 0, W - 1), ("qk", 0, 945), ("tu", -6, 6), ("gl", 0, 63), ("rm", 0, 1)):
        v = np.asarray(d[k]).astype(np.float64)
        if not (np.min(v) >= lo and np.max(v) <= hi): bad.append("range of " + k)
        elif np.any(v != np.rint(v)): bad.append("whole numbers in " + k)
    for k in ("st0", "ef", "gl", "rm"):
        v = np.asarray(d[k]).astype(np.float64).reshape(N, 8, 16, -1)[:, :, 15]
        if not (np.min(v) >= 0 and np.max(v) <= (1 if k == "st0" else 0)): bad.append("last row of the groups in " + k)
    return bad
def ints(a):
    return a.astype(np.float32).astype(np.int32)
def reference(st0, ef, ot, qn, qk, tu, gl, rm):
    S = ints(st0).reshape(N, 8, 16, W); EF = ints(ef).reshape(N, 8, 16, E)[:, :, :15]; OT = ints(ot).reshape(N, 8, 16, D); M = ints(rm).reshape(N, 8, 16, 1, 1)[:, :, :15]
    Q = np.ascontiguousarray(ints(qn).reshape(N, 8, 16, 3, L).transpose(0, 1, 3, 2, 4)); K = np.ascontiguousarray(ints(qk).reshape(N, 8, 16, 3, L).transpose(0, 1, 3, 2, 4))
    P = ints(tu).reshape(N, 8, 3, L); G = ints(gl).reshape(N, 8, 16, 1, L)[:, :, :15]; A = np.zeros((N, 8, 1, 1), np.int64)
    cf = (2 * np.arange(15) + 1)[:, None]; kk = np.arange(16)[:, None]; lane = np.arange(L)
    def hs(y, g):
        dd = np.abs(y - g)
        return np.stack([np.add.reduce(dd, axis=2), 16 * np.add.reduce((dd > EPS).astype(np.int32), axis=2), np.add.reduce(dd * M, axis=2)], axis=2)
    for t in range(RO):
        if t > 0:
            Q, K, P, G = (np.roll(a, 1, axis=0) for a in (Q, K, P, G))
        j = np.argmin(P, axis=2); jj = j[:, :, None, None, :]
        q = np.take_along_axis(Q, jj, 2)[:, :, 0]; key = np.take_along_axis(K, jj, 2)[:, :, 0]
        s = np.take_along_axis(S, q.reshape(N, 8, 1, 16 * L), 3).reshape(N, 8, 16, 16, L)
        key = np.where(s[:, :, 15] == 1, 1023, key)
        k0 = np.argmin(key, axis=2)
        x = np.take_along_axis(s, k0[:, :, None, None, :], 3)[:, :, :15, 0]; xn = np.take_along_axis(q, k0[:, :, None], 2)[:, :, 0]
        u = np.add.reduce(cf * x, axis=2); v = np.add.reduce(np.maximum.reduce(s[:, :, :15], axis=3), axis=2)
        o = np.take_along_axis(OT, ((u + v) & (D - 1))[:, :, None, :], 3)
        n = (((o * u[:, :, None]) >> 5) + o + 37 * kk + A) & (E - 1)
        e = np.take_along_axis(EF, n.reshape(N, 8, 1, 16 * L), 3).reshape(N, 8, 15, 16, L)
        y = np.clip(x[:, :, :, None] + e, 0, 63)
        h = hs(y, G); hx = hs(x[:, :, :, None], G)[:, :, :, 0]
        ha = np.take_along_axis(h, jj, 2)[:, :, 0]; hb = np.take_along_axis(h, (jj + 1) % 3, 2)[:, :, 0]
        a = np.argmin(ha, axis=2); b = np.argmin(hb, axis=2)
        ya = np.take_along_axis(y, a[:, :, None, None, :], 3)[:, :, :, 0]; yb = np.take_along_axis(y, b[:, :, None, None, :], 3)[:, :, :, 0]
        np.put_along_axis(S[:, :, 15], xn, 1, 2)
        S[:, :, :15, t * L:(t + 1) * L] = ya; S[:, :, 15, t * L:(t + 1) * L] = 0
        S[:, :, :15, (RO + t) * L:(RO + t + 1) * L] = np.roll(yb, 1, axis=0); S[:, :, 15, (RO + t) * L:(RO + t + 1) * L] = 0
        np.put_along_axis(K, jj, key[:, :, None], 2)
        w = np.argmax(K, axis=3)[:, :, :, None]
        np.put_along_axis(Q, w, t * L + lane, 3); np.put_along_axis(K, w, hx[:, :, :, None], 3)
        go = (np.min(ha, axis=2) < np.take_along_axis(hx, j[:, :, None], 2)[:, :, 0]).astype(np.int32)
        np.put_along_axis(P, j[:, :, None], np.take_along_axis(P, j[:, :, None], 2) + 1 - 3 * go[:, :, None], 2)
        A = (np.add.reduce(go, axis=2) & 63)[:, :, None, None]
    yq = np.ascontiguousarray((4096 * K + Q).transpose(0, 1, 3, 2, 4)).reshape(N, 128, 3 * L)
    return {"ys": np.ascontiguousarray(S[..., :2 * RO * L]).reshape(N, 128, 2 * RO * L).astype(np.float32).astype(BF), "ym": np.ascontiguousarray(S[:, :, 15, 2 * RO * L:]).astype(np.float32).astype(BF),
            "yq": yq.astype(np.float32), "yp": P.reshape(N, 8, 3 * L).astype(np.float32)}

@@ -1,0 +1,790 @@
+import numpy as np
+from concourse.mybir import AluOpType as OP, AxisListType, ActivationFunctionType as AF
+
+RO = 5
+F32, BF, F16, I32, U16 = "float32", "bfloat16", "float16", "int32", "uint16"
+SB = {
+    "S": (1920, BF), "EF": (2672, BF), "OT": (256, BF), "GL": (128, BF), "RM": (8, BF),
+    "QN": (384, I32), "QK": (384, I32), "TU": (128, I32), "TUB": (128, BF),
+    "STG": (5 * 264, F16), "SL": (128, BF), "LU": (136, U16), "M3": (5 * 128, F16), "MC": (5 * 128, F32), "MK": (5 * 768, F16), "NG": (4 * 128, BF),
+    "OB": (4 * 264, F16), "OL": (128, BF), "O3": (4 * 128, F16), "OC": (4 * 128, F32), "R3": (48, BF), "OK": (5 * 768, F16), "NK": (384, F32), "PF": (32, F32),
+    "CI": (16, I32), "CC": (40, F32), "IB": (128, BF), "I15": (128, BF), "NIB": (128, BF), "I2K": (128, BF),
+    "N2K": (128, BF), "REP": (2048, BF), "BLK": (128, BF), "WU": (128, BF), "MX": (128, BF),
+    "CM": (16, BF), "B8": (8, F32), "BX": (32, F32), "DG": (384, BF), "PM": (128, BF), "WS": (32, BF), "WM": (24, BF),
+    "WX": (384, BF), "EC": (136, BF), "EN": (136, BF), "CR": (136, BF), "ONB": (1024, BF), "R17H": (136, BF),
+    "R17M": (136, BF), "RS0": (1024, BF), "RH": (384, BF), "IDU": (384, F16), "TRI": (512, BF), "BG": (512, BF),
+    "NBG": (512, BF), "OHW": (384, BF), "CT": (640, BF), "K2": (384, BF), "KR": (384, BF), "WD": (24, BF), "WT": (24, BF),
+    "ZB": (288, BF), "B8B": (8, BF), "I24": (24, BF), "IDL": (32, F32),
+    "LS": (144, U16), "XB": (1024, BF), "T1": (384, BF), "T3": (136, BF), "T4": (48, F32), "TI": (48, I32), "TB": (512, BF),
+    "SG": (2048, BF), "VS": (2048, BF), "E": (2048, BF), "Y": (2048, BF), "D": (2048, BF), "TT": (2048, BF),
+    "SCC": (144, F32), "ST": (144, F32), "PR": (136, F32), "SCS": (136, F32), "NI": (8, I32), "UI": (8, I32), "NA": (8, I32),
+    "UA": (8, I32),
+    "XN": (128, F16), "XO": (128, F16), "XD": (128, F16), "LX": (24, U16), "X": (128, BF), "XM": (128, BF), "XT": (128, BF),
+    "UP": (128, F32), "N1": (128, I32), "N2": (128, I32), "NL": (128, U16), "AC": (16, F32), "AI": (8, I32), "AG": (8, BF),
+    "DX": (128, BF), "TX": (128, BF), "NH": (24, F16), "SU": (384, F32), "PB": (48, F32), "P1": (48, F32), "AB": (16, I32),
+    "AL": (24, I32), "GO": (16, F32), "LA": (24, U16), "OH": (128, BF), "KM": (384, F16), "CQ": (384, F32), "SQ": (384, F32),
+    "EQ": (384, BF), "KH": (768, F16), "A2": (384, F32), "RN": (384, F32), "CK": (384, F32), "NX": (128, F16), "MN": (32, F32), "T2D": (8, F32),
+    "PX": (56, F32), "MM": (16, F32), "MI": (32, I32), "DL": (8, F32), "FF": (8, F32), "YQ": (384, F32),
+    "YP": (384, F32), "PE2": (384, BF), "GP": (128, BF), "JK": (128, BF),
+}
+PACK = {}
+for _n in list(SB):
+    _w, _d = SB[_n]
+    if _w <= 48 and _n != "RM":
+        _o = SB.get("small_" + _d, (0, _d))[0]
+        PACK[_n] = ("small_" + _d, _o)
+        SB["small_" + _d] = (_o + (_w + 15) // 16 * 16, _d)
+SCRATCH = {}
+for _n in SB:
+    if _n not in PACK:
+        SCRATCH[_n] = ("sbuf", [128, SB[_n][0]], SB[_n][1])
+SCRATCH["JS"] = ("sbuf", [128, 24, 16], F16)
+BANKS = ["Z0", "Z1", "W0", "W1", "J1", "J2", "M6", "M7"]
+for _n in BANKS:
+    SCRATCH[_n] = ("psum", [128, 8, 64] if _n == "M7" else [128, 512], F32)
+ENG = ["pe", "dve", "act", "pool", "sp"]
+NDMA = 23
+SEMAPHORES = ["c_" + e for e in ENG[:4]] + ["d%d" % i for i in range(NDMA)] + ["sent"] + \
+    ["r%d_%d" % (m, t) for m in range(5) for t in range(5)]
+
+PAR = {"cy": 0.95, "pcy": 0.5, "hop": 90.0, "rlat": 2200.0, "dlat": 2200.0, "issue": 500.0, "gf": 1.5,
+       "sa": 60, "eg": [("dve", 0, 32), ("act", 32, 64), ("act", 64, 96), ("act", 96, 128)],
+       "ch": [0, 512, 1024, 1536, 1792, 2048], "seed": 0, "iters": 3, "noise": 60.0,
+       "dd": "dve", "fu": 512,
+       "early": {'act:DX': 3000, 'act:D': 1500, 'pe:J2': 1500, 'dve:NH': -1000, 'dve:TT': 300, 'dve:PR': -1000, 'act:CQ': 800,
+                 'dve:NA': 5000, 'dve:EQ': 800, 'dve:NL': 300, 'dve:OC': -1000, 'dve:PB': 800, 'dve:XD': -1000, 'dve:SCC': -300,
+                 'dve:FF': -1000, 'dve:SU': 5000, 'dve:T2D': 300, 'sp:S': 3000, 'dve:MI': -300, 'act:X': -1000, 'dve:LU': 800,
+                 'act:AC': 1500, 'act:XT': 5000}}
+PAR["off"] = []
+
+
+def A(n, a=0, b=None, s=1, p0=0, p1=128):
+    if b is None:
+        b = 512 if n in BANKS else (384 if n == "JS" else SB[n][0])
+    if n in PACK:
+        return (PACK[n][0], a + PACK[n][1], b + PACK[n][1], s, p0, p1)
+    return (n, a, b, s, p0, p1)
+
+
+def G(a, b):
+    return ("M7", a, 448 + b, 1, 0, 128, (a, b))
+
+
+def cnt(x):
+    if len(x) == 7:
+        return 8 * (x[6][1] - x[6][0])
+    return (x[2] - x[1] + x[3] - 1) // x[3]
+
+
+def two(x):
+    return x[0] == "JS" or (x[0] in SB and SB[x[0]][1] in (BF, F16, U16))
+
+
+def build():
+    ops = []
+    now = [-1]
+    CY, PCY, GF = PAR["cy"], PAR["pcy"], PAR["gf"]
+
+    def op(eng, kind, args, rd, wr, cost, **kw):
+        d = {"e": eng, "k": kind, "a": args, "rd": [r for r in rd if isinstance(r, tuple)], "wr": wr, "c": cost, "st": now[0]}
+        d.update(kw)
+        ops.append(d)
+        return d
+
+    def vc(n, *aps):
+        f = 0.5 if all(two(x) for x in aps) else 1.0
+        return max(64.0, n * f) * CY
+
+    def cp(o, i):
+        op("dve", "cp", (o, i), [i], [o], vc(cnt(o), o, i))
+
+    def tt(o, a, b, f):
+        k = 1 if (a[0] in BANKS or b[0] in BANKS) else 2
+        op("dve", "tt", (o, a, b, f), [a, b], [o], vc(cnt(o) * k, o, a, b))
+
+    def ts(o, a, s1, s2, f0, f1=None):
+        op("dve", "ts", (o, a, s1, s2, f0, f1), [a, s1, s2], [o], vc(cnt(o), o, a))
+
+    def scan(o, d0, d1, f0, f1):
+        op("dve", "scan", (o, d0, d1, f0, f1), [d0, d1], [o], vc(cnt(o), o, d0, d1))
+
+    def ms(o, v):
+        op("dve", "ms", (o, v), [], [o], vc(cnt(o), o))
+
+    def gat(e, o, w, l):
+        op(e, "gat", (o, w, l), [w, l], [o], 60 + cnt(o) * GF * CY)
+
+    def gtt(o, w, l, b, f):
+        op("dve", "gtt", (o, w, l, b, f), [w, l, b], [o], 55 + cnt(o) * GF * CY)
+
+    def act(o, i, f=AF.Identity, bias=0.0, scale=1.0, acc=None):
+        op("act", "act", (o, i, f, bias, scale, acc), [i, bias, scale], [o] + ([acc] if acc else []), max(64.0, cnt(o)) * CY + 30)
+
+    def mm(o, l, r, st, sp):
+        f = 4 if SB.get(l[0], (0, 0))[1] == F32 else 1
+        op("pe", "mm", (o, l, r, st, sp), [l, r], [o], max(min(64, cnt(l)), cnt(r)) * f * PCY)
+
+    def iota(o, pat, base, cm):
+        op("pool", "iota", (o, pat, base, cm), [], [o], 130 + 2 * cnt(o) * CY)
+
+    def asel(o, i, pat, f, base, cm):
+        op("pool", "asel", (o, i, pat, f, 0.0, base, cm), [i], [o], 170 + 2 * cnt(o) * CY)
+
+    nd = [0]
+
+    def dma(e, o, i, rd, wr, extra=0.0):
+        op(e, "dma", (o, i), rd, wr, 60.0, lat=PAR["dlat"] + extra, sem="d%d" % nd[0])
+        nd[0] += 1
+
+    def send(m, t, prs, extra=0.0):
+        op("pool", "send", (m, t, prs), [p[1] for p in prs], [p[0] for p in prs], PAR["issue"], lat=PAR["rlat"] + extra,
+           sem="r%d_%d" % (m, t))
+
+    def C(j):
+        return A("CC", j, j + 1)
+
+    def blk(n, j, w=128, o=0):
+        return A(n, o + w * j, o + w * j + w)
+
+    for q in range(8):
+        dma("act" if q % 2 else "sp", A("TU", 16 * q, 16 * q + 16, p1=24), ("tu", q), [], [A("TU", 16 * q, 16 * q + 16)])
+    dma("act", A("QN"), "qn", [], [A("QN")], 300)
+    dma("sp", A("S", 0, 1792), "st0", [], [A("S", 0, 1792)], 1200)
+    dma("act", A("QK"), "qk", [], [A("QK")], 1500)
+    dma("sp", A("GL"), "gl", [], [A("GL")], 1500)
+    dma("sp", A("OT"), "ot", [], [A("OT")], 1700)
+    dma("sp", A("RM", 0, 1), "rm", [], [A("RM")], 1700)
+    dma("sp", A("EF", 0, 2048), "ef", [], [A("EF", 0, 2048)], 2800)
+    dma("sp", A("EF", 2048, 2672), ("ef", 0, 624), [], [A("EF", 2048, 2672)], 3200)
+
+    iota(A("CI", 0, 1), [[0, 1]], 0, 1)
+    iota(A("TI", 0, 24), [[1, 24]], 0, 0)
+    iota(A("T1"), [[0, 24], [1, 16]], 0, 0)
+    iota(A("IDL"), [[128, 4], [16, 8]], 0, 0)
+    ms(A("ONB"), 1.0)
+    ms(A("K2"), -2048.0)
+    ms(A("I24"), 1.0)
+    asel(A("I24"), A("I24"), [[1, 24]], OP.is_equal, 0, -1)
+    asel(A("IB"), A("ONB", 0, 128), [[-1, 128]], OP.is_equal, 0, 1)
+    iota(A("T3"), [[1, 136]], 0, 0)
+    ts(A("CI", 1, 2), A("CI", 0, 1), 15, None, OP.bitwise_and)
+    ts(A("CI", 2, 3), A("CI", 0, 1), 4, None, OP.arith_shift_right)
+    ts(A("CI", 3, 4), A("CI", 0, 1), 1, None, OP.bitwise_and)
+    ts(A("CI", 4, 5), A("CI", 0, 1), 1, 7, OP.arith_shift_right, OP.bitwise_and)
+    ts(A("CI", 5, 6), A("CI", 0, 1), 7, None, OP.bitwise_and)
+    ts(A("CI", 6, 7), A("CI", 0, 1), 3, None, OP.arith_shift_right)
+    cp(A("CC", 0, 7), A("CI", 0, 7))
+    ts(A("DG"), A("T1"), C(1), None, OP.is_equal)
+    ms(A("RS0"), 1.0)
+    ms(A("RS0", 0, 1024, 16), 0.0)
+    ts(A("IDL"), A("IDL"), C(1), 1.0 / 2048, OP.add, OP.mult)
+    cp(A("LS", 0, 24), A("TI", 0, 24))
+    ts(A("LS", 24, 48), A("TI", 0, 24), 16.0, 15.0, OP.mult, OP.add)
+    ts(C(10), C(5), 16.0, None, OP.mult)
+    ts(A("LS", 52, 54), A("TI", 0, 2), 0.0, C(10), OP.mult, OP.add)
+    ts(A("LS", 52, 54), A("LS", 52, 54), 0.0625, None, OP.mult)
+    ts(A("LS", 76, 140), A("T3", 0, 64), 0.0, None, OP.add)
+    ts(A("T4", 16, 19), A("TI", 0, 3), 16.0, C(1), OP.mult, OP.add)
+    ts(A("T4", 20, 23), A("T4", 16, 19), 24.0, -24.0, OP.is_ge, OP.mult)
+    tt(A("T4", 16, 19), A("T4", 16, 19), A("T4", 20, 23), OP.add)
+    ts(A("TI", 44, 47), A("T4", 16, 19), 1.0 / 3, -0.33, OP.mult, OP.add)
+    ts(A("T4", 20, 23), A("TI", 44, 47), -368.0, 15.0, OP.mult, OP.add)
+    ts(A("T4", 16, 19), A("T4", 16, 19), 128.0, None, OP.mult)
+    tt(A("T4", 24, 27), A("T4", 16, 19), A("T4", 20, 23), OP.add)
+    cp(A("LS", 48, 51), A("T4", 24, 27))
+    ts(C(11), C(1), 8.0, C(10), OP.is_ge, OP.add)
+    ts(A("LS", 58, 66), A("TI", 0, 8), 2.0, C(11), OP.mult, OP.add)
+    ts(A("T4", 0, 9), A("TI", 0, 9), 16.0, C(1), OP.mult, OP.add)
+    ts(A("TI", 32, 41), A("T4", 0, 9), 1.0 / 17, -0.47, OP.mult, OP.add)
+    ts(A("LS", 66, 75), A("TI", 32, 41), 7.0, None, OP.min)
+    ts(C(3), C(3), 8.0, C(2), OP.mult, OP.add)
+    ts(C(5), C(10), C(6), None, OP.add)
+    ts(C(6), C(0), 1792.0, None, OP.add)
+    ts(C(7), C(1), 37.0, None, OP.mult)
+    ts(C(8), C(1), 15.0, None, OP.not_equal)
+    ts(C(9), C(1), 15.0, None, OP.is_equal)
+    ts(C(12), C(1), 0.5, C(8), OP.add, OP.mult)
+    ts(C(14), C(1), 3.0, -2048.0, OP.is_lt, OP.mult)
+    ts(C(15), C(0), 1.0, 2048.0, OP.is_equal, OP.mult)
+    ts(C(16), C(0), 2.0 ** 24 - 2048, -2.0 ** 24, OP.mult, OP.add)
+    ts(C(21), C(1), 128.0, None, OP.mult)
+    ms(C(23), 32.0)
+    ms(C(13), -63.5)
+    ms(C(22), -127.5)
+    ts(C(32), C(1), 37.0, -64.0, OP.mult, OP.add)
+    ms(A("MC", 104, 112), 0.0)
+    ts(A("CC", 17, 20), A("TI", 0, 3), C(1), None, OP.is_equal)
+    ts(A("CC", 29, 32), A("CC", 17, 20), 2047.0, C(14), OP.mult, OP.add)
+    ts(A("B8"), A("TI", 0, 8), C(2), None, OP.is_equal)
+    act(A("BX", 0, 8), A("B8"), scale=C(9))
+    act(A("BX", 8, 16), A("B8"), scale=C(12))
+    act(A("BX", 16, 24), A("B8"), scale=C(8))
+    act(A("WS", 0, 8), A("BX", 0, 8), scale=2.0 ** 26)
+    act(A("WS", 9, 24, 2), A("BX", 8, 16), scale=16.0)
+    act(A("WS", 8, 24, 2), A("BX", 8, 16), scale=-16.0)
+    act(A("WS", 24, 32), A("BX", 16, 24), scale=8.0)
+    for l in range(3):
+        act(blk("WM", l, 8), A("BX", 0, 8), scale=1024.0)
+    ts(A("CM", 0, 8), A("TI", 0, 8), C(4), None, OP.is_equal)
+    act(A("CM", 8, 16), A("CM", 0, 8), scale=0.125)
+    ts(A("MX"), A("T1", 0, 128), C(3), None, OP.is_equal)
+    asel(A("EN"), A("ONB", 0, 136), [[-16, 8], [-1, 17]], OP.is_equal, 1, 1)
+    ms(A("EN", 0, 136, 17), 0.0)
+    act(A("EC"), A("EN"), scale=32768.0)
+    asel(A("EN", 0, 136, 17), A("ONB", 0, 8), [[-16, 8]], OP.is_equal, 0, 1)
+    iota(A("CR"), [[0, 8], [1, 17]], 0, 0)
+    ts(A("CR", p1=2), A("CR", p1=2), A("CC", 15, 16, p1=2), A("CC", 16, 17, p1=2), OP.mult, OP.add)
+    ms(A("CR", 0, 136, 17), 244.0 * 32768)
+    ms(A("R17H"), 0.0)
+    ms(A("R17H", 0, 136, 17), 2.0 ** 27)
+    ms(A("R17M"), 1.0)
+    ms(A("R17M", 0, 136, 17), 0.0)
+    ms(A("SCC", 136, 144), 0.0)
+    ms(A("S", 1792, 1920), 0.0)
+    ms(A("ZB"), 0.0)
+    ms(A("R3"), 1.0)
+    ms(A("R3", 0, 48, 3), 0.0)
+    asel(A("BLK"), A("ONB", 0, 128), [[-16, 8], [0, 16]], OP.is_ge, 0, 1)
+    asel(A("BLK"), A("BLK"), [[16, 8], [0, 16]], OP.is_ge, 15, -1)
+    act(A("WU"), A("BLK"), scale=C(12))
+    act(A("I15"), A("IB"), scale=C(8))
+    act(A("NIB"), A("IB"), scale=-1.0)
+    act(A("I2K"), A("IB"), scale=2048.0)
+    act(A("N2K"), A("IB"), scale=-2048.0)
+    for l in range(3):
+        act(blk("OHW", l), A("ONB", 0, 128), scale=C(17 + l))
+        act(blk("WX", l), A("BLK"), scale=C(29 + l))
+        ts(blk("IDU", l), A("T3", 0, 128), C(21), 1.0 / 2048, OP.add, OP.mult)
+    iota(A("KR", p1=1), [[0, 24], [-1, 16]], 15, 0)
+    for h in range(2):
+        asel(blk("REP", h, 1024), A("ONB"), [[-1, 64], [0, 16]], OP.is_equal, -64 * h, 1)
+    ts(A("PM"), A("T3", 0, 128), C(5), -1.0, OP.is_equal, OP.mult)
+    ms(A("RH"), 0.0)
+    ms(A("RH", 0, 384, 16), 2.0 ** 27)
+    for h in range(2):
+        asel(A("TRI", p0=64 * h, p1=64 * h + 64), A("ONB", 0, 512, p0=64 * h, p1=64 * h + 64), [[0, 8], [1, 64]], OP.is_ge, 0, -1)
+    for q in range(8):
+        act(blk("BG", q, 64), A("ONB", 0, 64), scale=A("B8", q, q + 1))
+    act(A("NBG"), A("BG"), scale=-1.0)
+    for t in range(RO):
+        act(blk("CT", t), A("ONB", 0, 128), scale=128.0 * t - 2048.0)
+    ms(A("WD", 8, 16), 0.0)
+    ms(A("WT"), 0.0)
+    act(A("WD", 0, 8), A("BX", 16, 24))
+    ts(A("WD", 16, 24), A("B8"), A("RM", 0, 1), None, OP.mult)
+    act(A("WT", 8, 16), A("BX", 16, 24), scale=16.0)
+    act(A("AC", 0, 1), C(7))
+    act(A("B8B"), A("B8"))
+
+    def control(t, n, o):
+        tt(A("PF"), A(n, o + 80, o + 112), A("IDL"), OP.add)
+        pc = lambda l: blk("PF", l, 8)
+        tt(A("MM", 0, 8), pc(0), pc(1), OP.min)
+        tt(A("MM", 0, 8), A("MM", 0, 8), pc(2), OP.min)
+        gtt(A(n, o + 48, o + 80), A("MM", 0, 8), A("LS", 52, 54), A("PF"), OP.is_equal)
+        for l in range(3):
+            act(A(n, o + l, o + 24, 3), blk(n, l, 8, o + 48))
+            act(A(n, o + 24 + (l + 1) % 3, o + 48, 3), blk(n, l, 8, o + 48))
+        if t < RO - 1:
+            tt(A("PX", 0, 24), A(n, o + 48, o + 72), A("PF", 0, 24), OP.add)
+            tt(A("MM", 8, 16), A("PX", 0, 8), A("PX", 8, 16), OP.min)
+            tt(A("MM", 8, 16), A("MM", 8, 16), A("PX", 16, 24), OP.min)
+            ts(A("MI", 0, 16), A("MM"), 2048.0, None, OP.mult)
+            ts(A("MI", 16, 32), A("MI", 0, 16), 2047, None, OP.bitwise_and)
+            tt(A(n, o + 112, o + 120), A("MI", 16, 24), A("MI", 24, 32), OP.subtract)
+            cp(A(n, o + 120, o + 128), A("MI", 24, 32))
+
+    cp(A("TUB", p1=24), A("TU", p1=24))
+    mm(A("M6", 0, 24), A("TUB", p1=24), A("I24", p1=24), True, True)
+    tt(A("PF", 0, 24), A("IDL", 0, 24), A("M6", 0, 24), OP.add)
+    cp(A("MC", 80, 104), A("M6", 0, 24))
+    tt(A("FF"), A("PF", 0, 8), A("PF", 8, 16), OP.min)
+    tt(A("DL"), A("FF"), A("PF", 16, 24), OP.min)
+    ts(A("AB", 0, 8), A("DL"), 2048.0, None, OP.mult)
+    ts(A("AL", 0, 8), A("AB", 0, 8), 2047, None, OP.bitwise_and)
+    cp(A("LU", 128, 136), A("AL", 0, 8))
+    gat("dve", A("LU", 0, 128), A("QN"), A("LU", 128, 136))
+    gat("dve", A("M3", 0, 128), A("QK"), A("LU", 128, 136))
+    gat("dve", A("STG", 128, 256), A("QN"), A("LU", 128, 136))
+    for h, src, bank in ((0, "QK", "J2"), (1, "QN", "W0")):
+        cp(blk("KH", h, 384), A(src))
+        for l in range(3):
+            mm(blk(bank, l), blk("KH", 3 * h + l), A("IB"), True, True)
+        cp(blk("MK", h, 384), A(bank, 0, 384))
+    control(0, "MC", 0)
+    gat("act", A("GP"), A("GL"), A("LS", 58, 66))
+    mm(A("J1", 0, 128), A("GP"), A("NIB"), True, True)
+    act(A("NG", 0, 128), A("J1", 0, 128))
+
+    SW = A("S", 0, 1792)
+    fu = PAR["fu"]
+    for t in range(RO):
+        last = t == RO - 1
+        now[0] = t
+        u0, u1, m3 = 0, 264 * t, 128 * t
+        ng = blk("NG", t % 4)
+        jl = A("LU", u0 + 128, u0 + 136)
+        names, newnames, newkeys = blk("MK", 2 * t + 1, 384), blk("OK", 2 * t + 1, 384), blk("OK", 2 * t, 384)
+        if t < 3:
+            send(0, t + 1, [(blk("NG", t + 1), ng)])
+        sa = PAR["sa"]
+        gat("dve", A("SG", 0, 16 * sa), SW, A("LU", u0, u0 + sa))
+        gat("act", A("SG", 16 * sa, 2048), SW, A("LU", u0 + sa, u0 + 128))
+        mm(A("M6", 0, 136), A("ONB", 0, 128, p1=2), A("CR", p1=2), True, False)
+        mm(A("M6", 0, 136), A("STG", u1 + 128, u1 + 256), A("EN"), False, False)
+        mm(G(0, 17), A("IB"), A("ZB", 0, 136), True, False)
+        for k in range(16):
+            mm(A("M6", 1 + k, 136, 17), A("SG", k, 2048, 16), A("WS", 0, 8), False, False)
+        mm(A("M6", 0, 136), A("M3", m3, m3 + 128), A("EC"), False, True)
+        mm(G(1, 2), A("SG", 0, 2048, 16), A("WS", 9, 24, 2), False, False)
+        for k in range(1, 16):
+            mm(G(k, k + 2), A("SG", k, 2048, 16), A("WS", 8, 24), False, False)
+        for a, b in ((0, 16 * sa), (16 * sa, 8 * sa + 1024), (8 * sa + 1024, 2048)):
+            scan(A("VS", a, b), A("RS0", 0, b - a), A("SG", a, b), OP.mult, OP.max)
+        mm(G(16, 17), A("VS", 15, 2048, 16), A("WS", 24, 32), False, True)
+        gat("act", A("OH"), A("OHW"), jl)
+        mm(A("J1", 0, 384), A("OH"), A("WX"), True, False)
+        for k in range(16):
+            mm(A("J1", k, 384, 16), A("SG", k, 2048, 16), A("WM"), False, k == 15)
+        scan(A("SCC", 0, 136), A("R17H"), A("M6", 0, 136), OP.add, OP.min)
+        cp(A("NI"), A("SCC", 16, 136, 17))
+        gtt(A("ST"), A("NI"), A("LS", 66, 75), A("SCC"), OP.is_equal)
+        ts(A("NA"), A("NI"), 2047, None, OP.bitwise_and)
+        tt(A("PR"), G(0, 17), A("ST", 0, 136), OP.mult)
+        gtt(A("XN"), A("NA"), A("LS", 0, 8), A("MX"), OP.mult)
+        scan(A("SCS"), A("R17M"), A("PR"), OP.mult, OP.add)
+        mm(A("M6", 0, 8), A("XN"), A("CM", 0, 8), True, True)
+        cp(A("UI"), A("SCS", 16, 136, 17))
+        cp(A("LX", 0, 8), A("M6", 0, 8))
+        ts(A("UA"), A("UI"), 2047, None, OP.bitwise_and)
+        gtt(A("XO"), A("UA"), A("LS", 0, 8), A("MX"), OP.mult)
+        gat("act", A("X"), SW, A("LX", 0, 8))
+        mm(A("M6", 8, 16), A("XO"), A("CM", 8, 16), True, True)
+        mm(A("Z1", 0, 128), A("WU"), A("X"), True, True)
+        mm(A("Z0", 0, 128), A("X"), A("I15"), True, True)
+        cp(A("LX", 8, 16), A("M6", 8, 16))
+        act(A("UP"), A("Z1", 0, 128), bias=C(23), scale=2.0)
+        act(A("XT"), A("Z0", 0, 128))
+        gtt(A("N1"), A("OT"), A("LX", 8, 16), A("UP"), OP.mult)
+        ts(A("N2"), A("N1"), 5, 2047, OP.arith_shift_right, OP.bitwise_and)
+        ts(A("NL"), A("N2"), A("AC", 0, 1), None, OP.add)
+        mm(A("W1", 0, 128), A("XN"), A("IB"), True, True)
+        cp(A("NX"), A("W1", 0, 128))
+        if fu:
+            op("act", "gatm", (A("XB", 0, fu), A("X"), A("LS", 76, 76 + fu // 16), 0.0, C(8)), [A("X"), A("LS", 76, 140), C(8)],
+               [A("XB", 0, fu)], 60 + fu * GF * CY)
+        mm(A("J2", 0, 128), ng, A("IB"), True, False)
+        mm(A("J2", 0, 128), A("I15"), A("X"), False, True)
+        act(A("DX"), A("J2", 0, 128), AF.Abs)
+        ts(A("TX"), A("DX"), 5.0, None, OP.is_gt)
+        mm(A("J2", 128, 152), A("DX"), A("WD"), True, False)
+        mm(A("J2", 128, 152), A("TX"), A("WT"), False, True)
+        ts(A("NH"), A("J2", 128, 152), -1.0, None, OP.mult)
+        tt(A("KM"), A("J1", 0, 384), blk("MK", 2 * t, 384), OP.max)
+        mm(A("M6", 0, 384), A("ONB", 0, 128, p1=1), A("KR", p1=1), True, False)
+        mm(A("M6", 0, 384), A("I2K"), A("KM"), False, True)
+        act(A("CQ"), A("M6", 0, 384))
+        scan(A("SQ"), A("RS0", 0, 384), A("CQ"), OP.mult, OP.max)
+        gtt(A("EQ"), A("SQ"), A("LS", 24, 48), A("CQ"), OP.is_equal)
+        for e, a, b in PAR["eg"]:
+            if 16 * b <= fu:
+                gtt(A("E", 16 * a, 16 * b), A("EF"), A("NL", a, b), A("XB", 16 * a, 16 * b), OP.add)
+            else:
+                gat(e, A("E", 16 * a, 16 * b), A("EF"), A("NL", a, b))
+        mm(A("J1", 0, 288), A("IB"), A("ZB"), True, False)
+        mm(A("J2", 0, 96), A("IB"), A("ZB", 0, 96), True, False)
+        jo = lambda b: A("J1", b, 288, 12) if b < 12 else A("J2", b - 12, 96, 4)
+        for b in range(16):
+            mm(jo(b), blk("REP", b), A("NH"), False, False)
+        mm(A("M6", 0, 384), A("I2K"), A("IDU"), True, False)
+        ch = PAR["ch"]
+        for c in range(len(ch) - 1):
+            a, b = ch[c], ch[c + 1]
+            z, w = A("Z%d" % (c % 2), 0, b - a), A("W%d" % (c % 2), 0, b - a)
+            if b <= fu:
+                z = A("E", a, b)
+            else:
+                mm(z, A("XT"), A("REP", a, b), True, False)
+                mm(z, A("IB"), A("E", a, b), False, True)
+            ts(A("Y", a, b), z, 0.0, 63.0, OP.max, OP.min)
+            mm(w, ng, A("REP", a, b), True, False)
+            mm(w, A("IB"), A("Y", a, b), False, True)
+            act(A("D", a, b), w, AF.Abs)
+            ts(A("TT", a, b), A("D", a, b), 5.0, None, OP.is_gt)
+            for q in range(a // 128, b // 128):
+                mm(jo(q), blk("D", q), A("WD"), False, False)
+            for q in range(a // 128, b // 128):
+                mm(jo(q), blk("TT", q), A("WT"), False, q in (11, 15))
+            if b == 1536:
+                op("dve", "cpj", (0, 12, A("J1", 0, 288)), [A("J1", 0, 288)], [A("JS", 0, 288)], 288 * CY)
+        op("dve", "cpj", (12, 16, A("J2", 0, 96)), [A("J2", 0, 96)], [A("JS", 288, 384)], 96 * CY)
+        for l in range(3):
+            op("pe", "mmj", (blk("M6", l), l, A("I2K"), l == 2), [A("JS"), A("I2K")], [A("M6", 0, 384)], 128 * PCY)
+        mm(A("Z1", 0, 384), A("IB"), names, True, False)
+        mm(A("Z1", 0, 384), A("N2K"), A("EQ"), False, True)
+        act(A("RN"), A("Z1", 0, 384), AF.Relu)
+        mm(A("Z0", 0, 384), A("T3", 0, 128, p1=1), A("ONB", 0, 384, p1=1), True, False)
+        mm(A("Z0", 0, 384), A("CT", 128 * t, 128 * t + 128, p1=1), A("ONB", 0, 384, p1=1), False, False)
+        mm(A("Z0", 0, 384), A("I2K"), A("EQ"), False, True)
+        tt(newnames, A("Z0", 0, 384), A("RN"), OP.max)
+        if not last:
+            for l in range(3):
+                mm(blk("Z1", l), blk("OK", 6 * t + 3 + l), A("IB"), True, True)
+            act(A("NK"), A("Z1", 0, 384))
+        w = "M7"
+        mm(G(0, 64), A("I2K"), A("TRI"), True, False)
+        for q in range(8):
+            for h in range(2):
+                mm(A(w, 64 * q, 64 * q + 64, 1, 64 * h, 64 * h + 64), blk("BG", q, 64), blk("NX", h, 64), False, False)
+        mm(G(0, 64), A("NX"), A("NBG"), False, True)
+        if PAR["dd"] == "act":
+            act(A("TB"), G(0, 64), AF.Abs)
+            for q in range(8):
+                act(blk("TB", q, 64), blk("TB", q, 64), AF.Relu, 1.0, -1.0, A("MN", q, q + 1))
+            act(A("MN", 8, 16), A("MN", 0, 8), AF.Sign)
+        else:
+            for q in range(8):
+                op("dve", "red", (A("MN", q, q + 1), blk(w, q, 64), OP.min, True), [blk(w, q, 64)], [A("MN", q, q + 1)], 64 * CY)
+            ts(A("MN", 8, 16), A("MN", 0, 8), 0.0, None, OP.is_equal)
+        scan(A("SU"), A("RH"), A("M6", 0, 384), OP.add, OP.min)
+        gtt(A("PB"), A("SU"), A("LS", 48, 51), A("MC", m3, m3 + 48), OP.mult)
+        scan(A("P1"), A("R3"), A("PB"), OP.mult, OP.add)
+        ts(A("GO", 0, 8), A("P1", 2, 24, 3), 0.0, None, OP.is_lt)
+        cp(A("AB"), A("P1", 2, 48, 3))
+        if not last:
+            tt(A("GO", 8, 16), A("GO", 0, 8), A("MC", m3 + 112, m3 + 120), OP.mult)
+        ts(A("AL", 0, 16), A("AB"), 2047, None, OP.bitwise_and)
+        if not last:
+            njl = A("LA", 16, 24)
+            tt(A("OB", u1 + 256, u1 + 264), A("GO", 8, 16), A("MC", m3 + 120, m3 + 128), OP.add)
+            cp(A("LA", 0, 16), A("AL", 0, 16))
+            cp(njl, A("OB", u1 + 256, u1 + 264))
+            gat("dve", A("OB", u1, u1 + 128), A("Y"), A("LA", 8, 16))
+            gat("dve", A("OB", u1 + 128, u1 + 256), A("NK"), njl)
+            send(2, t, [(blk("STG", t + 1, 264), blk("OB", t, 264))])
+        else:
+            cp(A("LA", 0, 16), A("AL", 0, 16))
+            gat("act", A("OL"), A("Y"), A("LA", 8, 16))
+            send(2, t, [(A("SL"), A("OL"))])
+        mm(A("W1", 0, 384), A("IB"), A("KM"), True, False)
+        mm(A("W1", 0, 384), A("N2K"), A("EQ"), False, True)
+        act(A("A2"), A("W1", 0, 384), AF.Relu)
+        mm(A("W0", 0, 384), A("I2K"), A("EQ"), True, False)
+        mm(A("W0", 0, 384), A("ONB", 0, 128, p1=1), A("K2", p1=1), False, False)
+        for k in range(16):
+            mm(A("W0", k, 384, 16), A("PM"), A("NH"), False, k == 15)
+        tt(newkeys, A("W0", 0, 384), A("A2"), OP.max)
+        ts(A("FF"), A("GO", 0, 8), -3.0, 1.0, OP.mult, OP.add)
+        gtt(A("PX", 24, 56), A("FF"), A("LS", 52, 54), A("MC", m3 + 48, m3 + 80), OP.mult)
+        if not last:
+            for l in range(3):
+                mm(blk("W1", l), blk("OK", 6 * t + l), A("IB"), True, True)
+            act(A("CK"), A("W1", 0, 384))
+            gat("dve", A("O3", m3, m3 + 128), A("CK"), njl)
+            tt(A("OC", m3 + 80, m3 + 112), A("PX", 24, 56), A("MC", m3 + 80, m3 + 112), OP.add)
+            control(t + 1, "OC", m3)
+            send(3, t, [(blk("M3", t + 1), blk("O3", t))])
+            wc = 128 if t < RO - 2 else 112
+            send(4, t, [(A("MC", m3 + 128, m3 + 128 + wc), A("OC", m3, m3 + wc))], 300)
+            send(1, t, [(blk("MK", t + 1, 768), blk("OK", t, 768))], 1500)
+            act(A("AG"), A("GO", 0, 8))
+            mm(A("J1", 0, 8), A("BLK"), A("AG"), True, True)
+            act(A("AC", 8, 16), A("J1", 0, 8), acc=A("AC", 4, 5))
+            act(A("AC", 5, 6), A("AC", 4, 5), AF.Sign, C(13))
+            act(A("AC", 6, 7), A("AC", 4, 5), AF.Sign, C(22))
+            act(A("AC", 7, 8), A("AC", 4, 5), bias=C(32))
+            act(A("AC", 3, 4), A("AC", 5, 6), bias=A("AC", 7, 8), scale=-32.0)
+            act(A("AC", 0, 1), A("AC", 6, 7), bias=A("AC", 3, 4), scale=-32.0)
+        else:
+            for l in range(3):
+                mm(blk("W1", l), blk("OK", 6 * t + 3 + l), A("IB"), True, False)
+                mm(blk("W1", l), blk("OK", 6 * t + l), A("I2K"), False, False)
+                mm(blk("W1", l), blk("OK", 6 * t + l), A("I2K"), False, True)
+            act(A("YQ"), A("W1", 0, 384))
+            dma("sp", "yq", A("YQ"), [A("YQ")], [])
+            tt(A("T4", 24, 48), A("PX", 24, 48), A("MC", m3 + 80, m3 + 104), OP.add)
+            gtt(A("PE2"), A("T4", 24, 48), A("LS", 0, 24), A("DG"), OP.mult)
+            mm(A("J1", 0, 384, p1=8), A("B8B"), A("PE2"), True, True)
+            act(A("YP", p1=8), A("J1", 0, 384, p1=8))
+            dma("act", "yp", A("YP", p1=8), [A("YP")], [])
+        ts(A("MN", 16, 24), A("NA"), -1.0, C(6), OP.mult, OP.add)
+        tt(A("MN", 24, 32), A("MN", 16, 24), A("MN", 8, 16), OP.mult)
+        tt(A("T2D"), A("MN", 24, 32), A("NA"), OP.add)
+        gtt(A("XD"), A("T2D"), A("LS", 0, 8), A("DG", 0, 128), OP.mult)
+        mm(A("J2", 0, 8), A("XD"), A("B8B"), True, True)
+        cp(A("LX", 16, 24), A("J2", 0, 8))
+        op("act", "gatm", (A("XM"), A("S"), A("LX", 16, 24), C(9), C(8)), [A("S"), A("LX", 16, 24), C(9), C(8)], [A("XM")],
+           60 + 128 * GF * CY)
+        for h in range(2):
+            op("dve", "sca", (A("S"), blk("LX", h, 4, 16), blk("XM", h, 64)), [blk("LX", h, 4, 16), blk("XM", h, 64)], [A("S")],
+               55 + 64 * 3 * CY)
+        if not last:
+            gat("act", blk("S", t), A("Y"), A("LA", 0, 8))
+            cp(A("LU"), A("STG", u1 + 392, u1 + 528))
+            cp(blk("S", RO + t), A("STG", u1 + 264, u1 + 392))
+        else:
+            gat("act", A("GP"), A("Y"), A("LA", 0, 8))
+            dma("act", ("ys", 512, 640), A("GP"), [A("GP")], [])
+            dma("sp", ("ys", 0, 512), A("S", 0, 512), [A("S", 0, 512)], [])
+            dma("act", ("ys", 640, 1152), A("S", 640, 1152), [A("S", 640, 1152)], [])
+            dma("sp", "ym", "marks", [A("S", 1280, 1792)], [])
+            dma("sp", ("ys", 1152, 1280), A("SL"), [A("SL")], [])
+    return ops
+
+
+def deps_of(ops):
+    hist = {}
+    for n, o in enumerate(ops):
+        dp = {}
+        acc = [(r, False) for r in o["rd"]] + [(w, True) for w in o["wr"]]
+        for r, isw in acc:
+            bank = r[0] in BANKS
+            for m, q, w in hist.get(r[0], []):
+                if m == n:
+                    continue
+                oe = ops[m]["e"]
+                if bank and oe != o["e"]:
+                    dp[m] = True
+                elif (w or isw) and q[1] < r[2] and r[1] < q[2]:
+                    dp[m] = dp.get(m, False) or not (oe == "pe" and o["e"] == "pe")
+                elif bank and oe == "pe":
+                    dp[m] = dp.get(m, False)
+        for r, isw in acc:
+            h = hist.setdefault(r[0], [])
+            if isw:
+                h[:] = [x for x in h if not (r[1] <= x[1][1] and x[1][2] <= r[2] and r[3] == 1 and cnt(r) == r[2] - r[1] and r[4] == 0 and r[5] == 128)]
+            h.append((n, r, isw))
+        o["dp"] = dp
+
+
+def place(ops, keys, before, after, gap, lead):
+    n = len(ops)
+    left = [len(before[i]) for i in range(n)]
+    ready = list(lead)
+    start = [0.0] * n
+    busy = dict((e, []) for e in ENG)
+    todo = sorted((keys[i], i) for i in range(n) if left[i] == 0)
+    while todo:
+        i = todo.pop(0)[1]
+        c, st, bz = ops[i]["c"], ready[i], busy[ops[i]["e"]]
+        lo, hi = 0, len(bz)
+        while lo < hi:
+            mid = (lo + hi) // 2
+            if bz[mid][1] <= st:
+                lo = mid + 1
+            else:
+                hi = mid
+        while lo < len(bz) and bz[lo][0] < st + c - 1e-6:
+            st = max(st, bz[lo][1])
+            lo += 1
+        bz.insert(lo, (st, st + c))
+        start[i] = st
+        new = False
+        for j in after[i]:
+            ready[j] = max(ready[j], st + c + gap(i, j))
+            left[j] -= 1
+            if left[j] == 0:
+                todo.append((keys[j], j))
+                new = True
+        if new:
+            todo.sort()
+    return start
+
+
+def label(o):
+    x = (o["wr"] + o["rd"])[0]
+    return ([k for k, v in PACK.items() if v[0] == x[0] and v[1] <= x[1] < v[1] + SB[k][0]] + [x[0]])[0]
+
+
+def kinds(ops):
+    seen, names, out, prev = {}, {}, [], None
+    for o in ops:
+        if o["st"] < 0:
+            out.append(-1)
+            continue
+        key = (o["st"], o["e"], label(o))
+        if not (o["e"] == "pe" and prev == key):
+            seen[key] = seen.get(key, 0) + 1
+        prev = key
+        out.append(names.setdefault((key[1], key[2], seen[key]), len(names)))
+    return out
+
+
+def schedule(ops):
+    deps_of(ops)
+    n = len(ops)
+    pred = [list(o["dp"]) for o in ops]
+    succ = [[] for _ in range(n)]
+    for i in range(n):
+        for m in pred[i]:
+            succ[m].append(i)
+    lat = [o.get("lat", 0.0) for o in ops]
+    gap = lambda m, i: lat[m] + (PAR["hop"] if ops[i]["dp"][m] else 0.0)
+    tail = [0.0] * n
+    for i in range(n - 1, -1, -1):
+        tail[i] = ops[i]["c"] + max([gap(i, j) + tail[j] for j in succ[i]] + [lat[i]])
+    early = [PAR["early"].get(o["e"] + ":" + label(o), 0.0) for o in ops]
+    keys = [-tail[i] - early[i] for i in range(n)]
+    best = None
+    rs = np.random.RandomState(PAR["seed"])
+    for it in range(PAR["iters"]):
+        st = place(ops, keys, pred, succ, gap, [0.0] * n)
+        total = max(st[i] + ops[i]["c"] + lat[i] for i in range(n))
+        if best is None or total < best[0]:
+            best = (total, st)
+        back = place(ops, [-(st[i] + ops[i]["c"] + lat[i]) for i in range(n)], succ, pred, lambda j, i: gap(i, j), lat)
+        noise = rs.uniform(0.0, PAR["noise"], n)
+        keys = [float(-(back[i] + ops[i]["c"]) + noise[i] - early[i]) for i in range(n)]
+    total, st = best
+    if PAR["off"]:
+        kind = kinds(ops)
+        keys = [st[i] if kind[i] < 0 else 4000.0 + 17000.0 * ops[i]["st"] + 10.0 * PAR["off"][kind[i]] + 1e-3 * i for i in range(n)]
+        st = place(ops, keys, pred, succ, gap, [0.0] * n)
+        total = max(st[i] + ops[i]["c"] + lat[i] for i in range(n))
+    for i in range(n):
+        ops[i]["t"] = st[i]
+    return sorted(range(n), key=lambda i: (st[i], i)), total
+
+
+def plan():
+    ops = build()
+    order, total = schedule(ops)
+    count = dict((e, 0) for e in ENG)
+    known = dict((e, {}) for e in ENG)
+    for i in order:
+        o = ops[i]
+        e = o["e"]
+        waits = {}
+        for m, need in o["dp"].items():
+            if need:
+                s, v = ops[m]["sig"]
+                if known[e].get(s, 0) < v:
+                    waits[s] = max(waits.get(s, 0), v)
+        src = dict(((ops[m]["sig"]), m) for m in o["dp"])
+        keep = []
+        for s, v in waits.items():
+            if not any(s2 != s and ops[src[(s2, v2)]]["kn"].get(s, 0) >= v for s2, v2 in waits.items()):
+                keep.append((s, v))
+        for s, v in waits.items():
+            for s2, v2 in ops[src[(s, v)]]["kn"].items():
+                known[e][s2] = max(known[e].get(s2, 0), v2)
+            known[e][s] = max(known[e].get(s, 0), v)
+        o["w"] = keep
+        if o["k"] == "send":
+            o["sig"] = (o["sem"], 8)
+            o["kn"] = {}
+        elif o["k"] == "dma":
+            o["sig"] = (o["sem"], 16)
+            o["kn"] = dict(known[e])
+        else:
+            count[e] += 1
+            o["sig"] = ("c_" + e, count[e])
+            o["kn"] = dict(known[e])
+    return ops, order, total, count
+
+
+PLAN = []
+
+
+def rank_program(g, core, T, topo):
+    rank = T.rank_of(core)
+    if rank is None:
+        return
+    if not PLAN:
+        PLAN.append(plan())
+    ops, order, total, count = PLAN[0]
+    nxt = T.cores[(rank + 1) % len(T.cores)]
+    rid, pid = topo.addr(nxt, core)
+    mask, nout = topo.mask(core, nxt), len(topo.engines(core, nxt))
+    nin = len(topo.engines(T.cores[rank - 1], core))
+
+    def wait(q, s, v):
+        q.wait_ge(T.sem[s], nin if s[0] == "r" else v)
+    Q = {"pe": g.tensor, "dve": g.vector, "act": g.scalar, "pool": g, "sp": g.sync}
+
+    def ap(x):
+        if not isinstance(x, tuple):
+            return x
+        if len(x) == 7:
+            return T["M7"][:, :, x[6][0]:x[6][1]]
+        if x[0] == "M7":
+            return T["M7"][x[4]:x[5], x[1] // 64, x[1] % 64:x[1] % 64 + x[2] - x[1]]
+        if x[3] == 1:
+            return T[x[0]][x[4]:x[5], x[1]:x[2]]
+        return T[x[0]][x[4]:x[5], x[1]:x[2]:x[3]]
+
+    def ext(x):
+        if x == "marks":
+            return T["S"][15::16, 1280:1792]
+        if isinstance(x, str):
+            return T[x][:]
+        if len(x) == 2:
+            return T[x[0]][x[1]]
+        if len(x) == 3:
+            return T[x[0]][:, x[1]:x[2]]
+        return ap(x)
+
+    nsent = 0
+    ends = []
+    for i in order:
+        o = ops[i]
+        q, k, a = Q[o["e"]], o["k"], o["a"]
+        for s, v in o["w"]:
+            wait(q, s, v)
+        if k == "send":
+            g.remote_dma(ap(a[2][0][0]), ap(a[2][0][1]), T.sem[o["sem"]], T.sem["sent"], pid, rid, mask)
+            nsent += nout
+            ends.append(o["sig"])
+            continue
+        if k == "dma":
+            q.dma_start(ext(a[0]), ext(a[1])).then_inc(T.sem[o["sem"]], 16)
+            ends.append(o["sig"])
+            continue
+        if k == "cp":
+            r = q.tensor_copy(ap(a[0]), ap(a[1]))
+        elif k == "cpj":
+            r = q.tensor_copy(T["JS"][:, :, a[0]:a[1]], ap(a[2]))
+        elif k == "tt":
+            r = q.tensor_tensor(ap(a[0]), ap(a[1]), ap(a[2]), a[3])
+        elif k == "ts":
+            if a[5] is None:
+                r = q.tensor_scalar(ap(a[0]), ap(a[1]), ap(a[2]), None, a[4])
+            else:
+                r = q.tensor_scalar(ap(a[0]), ap(a[1]), ap(a[2]), ap(a[3]), a[4], a[5])
+        elif k == "scan":
+            r = q.tensor_tensor_scan(ap(a[0]), ap(a[1]), ap(a[2]), 0.0, a[3], a[4])
+        elif k == "ms":
+            r = q.memset(ap(a[0]), a[1])
+        elif k == "red":
+            r = q.tensor_reduce(ap(a[0]), ap(a[1]), AxisListType.X, a[2], apply_absolute_value=a[3])
+        elif k == "gatm":
+            r = q.activation(ap(a[0]), ap(a[1]).indirect(ap(a[2])), AF.Identity, ap(a[3]), ap(a[4]))
+        elif k == "gat":
+            w = ap(a[1]).indirect(ap(a[2]))
+            r = q.tensor_copy(ap(a[0]), w) if o["e"] == "dve" else q.activation(ap(a[0]), w, AF.Identity)
+        elif k == "gtt":
+            r = q.tensor_tensor(ap(a[0]), ap(a[1]).indirect(ap(a[2])), ap(a[3]), a[4])
+        elif k == "sca":
+            r = q.tensor_copy(ap(a[0]).indirect(ap(a[1])), ap(a[2]))
+        elif k == "act":
+            if a[5] is None:
+                r = q.activation(ap(a[0]), ap(a[1]), a[2], ap(a[3]), ap(a[4]))
+            else:
+                r = q.activation(ap(a[0]), ap(a[1]), a[2], ap(a[3]), ap(a[4]), accum_out=ap(a[5]))
+        elif k == "mm":
+            r = q.matmul(ap(a[0]), ap(a[1]), ap(a[2]), a[3], a[4])
+        elif k == "mmj":
+            r = q.matmul(ap(a[0]), T["JS"][:, 8 * a[1]:8 * a[1] + 8, :], ap(a[2]), False, a[3])
+        elif k == "iota":
+            if SB[a[0][0]][1] == I32:
+                r = q.iota(ap(a[0]), a[1], a[2], a[3])
+            else:
+                r = q.iota(ap(a[0]), a[1], a[2], a[3], allow_small_or_imprecise_dtypes=True)
+        elif k == "asel":
+            r = q.affine_select(ap(a[0]), ap(a[1]), a[2], a[3], a[4], a[5], a[6])
+        r.then_inc(T.sem[o["sig"][0]], 1)
+    for s, v in ends:
+        wait(g, s, v)
+    g.wait_ge(T.sem["sent"], nsent)
+    for e in ENG[:4]:
+        g.wait_ge(T.sem["c_" + e], count[e])

@@ -4,7 +4,7 @@ from concourse.mybir import AluOpType as OP, AxisListType, ActivationFunctionTyp
 RO = 5
 F32, BF, F16, I32, U16 = "float32", "bfloat16", "float16", "int32", "uint16"
 SB = {
-    "S": (1920, BF), "EF": (2672, BF), "OT": (256, BF), "GL": (128, BF), "RM": (8, BF),
+    "S": (1920, BF), "EF": (2672, BF), "OT": (15136, BF), "SC2": (136, F32), "XF": (128, F32), "CF": (8, F32), "C32": (128, BF), "GL": (128, BF), "RM": (8, BF),
     "QN": (384, I32), "QK": (384, I32), "TU": (128, I32), "TUB": (128, BF),
     "STG": (5 * 264, F16), "SL": (128, BF), "LU": (136, U16), "M3": (5 * 128, F16), "MC": (5 * 128, F32), "MK": (5 * 768, F16), "NG": (4 * 128, BF),
     "OB": (4 * 264, F16), "OL": (128, BF), "O3": (4 * 128, F16), "OC": (4 * 128, F32), "R3": (48, BF), "OK": (5 * 768, F16), "NK": (384, F32), "PF": (32, F32),
@@ -15,7 +15,7 @@ SB = {
     "R17M": (136, BF), "RS0": (1024, BF), "RH": (384, BF), "IDU": (384, F16), "TRI": (512, BF), "BG": (512, BF),
     "NBG": (512, BF), "OHW": (384, BF), "CT": (640, BF), "K2": (384, BF), "KR": (384, BF), "WD": (24, BF), "WT": (24, BF),
     "ZB": (288, BF), "B8B": (8, BF), "I24": (24, BF), "IDL": (32, F32),
-    "LS": (144, U16), "XB": (1024, BF), "T1": (384, BF), "T3": (136, BF), "T4": (48, F32), "TI": (48, I32), "TB": (512, BF),
+    "LS": (152, U16), "XB": (1024, BF), "T1": (384, BF), "T3": (136, BF), "T4": (48, F32), "TI": (48, I32), "TB": (512, BF),
     "SG": (2048, BF), "VS": (2048, BF), "E": (2048, BF), "Y": (2048, BF), "D": (2048, BF), "TT": (2048, BF),
     "SCC": (144, F32), "ST": (144, F32), "PR": (136, F32), "SCS": (136, F32), "NI": (8, I32), "UI": (8, I32), "NA": (8, I32),
     "UA": (8, I32),
@@ -43,18 +43,19 @@ BANKS = ["Z0", "Z1", "W0", "W1", "J1", "J2", "M6", "M7"]
 for _n in BANKS:
     SCRATCH[_n] = ("psum", [128, 8, 64] if _n == "M7" else [128, 512], F32)
 ENG = ["pe", "dve", "act", "pool", "sp"]
-NDMA = 23
+NDMA = 30
 SEMAPHORES = ["c_" + e for e in ENG[:4]] + ["d%d" % i for i in range(NDMA)] + ["sent"] + \
     ["r%d_%d" % (m, t) for m in range(5) for t in range(5)]
 
-PAR = {"cy": 0.95, "pcy": 0.5, "hop": 90.0, "rlat": 2200.0, "dlat": 2200.0, "issue": 500.0, "gf": 1.5,
-       "sa": 60, "eg": [("dve", 0, 32), ("act", 32, 64), ("act", 64, 96), ("act", 96, 128)],
-       "ch": [0, 512, 1024, 1536, 1792, 2048], "seed": 0, "iters": 3, "noise": 60.0,
-       "dd": "dve", "fu": 512,
-       "early": {'act:DX': 3000, 'act:D': 1500, 'pe:J2': 1500, 'dve:NH': -1000, 'dve:TT': 300, 'dve:PR': -1000, 'act:CQ': 800,
-                 'dve:NA': 5000, 'dve:EQ': 800, 'dve:NL': 300, 'dve:OC': -1000, 'dve:PB': 800, 'dve:XD': -1000, 'dve:SCC': -300,
-                 'dve:FF': -1000, 'dve:SU': 5000, 'dve:T2D': 300, 'sp:S': 3000, 'dve:MI': -300, 'act:X': -1000, 'dve:LU': 800,
-                 'act:AC': 1500, 'act:XT': 5000}}
+PAR = {"cy": 1.0, "pcy": 0.5, "hop": 150.0, "rlat": 1500.0, "dlat": 2200.0, "issue": 700.0, "gf": 1.6, "bw": 100.0, "fix": 20.0, "sf": 4.0,
+       "sa": 56, "eg": [("dve", 0, 32), ("act", 32, 64), ("act", 64, 96), ("act", 96, 128)],
+       "ch": [0, 512, 1024, 1536, 2048], "seed": 0, "iters": 3, "noise": 60.0,
+       "dd": "act", "fu": 512,
+       "early": {'act:D': 300, 'dve:NA': 800, 'dve:EQ': 800, 'dve:PB': 1500, 'dve:Y': 3000, 'dve:KM': 3000, 'dve:SQ': 800,
+                 'dve:LU': -300, 'dve:OK': 3000, 'dve:O3': 800, 'dve:PX': 3000, 'act:OH': 300, 'dve:PE2': -300, 'act:GP': 3000,
+                 'dve:UI': -300, 'act:OL': 1500, 'act:NK': -1000, 'dve:S': -300, 'dve:UP': -1000, 'dve:P1': -1000,
+                 'act:CQ': 1500, 'dve:XO': -300, 'act:TB': 800, 'act:MN': 5000, 'act:A2': 5000, 'dve:XD': 3000, 'act:YP': -300,
+                 'pe:M6': 3000, 'dve:PF': 3000}}
 PAR["off"] = []
 
 
@@ -86,7 +87,8 @@ def build():
     CY, PCY, GF = PAR["cy"], PAR["pcy"], PAR["gf"]
 
     def op(eng, kind, args, rd, wr, cost, **kw):
-        d = {"e": eng, "k": kind, "a": args, "rd": [r for r in rd if isinstance(r, tuple)], "wr": wr, "c": cost, "st": now[0]}
+        d = {"e": eng, "k": kind, "a": args, "rd": [r for r in rd if isinstance(r, tuple)], "wr": wr,
+             "c": cost + (PAR["fix"] if eng in ("dve", "act") else 0.0), "st": now[0]}
         d.update(kw)
         ops.append(d)
         return d
@@ -137,7 +139,8 @@ def build():
         nd[0] += 1
 
     def send(m, t, prs, extra=0.0):
-        op("pool", "send", (m, t, prs), [p[1] for p in prs], [p[0] for p in prs], PAR["issue"], lat=PAR["rlat"] + extra,
+        op("pool", "send", (m, t, prs), [p[1] for p in prs], [p[0] for p in prs],
+           PAR["issue"] + cnt(prs[0][0]) * (256 if two(prs[0][0]) else 512) / PAR["bw"], lat=PAR["rlat"],
            sem="r%d_%d" % (m, t))
 
     def C(j):
@@ -152,10 +155,12 @@ def build():
     dma("sp", A("S", 0, 1792), "st0", [], [A("S", 0, 1792)], 1200)
     dma("act", A("QK"), "qk", [], [A("QK")], 1500)
     dma("sp", A("GL"), "gl", [], [A("GL")], 1500)
-    dma("sp", A("OT"), "ot", [], [A("OT")], 1700)
+    dma("sp", A("OT", 0, 256), "ot", [], [A("OT", 0, 256)], 1700)
     dma("sp", A("RM", 0, 1), "rm", [], [A("RM")], 1700)
     dma("sp", A("EF", 0, 2048), "ef", [], [A("EF", 0, 2048)], 2800)
     dma("sp", A("EF", 2048, 2672), ("ef", 0, 624), [], [A("EF", 2048, 2672)], 3200)
+    for a, b in ((256, 256), (512, 512), (1024, 1024), (2048, 2048), (4096, 4096), (8192, 4096), (12288, 2848)):
+        dma("sp", A("OT", a, a + b), A("OT", 0, b), [A("OT", 0, b)], [A("OT", a, a + b)], 1.5 * b)
 
     iota(A("CI", 0, 1), [[0, 1]], 0, 1)
     iota(A("TI", 0, 24), [[1, 24]], 0, 0)
@@ -196,7 +201,9 @@ def build():
     ts(A("LS", 58, 66), A("TI", 0, 8), 2.0, C(11), OP.mult, OP.add)
     ts(A("T4", 0, 9), A("TI", 0, 9), 16.0, C(1), OP.mult, OP.add)
     ts(A("TI", 32, 41), A("T4", 0, 9), 1.0 / 17, -0.47, OP.mult, OP.add)
-    ts(A("LS", 66, 75), A("TI", 32, 41), 7.0, None, OP.min)
+    ts(A("T4", 32, 41), A("TI", 32, 41), 17.0, 16.0, OP.mult, OP.add)
+    ts(A("LS", 66, 75), A("T4", 32, 41), 135.0, None, OP.min)
+    ts(A("LS", 140, 148), A("TI", 0, 8), 17.0, 16.0, OP.mult, OP.add)
     ts(C(3), C(3), 8.0, C(2), OP.mult, OP.add)
     ts(C(5), C(10), C(6), None, OP.add)
     ts(C(6), C(0), 1792.0, None, OP.add)
@@ -208,7 +215,7 @@ def build():
     ts(C(15), C(0), 1.0, 2048.0, OP.is_equal, OP.mult)
     ts(C(16), C(0), 2.0 ** 24 - 2048, -2.0 ** 24, OP.mult, OP.add)
     ts(C(21), C(1), 128.0, None, OP.mult)
-    ms(C(23), 32.0)
+    ms(A("C32"), 32.0)
     ms(C(13), -63.5)
     ms(C(22), -127.5)
     ts(C(32), C(1), 37.0, -64.0, OP.mult, OP.add)
@@ -227,6 +234,7 @@ def build():
         act(blk("WM", l, 8), A("BX", 0, 8), scale=1024.0)
     ts(A("CM", 0, 8), A("TI", 0, 8), C(4), None, OP.is_equal)
     act(A("CM", 8, 16), A("CM", 0, 8), scale=0.125)
+    act(A("CF"), A("CM", 0, 8), scale=0.125)
     ts(A("MX"), A("T1", 0, 128), C(3), None, OP.is_equal)
     asel(A("EN"), A("ONB", 0, 136), [[-16, 8], [-1, 17]], OP.is_equal, 1, 1)
     ms(A("EN", 0, 136, 17), 0.0)
@@ -246,7 +254,7 @@ def build():
     ms(A("R3", 0, 48, 3), 0.0)
     asel(A("BLK"), A("ONB", 0, 128), [[-16, 8], [0, 16]], OP.is_ge, 0, 1)
     asel(A("BLK"), A("BLK"), [[16, 8], [0, 16]], OP.is_ge, 15, -1)
-    act(A("WU"), A("BLK"), scale=C(12))
+    ts(A("WU"), A("BLK"), C(12), 2.0, OP.mult, OP.mult)
     act(A("I15"), A("IB"), scale=C(8))
     act(A("NIB"), A("IB"), scale=-1.0)
     act(A("I2K"), A("IB"), scale=2048.0)
@@ -347,25 +355,31 @@ def build():
         for k in range(16):
             mm(A("J1", k, 384, 16), A("SG", k, 2048, 16), A("WM"), False, k == 15)
         scan(A("SCC", 0, 136), A("R17H"), A("M6", 0, 136), OP.add, OP.min)
+        scan(A("SC2"), A("R17H"), A("M6", 0, 136), OP.add, OP.min)
         cp(A("NI"), A("SCC", 16, 136, 17))
-        gtt(A("ST"), A("NI"), A("LS", 66, 75), A("SCC"), OP.is_equal)
+        gtt(A("ST"), A("SC2"), A("LS", 66, 75), A("SCC"), OP.is_equal)
         ts(A("NA"), A("NI"), 2047, None, OP.bitwise_and)
         tt(A("PR"), G(0, 17), A("ST", 0, 136), OP.mult)
         gtt(A("XN"), A("NA"), A("LS", 0, 8), A("MX"), OP.mult)
         scan(A("SCS"), A("R17M"), A("PR"), OP.mult, OP.add)
         mm(A("M6", 0, 8), A("XN"), A("CM", 0, 8), True, True)
-        cp(A("UI"), A("SCS", 16, 136, 17))
         cp(A("LX", 0, 8), A("M6", 0, 8))
-        ts(A("UA"), A("UI"), 2047, None, OP.bitwise_and)
-        gtt(A("XO"), A("UA"), A("LS", 0, 8), A("MX"), OP.mult)
         gat("act", A("X"), SW, A("LX", 0, 8))
-        mm(A("M6", 8, 16), A("XO"), A("CM", 8, 16), True, True)
-        mm(A("Z1", 0, 128), A("WU"), A("X"), True, True)
+        if t == 0:
+            cp(A("UI"), A("SCS", 16, 136, 17))
+            ts(A("UA"), A("UI"), 2047, None, OP.bitwise_and)
+            gtt(A("XO"), A("UA"), A("LS", 0, 8), A("MX"), OP.mult)
+            mm(A("W0", 0, 8), A("XO"), A("CM", 8, 16), True, True)
+        else:
+            gtt(A("XF"), A("SCS"), A("LS", 140, 148), A("MX"), OP.mult)
+            mm(A("W0", 0, 8), A("XF"), A("CF"), True, True)
+        mm(A("Z1", 0, 128), A("ONB", 0, 128, p1=1), A("C32", p1=1), True, False)
+        mm(A("Z1", 0, 128), A("WU"), A("X"), False, True)
         mm(A("Z0", 0, 128), A("X"), A("I15"), True, True)
-        cp(A("LX", 8, 16), A("M6", 8, 16))
-        act(A("UP"), A("Z1", 0, 128), bias=C(23), scale=2.0)
+        cp(A("LX", 8, 16), A("W0", 0, 8))
         act(A("XT"), A("Z0", 0, 128))
-        gtt(A("N1"), A("OT"), A("LX", 8, 16), A("UP"), OP.mult)
+        gat("dve", A("UP"), A("OT", 0, 256 if t == 0 else 15136), A("LX", 8, 16))
+        tt(A("N1"), A("Z1", 0, 128), A("UP"), OP.mult)
         ts(A("N2"), A("N1"), 5, 2047, OP.arith_shift_right, OP.bitwise_and)
         ts(A("NL"), A("N2"), A("AC", 0, 1), None, OP.add)
         mm(A("W1", 0, 128), A("XN"), A("IB"), True, True)
@@ -517,7 +531,7 @@ def build():
            60 + 128 * GF * CY)
         for h in range(2):
             op("dve", "sca", (A("S"), blk("LX", h, 4, 16), blk("XM", h, 64)), [blk("LX", h, 4, 16), blk("XM", h, 64)], [A("S")],
-               55 + 64 * 3 * CY)
+               55 + 64 * PAR["sf"] * CY)
         if not last:
             gat("act", blk("S", t), A("Y"), A("LA", 0, 8))
             cp(A("LU"), A("STG", u1 + 392, u1 + 528))

@@ -1,36 +1,36 @@
 import numpy as np
-from concourse.mybir import AluOpType as OP, AxisListType, ActivationFunctionType as AF
+from concourse.mybir import AluOpType as OP, ActivationFunctionType as AF
 
 RO = 5
 F32, BF, F16, I32, U16 = "float32", "bfloat16", "float16", "int32", "uint16"
 SB = {
-    "S": (1920, BF), "EF": (2672, BF), "OT": (15136, BF), "SC2": (136, F32), "XF": (128, F32), "CF": (8, F32), "C32": (128, BF), "GL": (128, BF), "RM": (8, BF),
-    "QN": (384, I32), "QK": (384, I32), "TU": (128, I32), "TUB": (128, BF),
-    "STG": (5 * 264, F16), "SL": (128, BF), "LU": (136, U16), "M3": (5 * 128, F16), "MC": (5 * 128, F32), "MK": (5 * 768, F16), "NG": (4 * 128, BF),
-    "OB": (4 * 264, F16), "OL": (128, BF), "O3": (4 * 128, F16), "OC": (4 * 128, F32), "R3": (48, BF), "OK": (5 * 768, F16), "NK": (384, F32), "PF": (32, F32),
-    "CI": (16, I32), "CC": (40, F32), "IB": (128, BF), "I15": (128, BF), "NIB": (128, BF), "I2K": (128, BF),
-    "N2K": (128, BF), "REP": (2048, BF), "BLK": (128, BF), "WU": (128, BF), "MX": (128, BF),
-    "CM": (16, BF), "B8": (8, F32), "BX": (32, F32), "DG": (384, BF), "PM": (128, BF), "WS": (32, BF), "WM": (24, BF),
-    "WX": (384, BF), "EC": (136, BF), "EN": (136, BF), "CR": (136, BF), "ONB": (1024, BF), "R17H": (136, BF),
-    "R17M": (136, BF), "RS0": (1024, BF), "RH": (384, BF), "IDU": (384, F16), "TRI": (512, BF), "BG": (512, BF),
-    "NBG": (512, BF), "OHW": (384, BF), "CT": (640, BF), "K2": (384, BF), "KR": (384, BF), "WD": (24, BF), "WT": (24, BF),
-    "ZB": (288, BF), "B8B": (8, BF), "I24": (24, BF), "IDL": (32, F32),
-    "LS": (152, U16), "XB": (1024, BF), "T1": (384, BF), "T3": (136, BF), "T4": (48, F32), "TI": (48, I32), "TB": (512, BF),
-    "SG": (2048, BF), "VS": (2048, BF), "E": (2048, BF), "Y": (2048, BF), "D": (2048, BF), "TT": (2048, BF),
-    "SCC": (144, F32), "ST": (144, F32), "PR": (136, F32), "SCS": (136, F32), "NI": (8, I32), "UI": (8, I32), "NA": (8, I32),
-    "UA": (8, I32),
-    "XN": (128, F16), "XO": (128, F16), "XD": (128, F16), "LX": (24, U16), "X": (128, BF), "XM": (128, BF), "XT": (128, BF),
-    "UP": (128, F32), "N1": (128, I32), "N2": (128, I32), "NL": (128, U16), "AC": (16, F32), "AI": (8, I32), "AG": (8, BF),
-    "DX": (128, BF), "TX": (128, BF), "NH": (24, F16), "SU": (384, F32), "PB": (48, F32), "P1": (48, F32), "AB": (16, I32),
-    "AL": (24, I32), "GO": (16, F32), "LA": (24, U16), "OH": (128, BF), "KM": (384, F16), "CQ": (384, F32), "SQ": (384, F32),
-    "EQ": (384, BF), "KH": (768, F16), "A2": (384, F32), "RN": (384, F32), "CK": (384, F32), "NX": (128, F16), "MN": (32, F32), "T2D": (8, F32),
-    "PX": (56, F32), "MM": (16, F32), "MI": (32, I32), "DL": (8, F32), "FF": (8, F32), "YQ": (384, F32),
-    "YP": (384, F32), "PE2": (384, BF), "GP": (128, BF), "JK": (128, BF),
+    "S": (2048, BF), "EF": (2672, BF), "OT": (15136, BF), "GL": (128, BF), "RM": (8, BF),
+    "QN": (384, I32), "QK": (384, I32), "TU": (128, I32), "MKS": (128, BF),
+    "STG": (5 * 256, F16), "SL": (128, BF), "M3": (5 * 136, F16), "MC": (5 * 136, F32), "MK": (5 * 768, F16), "NG": (4 * 128, BF),
+    "OB": (4 * 256, F16), "OL": (128, BF), "O3": (4 * 136, F16), "OC": (4 * 136, F32), "OK": (5 * 768, F16),
+    "YQ": (384, F32), "YP": (384, F32), "GP": (128, BF),
+    "CI": (16, I32), "CC": (48, F32), "IB": (128, BF), "I15": (128, BF), "NIB": (128, BF), "I8K": (128, BF), "I4K": (128, BF),
+    "I1K": (128, BF), "N1K": (128, BF), "IA": (128, F16), "IM": (128, F16), "REP": (1024, BF), "BLK": (128, BF), "MX": (128, BF),
+    "CM": (16, BF), "CF": (8, F32), "B8": (8, F32), "BX": (32, F32), "DG": (384, BF), "PM": (128, BF), "WU": (128, BF),
+    "WS": (16, BF), "WM": (24, BF), "WX": (384, BF), "EC": (136, BF), "EN": (136, BF), "CR": (136, BF), "ONB": (136, BF),
+    "R17H": (136, BF), "RS0": (512, BF), "RH": (384, BF), "IDU": (384, F16), "OHW": (384, BF),
+    "WD": (24, BF), "WT": (24, BF), "ZB": (384, BF), "BD": (432, BF), "JS": (384, F16), "B8B": (8, BF), "P24": (32, BF), "ID4": (32, F32), "R4": (32, F32),
+    "LI": (88, I32), "LS": (192, U16), "XB": (1024, BF), "T1": (512, BF), "T3": (144, BF), "T4": (48, F32), "TI": (48, I32),
+    "CH": (256, BF), "KP": (16, F32), "DH": (384, F16), "D0": (64, F32),
+    "TUB": (128, BF), "LU": (136, U16), "SG": (2048, BF), "VS": (2048, BF), "E": (2048, BF), "Y": (2048, BF), "D": (2048, BF),
+    "TT": (2048, BF), "SCI": (160, I32), "SC2": (160, F32), "ST": (144, F32), "SN": (136, F32), "PR": (136, F32), "SCS": (136, F32), "UI": (8, I32),
+    "NA": (8, I32), "UA": (8, I32), "XN": (128, F16), "XF": (128, F32), "LX": (16, U16), "X": (128, BF), "XT": (128, BF),
+    "UB": (128, F32), "U": (128, F32), "N1": (128, I32), "N2": (128, I32), "NL": (128, U16), "AC": (16, F32),
+    "DX": (128, BF), "TX": (128, BF), "NH": (48, F16), "NH2": (24, F16), "SU": (512, F32), "PB": (64, F32), "P1": (64, I32),
+    "GO": (8, BF), "LA": (24, U16), "AL": (16, I32), "OH": (128, BF), "KM": (384, F16), "SQ": (400, F16), "EQ": (384, BF), "KH": (384, F16),
+    "A2": (384, F16), "RN": (384, F16), "NK": (384, F32), "CK": (384, F32), "PF": (32, F32), "PX": (32, F32), "MM": (64, I32),
+    "EQ4": (32, F32), "E5": (32, F32), "MI": (16, I32), "HI": (16, I32), "LO": (8, F32), "OHH": (256, BF), "OHL": (1024, BF),
+    "PI": (32, I32), "PJ": (32, I32), "PE2": (384, BF),
 }
 PACK = {}
 for _n in list(SB):
     _w, _d = SB[_n]
-    if _w <= 48 and _n != "RM":
+    if _w <= 64 and _n != "RM":
         _o = SB.get("small_" + _d, (0, _d))[0]
         PACK[_n] = ("small_" + _d, _o)
         SB["small_" + _d] = (_o + (_w + 15) // 16 * 16, _d)
@@ -38,25 +38,33 @@ SCRATCH = {}
 for _n in SB:
     if _n not in PACK:
         SCRATCH[_n] = ("sbuf", [128, SB[_n][0]], SB[_n][1])
-SCRATCH["JS"] = ("sbuf", [128, 24, 16], F16)
 BANKS = ["Z0", "Z1", "W0", "W1", "J1", "J2", "M6", "M7"]
 for _n in BANKS:
-    SCRATCH[_n] = ("psum", [128, 8, 64] if _n == "M7" else [128, 512], F32)
+    SCRATCH[_n] = ("psum", [128, 2, 256] if _n == "Z0" else [128, 512], F32)
 ENG = ["pe", "dve", "act", "pool", "sp"]
-NDMA = 30
+NDMA = 40
 SEMAPHORES = ["c_" + e for e in ENG[:4]] + ["d%d" % i for i in range(NDMA)] + ["sent"] + \
     ["r%d_%d" % (m, t) for m in range(5) for t in range(5)]
 
-PAR = {"cy": 1.0, "pcy": 0.5, "hop": 150.0, "rlat": 1500.0, "dlat": 2200.0, "issue": 700.0, "gf": 1.6, "bw": 100.0, "fix": 20.0, "sf": 4.0,
-       "sa": 56, "eg": [("dve", 0, 32), ("act", 32, 64), ("act", 64, 96), ("act", 96, 128)],
-       "ch": [0, 512, 1024, 1536, 2048], "seed": 0, "iters": 3, "noise": 60.0,
-       "dd": "act", "fu": 512,
-       "early": {'act:D': 300, 'dve:NA': 800, 'dve:EQ': 800, 'dve:PB': 1500, 'dve:Y': 3000, 'dve:KM': 3000, 'dve:SQ': 800,
-                 'dve:LU': -300, 'dve:OK': 3000, 'dve:O3': 800, 'dve:PX': 3000, 'act:OH': 300, 'dve:PE2': -300, 'act:GP': 3000,
-                 'dve:UI': -300, 'act:OL': 1500, 'act:NK': -1000, 'dve:S': -300, 'dve:UP': -1000, 'dve:P1': -1000,
-                 'act:CQ': 1500, 'dve:XO': -300, 'act:TB': 800, 'act:MN': 5000, 'act:A2': 5000, 'dve:XD': 3000, 'act:YP': -300,
-                 'pe:M6': 3000, 'dve:PF': 3000}}
-PAR["off"] = []
+PAR = {"cy": 0.95, "pcy": 0.5, "hop": 180.0, "rlat": 1200.0, "dlat": 2200.0, "issue": 500.0, "gf": 1.56, "bw": 100.0, "fix": 0.0,
+       "sg": [("dve", 0, 32), ("dve", 32, 64), ("act", 64, 96), ("act", 96, 128)], "sm": [(0, 32), (64, 96), (32, 64), (96, 128)],
+       "vs": [0, 512, 1024, 1536, 1792, 2048],
+       "eg": [("dve", 64, 80), ("dve", 80, 96), ("dve", 96, 112), ("dve", 112, 128), ("act", 0, 16), ("act", 16, 48), ("act", 48, 64)],
+       "ch": [(1024, 1536, "", "W1"), (0, 256, "Z0", "W0"), (256, 768, "Z1", "J2"), (768, 1024, "Z0", "W1"), (1536, 1792, "", "W0"),
+              (1792, 2048, "", "J2")],
+       "seed": 0, "iters": 35000, "warm": 120.0, "fu": 1024,
+       "lead": 2000.0, "turned": 4,
+       "cases": [(1.09, 100.0, 0.0), (0.88, 250.0, 300.0)],
+       "on": {"N16": "dve", "JS": "dve", "O3": "dve", "LX0": "act", "LX1": "dve", "yb": "act", "nm": "dve", "Sb": "dve", "lab": "act"}}
+
+
+ORDER = {
+    "dve": "SG SG VS VS VS VS SCI SC2 NA ST XN PR VS HI HI SCS KM XF KM KM UI UA LX SQ N1 TX OHL*2 N2 OHL*3 NL OHL*3 E E OHH y0 y1 E y2 "
+           "y3 t0 E y4 t1 OHH y5 t2 t3 OHH js t4 t5 OHH SU PB MKS P1 AL GO OB OK OK PX PF MM O3 EQ4 OC MM MI LU S PI PJ PE2",
+    "act": "SG SG LU OH DH*3 SN LX LO X XB U XT DX XB XB NH NH NH2 E E E XB d0 EQ d1 d2 d3 d4 d5 RN D0 NK A2 LA lab OB OL O3 CK S GP ys AC*2 E5 OC*3 AC*4 OC*2",
+    "pe": "cd*3 mk0 cd*69 mk*17 J2 M6 v*17 Z1 W0 Z0 J2 wg0 wg1 zx1 zx2 J2*2 idu eq*20 wg2 hx*9 ze1 hx*8 wy0 ze2 wy1 zx3 ze3 sd0*4 wy2 wg3 wy3 st0*4 "
+          "rn*4 sd1*2 wg4 wy4 st1*2 wg5 wy5 sd2*4 st2*4 sd3*2 st3*2 sd4*4 sd5*4 st4*2 mmj*3 st5*2 mrk*10 nk*4 nr W1*2 W0*17 J1 W1*4",
+    "pool": "NG STG SL M3 MK MC", "sp": "S"}
 
 
 def A(n, a=0, b=None, s=1, p0=0, p1=128):
@@ -67,13 +75,13 @@ def A(n, a=0, b=None, s=1, p0=0, p1=128):
     return (n, a, b, s, p0, p1)
 
 
-def G(a, b):
-    return ("M7", a, 448 + b, 1, 0, 128, (a, b))
+def G(a, b, s=1, p0=0, p1=128):
+    return ("Z0", a, 256 + b, 2, p0, p1, (a, b, s))
 
 
 def cnt(x):
     if len(x) == 7:
-        return 8 * (x[6][1] - x[6][0])
+        return 2 * ((x[6][1] - x[6][0] + x[6][2] - 1) // x[6][2])
     return (x[2] - x[1] + x[3] - 1) // x[3]
 
 
@@ -83,12 +91,12 @@ def two(x):
 
 def build():
     ops = []
-    now = [-1]
-    CY, PCY, GF = PAR["cy"], PAR["pcy"], PAR["gf"]
+    now, tag = [-1], [""]
+    CY, PCY, GF, ON = PAR["cy"], PAR["pcy"], PAR["gf"], PAR["on"]
 
     def op(eng, kind, args, rd, wr, cost, **kw):
         d = {"e": eng, "k": kind, "a": args, "rd": [r for r in rd if isinstance(r, tuple)], "wr": wr,
-             "c": cost + (PAR["fix"] if eng in ("dve", "act") else 0.0), "st": now[0]}
+             "c": cost + (PAR["fix"] if eng in ("dve", "act") else 0.0), "st": now[0], "tag": tag[0]}
         d.update(kw)
         ops.append(d)
         return d
@@ -97,8 +105,14 @@ def build():
         f = 0.5 if all(two(x) for x in aps) else 1.0
         return max(64.0, n * f) * CY
 
-    def cp(o, i):
-        op("dve", "cp", (o, i), [i], [o], vc(cnt(o), o, i))
+    def act(o, i, f=AF.Identity, bias=0.0, scale=1.0, acc=None):
+        op("act", "act", (o, i, f, bias, scale, acc), [i, bias, scale], [o] + ([acc] if acc else []), max(64.0, cnt(o)) * CY)
+
+    def cp(o, i, e="dve"):
+        if e == "act":
+            act(o, i)
+        else:
+            op("dve", "cp", (o, i), [i], [o], vc(cnt(o), o, i))
 
     def tt(o, a, b, f):
         k = 1 if (a[0] in BANKS or b[0] in BANKS) else 2
@@ -113,14 +127,11 @@ def build():
     def ms(o, v):
         op("dve", "ms", (o, v), [], [o], vc(cnt(o), o))
 
-    def gat(e, o, w, l):
-        op(e, "gat", (o, w, l), [w, l], [o], 60 + cnt(o) * GF * CY)
+    def gat(e, o, w, l, bias=0.0, scale=1.0):
+        op(e, "gat", (o, w, l, bias, scale), [w, l, bias, scale], [o], 60 + cnt(o) * GF * CY)
 
     def gtt(o, w, l, b, f):
         op("dve", "gtt", (o, w, l, b, f), [w, l, b], [o], 55 + cnt(o) * GF * CY)
-
-    def act(o, i, f=AF.Identity, bias=0.0, scale=1.0, acc=None):
-        op("act", "act", (o, i, f, bias, scale, acc), [i, bias, scale], [o] + ([acc] if acc else []), max(64.0, cnt(o)) * CY + 30)
 
     def mm(o, l, r, st, sp):
         f = 4 if SB.get(l[0], (0, 0))[1] == F32 else 1
@@ -138,16 +149,18 @@ def build():
         op(e, "dma", (o, i), rd, wr, 60.0, lat=PAR["dlat"] + extra, sem="d%d" % nd[0])
         nd[0] += 1
 
-    def send(m, t, prs, extra=0.0):
-        op("pool", "send", (m, t, prs), [p[1] for p in prs], [p[0] for p in prs],
-           PAR["issue"] + cnt(prs[0][0]) * (256 if two(prs[0][0]) else 512) / PAR["bw"], lat=PAR["rlat"],
-           sem="r%d_%d" % (m, t))
+    def send(m, t, dst, src):
+        op("pool", "send", (dst, src), [src], [dst], PAR["issue"] + cnt(dst) * (256 if two(dst) else 512) / PAR["bw"],
+           lat=PAR["rlat"], sem="r%d_%d" % (m, t))
 
     def C(j):
         return A("CC", j, j + 1)
 
     def blk(n, j, w=128, o=0):
         return A(n, o + w * j, o + w * j + w)
+
+    def half(n, h, a=0, b=None):
+        return A(n, a, b, 1, 64 * h, 64 * h + 64)
 
     for q in range(8):
         dma("act" if q % 2 else "sp", A("TU", 16 * q, 16 * q + 16, p1=24), ("tu", q), [], [A("TU", 16 * q, 16 * q + 16)])
@@ -159,67 +172,74 @@ def build():
     dma("sp", A("RM", 0, 1), "rm", [], [A("RM")], 1700)
     dma("sp", A("EF", 0, 2048), "ef", [], [A("EF", 0, 2048)], 2800)
     dma("sp", A("EF", 2048, 2672), ("ef", 0, 624), [], [A("EF", 2048, 2672)], 3200)
+    ms(A("S", 1792, 2048), 0.0)
+    dma("sp", A("MKS"), "marks", [A("S")], [A("MKS")])
     for a, b in ((256, 256), (512, 512), (1024, 1024), (2048, 2048), (4096, 4096), (8192, 4096), (12288, 2848)):
         dma("sp", A("OT", a, a + b), A("OT", 0, b), [A("OT", 0, b)], [A("OT", a, a + b)], 1.5 * b)
 
+    BIG = 2.0 ** 24
     iota(A("CI", 0, 1), [[0, 1]], 0, 1)
     iota(A("TI", 0, 24), [[1, 24]], 0, 0)
-    iota(A("T1"), [[0, 24], [1, 16]], 0, 0)
-    iota(A("IDL"), [[128, 4], [16, 8]], 0, 0)
+    iota(A("ID4"), [[16, 8], [128, 4]], 0, 0)
     ms(A("ONB"), 1.0)
-    ms(A("K2"), -2048.0)
-    ms(A("I24"), 1.0)
-    asel(A("I24"), A("I24"), [[1, 24]], OP.is_equal, 0, -1)
+    ms(A("P24"), 512.0)
+    asel(A("P24"), A("P24"), [[1, 8], [8, 4]], OP.is_equal, 0, -1)
     asel(A("IB"), A("ONB", 0, 128), [[-1, 128]], OP.is_equal, 0, 1)
-    iota(A("T3"), [[1, 136]], 0, 0)
-    ts(A("CI", 1, 2), A("CI", 0, 1), 15, None, OP.bitwise_and)
-    ts(A("CI", 2, 3), A("CI", 0, 1), 4, None, OP.arith_shift_right)
-    ts(A("CI", 3, 4), A("CI", 0, 1), 1, None, OP.bitwise_and)
-    ts(A("CI", 4, 5), A("CI", 0, 1), 1, 7, OP.arith_shift_right, OP.bitwise_and)
-    ts(A("CI", 5, 6), A("CI", 0, 1), 7, None, OP.bitwise_and)
-    ts(A("CI", 6, 7), A("CI", 0, 1), 3, None, OP.arith_shift_right)
+    iota(A("T1"), [[0, 32], [1, 16]], 0, 0)
+    iota(A("T3"), [[1, 144]], 0, 0)
+    iota(A("REP"), [[1, 64], [0, 16]], 0, 0)
+    iota(A("CH"), [[0, 4], [-16, 2], [1, 32]], 0, 0)
+    for j, (sh, m) in enumerate(((0, 15), (4, 7), (0, 1), (1, 7), (0, 7), (3, 15), (2, 3), (0, 3), (0, 63))):
+        ts(A("CI", 1 + j, 2 + j), A("CI", 0, 1), sh, m, OP.arith_shift_right, OP.bitwise_and)
     cp(A("CC", 0, 7), A("CI", 0, 7))
-    ts(A("DG"), A("T1"), C(1), None, OP.is_equal)
-    ms(A("RS0"), 1.0)
-    ms(A("RS0", 0, 1024, 16), 0.0)
-    ts(A("IDL"), A("IDL"), C(1), 1.0 / 2048, OP.add, OP.mult)
-    cp(A("LS", 0, 24), A("TI", 0, 24))
-    ts(A("LS", 24, 48), A("TI", 0, 24), 16.0, 15.0, OP.mult, OP.add)
-    ts(C(10), C(5), 16.0, None, OP.mult)
-    ts(A("LS", 52, 54), A("TI", 0, 2), 0.0, C(10), OP.mult, OP.add)
-    ts(A("LS", 52, 54), A("LS", 52, 54), 0.0625, None, OP.mult)
-    ts(A("LS", 76, 140), A("T3", 0, 64), 0.0, None, OP.add)
-    ts(A("T4", 16, 19), A("TI", 0, 3), 16.0, C(1), OP.mult, OP.add)
-    ts(A("T4", 20, 23), A("T4", 16, 19), 24.0, -24.0, OP.is_ge, OP.mult)
-    tt(A("T4", 16, 19), A("T4", 16, 19), A("T4", 20, 23), OP.add)
-    ts(A("TI", 44, 47), A("T4", 16, 19), 1.0 / 3, -0.33, OP.mult, OP.add)
-    ts(A("T4", 20, 23), A("TI", 44, 47), -368.0, 15.0, OP.mult, OP.add)
-    ts(A("T4", 16, 19), A("T4", 16, 19), 128.0, None, OP.mult)
-    tt(A("T4", 24, 27), A("T4", 16, 19), A("T4", 20, 23), OP.add)
-    cp(A("LS", 48, 51), A("T4", 24, 27))
-    ts(C(11), C(1), 8.0, C(10), OP.is_ge, OP.add)
-    ts(A("LS", 58, 66), A("TI", 0, 8), 2.0, C(11), OP.mult, OP.add)
+    cp(A("CC", 22, 25), A("CI", 7, 10))
+    act(A("ID4"), A("ID4"), bias=C(1))
+    ms(A("ID4", 3, 32, 4), 2.0 ** 20)
+    ms(A("R4"), 0.0)
+    ms(A("R4", 0, 32, 4), 2 * BIG)
+    for a, pat, base in ((0, [[1, 32]], 0), (32, [[1, 8], [0, 2]], 0), (48, [[17, 16]], 16), (64, [[1, 3], [4, 8]], 0)):
+        iota(A("LI", a, a + int(np.prod([x[1] for x in pat]))), pat, base, 0)
+    cp(A("LS", 0, 88), A("LI"))
+    cp(A("LS", 114, 178), A("T3", 0, 64))
+    ts(C(25), C(22), 4.0, 3.0, OP.mult, OP.add)
+    ts(A("LS", 106, 108), A("TI", 0, 2), 16.0, C(25), OP.mult, OP.add)
+    ts(A("LS", 108, 110), A("TI", 0, 2), 4.0, C(22), OP.mult, OP.add)
+    ts(C(11), C(5), 16.0, None, OP.mult)
+    ts(C(26), C(1), 8.0, C(11), OP.is_ge, OP.add)
+    ts(A("LS", 88, 96), A("TI", 0, 8), 2.0, C(26), OP.mult, OP.add)
     ts(A("T4", 0, 9), A("TI", 0, 9), 16.0, C(1), OP.mult, OP.add)
     ts(A("TI", 32, 41), A("T4", 0, 9), 1.0 / 17, -0.47, OP.mult, OP.add)
-    ts(A("T4", 32, 41), A("TI", 32, 41), 17.0, 16.0, OP.mult, OP.add)
-    ts(A("LS", 66, 75), A("T4", 32, 41), 135.0, None, OP.min)
-    ts(A("LS", 140, 148), A("TI", 0, 8), 17.0, 16.0, OP.mult, OP.add)
-    ts(C(3), C(3), 8.0, C(2), OP.mult, OP.add)
-    ts(C(5), C(10), C(6), None, OP.add)
-    ts(C(6), C(0), 1792.0, None, OP.add)
-    ts(C(7), C(1), 37.0, None, OP.mult)
+    ts(A("T4", 16, 25), A("TI", 32, 41), 17.0, None, OP.mult)
+    tt(A("T4", 0, 9), A("T4", 0, 9), A("T4", 16, 25), OP.not_equal)
+    ts(A("T4", 16, 25), A("T4", 16, 25), 32.0, 152.0, OP.add, OP.min)
+    tt(A("LS", 96, 105), A("T4", 0, 9), A("T4", 16, 25), OP.mult)
+    ms(A("SC2"), -2.0 ** 30)
+    ms(A("SCI"), 0)
+    ms(C(38), 15.0)
+    act(C(27), C(22), bias=C(38), scale=16.0)
+    act(C(28), C(23), bias=C(27), scale=128.0)
+    ts(C(39), C(23), 2.0, -384.0, OP.is_ge, OP.mult)
+    ts(C(39), C(39), 128.0, C(28), OP.add, OP.add)
+    ts(A("LS", 110, 112), A("TI", 0, 2), 64.0, C(28), OP.mult, OP.add)
+    ts(A("LS", 112, 114), A("TI", 0, 2), 64.0, C(39), OP.mult, OP.add)
+    act(C(3), C(3), bias=C(2), scale=8.0)
+    act(C(5), C(6), bias=C(11))
+    act(C(7), C(1), scale=37.0)
     ts(C(8), C(1), 15.0, None, OP.not_equal)
     ts(C(9), C(1), 15.0, None, OP.is_equal)
     ts(C(12), C(1), 0.5, C(8), OP.add, OP.mult)
     ts(C(14), C(1), 3.0, -2048.0, OP.is_lt, OP.mult)
     ts(C(15), C(0), 1.0, 2048.0, OP.is_equal, OP.mult)
-    ts(C(16), C(0), 2.0 ** 24 - 2048, -2.0 ** 24, OP.mult, OP.add)
-    ts(C(21), C(1), 128.0, None, OP.mult)
-    ms(A("C32"), 32.0)
-    ms(C(13), -63.5)
-    ms(C(22), -127.5)
+    ts(C(16), C(0), BIG - 2048, -BIG, OP.mult, OP.add)
+    act(C(21), C(1), scale=128.0)
+    for j, v in ((13, -63.5), (20, -127.5), (33, -0.5), (34, -1024.0), (35, BIG), (36, 32.0), (37, 1024.0), (40, 2.0 ** 27)):
+        ms(C(j), v)
     ts(C(32), C(1), 37.0, -64.0, OP.mult, OP.add)
-    ms(A("MC", 104, 112), 0.0)
+    ts(C(41), C(1), -1.0, 2.5, OP.mult, OP.add)
+    act(A("KP", 0, 5), A("T3", 0, 5), AF.Abs, C(41))
+    ts(A("KP", 0, 5), A("KP", 0, 5), 2.5, None, OP.not_equal)
+    act(C(42), C(0), scale=0.5)
+    act(A("KP", 8, 13), A("T3", 0, 5), bias=C(42), scale=64.0)
     ts(A("CC", 17, 20), A("TI", 0, 3), C(1), None, OP.is_equal)
     ts(A("CC", 29, 32), A("CC", 17, 20), 2047.0, C(14), OP.mult, OP.add)
     ts(A("B8"), A("TI", 0, 8), C(2), None, OP.is_equal)
@@ -227,16 +247,17 @@ def build():
     act(A("BX", 8, 16), A("B8"), scale=C(12))
     act(A("BX", 16, 24), A("B8"), scale=C(8))
     act(A("WS", 0, 8), A("BX", 0, 8), scale=2.0 ** 26)
-    act(A("WS", 9, 24, 2), A("BX", 8, 16), scale=16.0)
-    act(A("WS", 8, 24, 2), A("BX", 8, 16), scale=-16.0)
-    act(A("WS", 24, 32), A("BX", 16, 24), scale=8.0)
+    act(A("WS", 8, 16), A("BX", 8, 16), scale=2.0)
     for l in range(3):
         act(blk("WM", l, 8), A("BX", 0, 8), scale=1024.0)
     ts(A("CM", 0, 8), A("TI", 0, 8), C(4), None, OP.is_equal)
-    act(A("CM", 8, 16), A("CM", 0, 8), scale=0.125)
-    act(A("CF"), A("CM", 0, 8), scale=0.125)
+    act(A("CF"), A("CM", 0, 8), scale=8192.0)
     ts(A("MX"), A("T1", 0, 128), C(3), None, OP.is_equal)
-    asel(A("EN"), A("ONB", 0, 136), [[-16, 8], [-1, 17]], OP.is_equal, 1, 1)
+    ts(A("DG"), A("T1", 0, 384), C(1), None, OP.is_equal)
+    act(A("RS0"), A("T1"), AF.Sign)
+    act(A("RH"), A("RS0", 0, 384), bias=C(40), scale=-2.0 ** 27)
+    ts(A("REP"), A("REP"), C(24), None, OP.is_equal)
+    asel(A("EN"), A("ONB"), [[-16, 8], [-1, 17]], OP.is_equal, 1, 1)
     ms(A("EN", 0, 136, 17), 0.0)
     act(A("EC"), A("EN"), scale=32768.0)
     asel(A("EN", 0, 136, 17), A("ONB", 0, 8), [[-16, 8]], OP.is_equal, 0, 1)
@@ -245,37 +266,29 @@ def build():
     ms(A("CR", 0, 136, 17), 244.0 * 32768)
     ms(A("R17H"), 0.0)
     ms(A("R17H", 0, 136, 17), 2.0 ** 27)
-    ms(A("R17M"), 1.0)
-    ms(A("R17M", 0, 136, 17), 0.0)
-    ms(A("SCC", 136, 144), 0.0)
-    ms(A("S", 1792, 1920), 0.0)
     ms(A("ZB"), 0.0)
-    ms(A("R3"), 1.0)
-    ms(A("R3", 0, 48, 3), 0.0)
+    ms(A("SQ", 0, 16), 0.0)
+    ms(A("SU", 384, 512), 0.0)
+    ms(A("D0"), -2 * BIG)
+    ms(A("D0", 0, 64, 4), 2 * BIG)
     asel(A("BLK"), A("ONB", 0, 128), [[-16, 8], [0, 16]], OP.is_ge, 0, 1)
     asel(A("BLK"), A("BLK"), [[16, 8], [0, 16]], OP.is_ge, 15, -1)
-    ts(A("WU"), A("BLK"), C(12), 2.0, OP.mult, OP.mult)
-    act(A("I15"), A("IB"), scale=C(8))
-    act(A("NIB"), A("IB"), scale=-1.0)
-    act(A("I2K"), A("IB"), scale=2048.0)
-    act(A("N2K"), A("IB"), scale=-2048.0)
+    for n, v in (("I15", C(8)), ("NIB", -1.0), ("I8K", 8192.0), ("I4K", 4096.0), ("I1K", 1024.0), ("N1K", -1024.0), ("IA", 1026.0),
+                 ("IM", -1025.0)):
+        act(A(n), A("IB"), scale=v)
     for l in range(3):
         act(blk("OHW", l), A("ONB", 0, 128), scale=C(17 + l))
         act(blk("WX", l), A("BLK"), scale=C(29 + l))
-        ts(blk("IDU", l), A("T3", 0, 128), C(21), 1.0 / 2048, OP.add, OP.mult)
-    iota(A("KR", p1=1), [[0, 24], [-1, 16]], 15, 0)
-    for h in range(2):
-        asel(blk("REP", h, 1024), A("ONB"), [[-1, 64], [0, 16]], OP.is_equal, -64 * h, 1)
+        act(blk("IDU", l), A("T3", 0, 128), bias=C(21))
     ts(A("PM"), A("T3", 0, 128), C(5), -1.0, OP.is_equal, OP.mult)
-    ms(A("RH"), 0.0)
-    ms(A("RH", 0, 384, 16), 2.0 ** 27)
-    for h in range(2):
-        asel(A("TRI", p0=64 * h, p1=64 * h + 64), A("ONB", 0, 512, p0=64 * h, p1=64 * h + 64), [[0, 8], [1, 64]], OP.is_ge, 0, -1)
-    for q in range(8):
-        act(blk("BG", q, 64), A("ONB", 0, 64), scale=A("B8", q, q + 1))
-    act(A("NBG"), A("BG"), scale=-1.0)
-    for t in range(RO):
-        act(blk("CT", t), A("ONB", 0, 128), scale=128.0 * t - 2048.0)
+    act(C(43), C(2), bias=C(38), scale=16.0)
+    act(C(44), C(8), scale=8192.0)
+    ts(C(45), C(0), 64.0, -1.0, OP.is_lt, OP.mult)
+    ts(C(46), C(0), 64.0, -1.0, OP.is_ge, OP.mult)
+    ts(A("BD", 0, 144), A("T3"), C(43), C(44), OP.is_equal, OP.mult)
+    act(A("BD", 144, 288), A("BD", 0, 144), scale=16.0)
+    ts(A("BD", 288, 432), A("BD", 0, 144), A("RM", 0, 1), None, OP.mult)
+    ts(A("WU"), A("BLK"), C(12), 2.0, OP.mult, OP.mult)
     ms(A("WD", 8, 16), 0.0)
     ms(A("WT"), 0.0)
     act(A("WD", 0, 8), A("BX", 16, 24))
@@ -285,42 +298,34 @@ def build():
     act(A("B8B"), A("B8"))
 
     def control(t, n, o):
-        tt(A("PF"), A(n, o + 80, o + 112), A("IDL"), OP.add)
-        pc = lambda l: blk("PF", l, 8)
-        tt(A("MM", 0, 8), pc(0), pc(1), OP.min)
-        tt(A("MM", 0, 8), A("MM", 0, 8), pc(2), OP.min)
-        gtt(A(n, o + 48, o + 80), A("MM", 0, 8), A("LS", 52, 54), A("PF"), OP.is_equal)
-        for l in range(3):
-            act(A(n, o + l, o + 24, 3), blk(n, l, 8, o + 48))
-            act(A(n, o + 24 + (l + 1) % 3, o + 48, 3), blk(n, l, 8, o + 48))
-        if t < RO - 1:
-            tt(A("PX", 0, 24), A(n, o + 48, o + 72), A("PF", 0, 24), OP.add)
-            tt(A("MM", 8, 16), A("PX", 0, 8), A("PX", 8, 16), OP.min)
-            tt(A("MM", 8, 16), A("MM", 8, 16), A("PX", 16, 24), OP.min)
-            ts(A("MI", 0, 16), A("MM"), 2048.0, None, OP.mult)
-            ts(A("MI", 16, 32), A("MI", 0, 16), 2047, None, OP.bitwise_and)
-            tt(A(n, o + 112, o + 120), A("MI", 16, 24), A("MI", 24, 32), OP.subtract)
-            cp(A(n, o + 120, o + 128), A("MI", 24, 32))
+        scan(A("MM", 0, 32), A("R4"), A("PF"), OP.add, OP.min)
+        if t == 0:
+            ts(A("AL", 0, 8), A("MM", 3, 32, 4), 511, None, OP.bitwise_and)
+            cp(A("LU", 128, 136), A("AL", 0, 8))
+        gtt(A("EQ4"), A("MM", 0, 32), A("LS", 106, 108), A("PF"), OP.is_equal)
+        act(A("E5"), A("EQ4"), scale=512.0)
+        act(A(n, o + 32, o + 64), A("EQ4"), scale=-1536.0)
+        for h in range(2):
+            act(A(n, o + 64 + 32 * h, o + 96 + 32 * h), A("EQ4"), bias=C(35), scale=4096.0 - BIG)
+        tt(A(n, o, o + 32), A("PF"), A("E5"), OP.add)
+        scan(A("MM", 32, 64), A("R4"), A(n, o, o + 32), OP.add, OP.min)
+        ts(A("MI"), A("MM", 3, 64, 4), 511, None, OP.bitwise_and)
+        act(A(n, o + 128, o + 136), A("MI", 0, 8), scale=-1.0)
+        act(A(n, o + 67, o + 96, 4), A("MI", 8, 16))
 
     cp(A("TUB", p1=24), A("TU", p1=24))
-    mm(A("M6", 0, 24), A("TUB", p1=24), A("I24", p1=24), True, True)
-    tt(A("PF", 0, 24), A("IDL", 0, 24), A("M6", 0, 24), OP.add)
-    cp(A("MC", 80, 104), A("M6", 0, 24))
-    tt(A("FF"), A("PF", 0, 8), A("PF", 8, 16), OP.min)
-    tt(A("DL"), A("FF"), A("PF", 16, 24), OP.min)
-    ts(A("AB", 0, 8), A("DL"), 2048.0, None, OP.mult)
-    ts(A("AL", 0, 8), A("AB", 0, 8), 2047, None, OP.bitwise_and)
-    cp(A("LU", 128, 136), A("AL", 0, 8))
-    gat("dve", A("LU", 0, 128), A("QN"), A("LU", 128, 136))
-    gat("dve", A("M3", 0, 128), A("QK"), A("LU", 128, 136))
-    gat("dve", A("STG", 128, 256), A("QN"), A("LU", 128, 136))
-    for h, src, bank in ((0, "QK", "J2"), (1, "QN", "W0")):
-        cp(blk("KH", h, 384), A(src))
-        for l in range(3):
-            mm(blk(bank, l), blk("KH", 3 * h + l), A("IB"), True, True)
-        cp(blk("MK", h, 384), A(bank, 0, 384))
+    mm(A("M6", 0, 32), A("TUB", p1=24), A("P24", p1=24), True, True)
+    tt(A("PF"), A("ID4"), A("M6", 0, 32), OP.add)
     control(0, "MC", 0)
-    gat("act", A("GP"), A("GL"), A("LS", 58, 66))
+    gat("dve", A("LU", 0, 128), A("QN"), A("LU", 128, 136))
+    gat("act", A("M3", 0, 128), A("QK"), A("LU", 128, 136))
+    gat("act", A("STG", 128, 256), A("QN"), A("LU", 128, 136))
+    cp(A("KH"), A("QK"), "act")
+    for l in range(3):
+        mm(blk("J2", l), blk("KH", l), A("IB"), True, True)
+    cp(blk("MK", 0, 384), A("J2", 0, 384), "act")
+    cp(blk("MK", 1, 384), A("QN"), "act")
+    gat("act", A("GP"), A("GL"), A("LS", 88, 96))
     mm(A("J1", 0, 128), A("GP"), A("NIB"), True, True)
     act(A("NG", 0, 128), A("J1", 0, 128))
 
@@ -329,225 +334,254 @@ def build():
     for t in range(RO):
         last = t == RO - 1
         now[0] = t
-        u0, u1, m3 = 0, 264 * t, 128 * t
-        ng = blk("NG", t % 4)
-        jl = A("LU", u0 + 128, u0 + 136)
-        names, newnames, newkeys = blk("MK", 2 * t + 1, 384), blk("OK", 2 * t + 1, 384), blk("OK", 2 * t, 384)
+        u1, m3 = 256 * t, 136 * t
+        ng = lambda h: half("NG", h, 128 * (t % 4), 128 * (t % 4) + 128)
+        jl = A("LU", 128, 136)
+        keys, names = blk("MK", 2 * t, 384), blk("MK", 2 * t + 1, 384)
+        newkeys, newnames = blk("OK", 2 * t, 384), blk("OK", 2 * t + 1, 384)
         if t < 3:
-            send(0, t + 1, [(blk("NG", t + 1), ng)])
-        sa = PAR["sa"]
-        gat("dve", A("SG", 0, 16 * sa), SW, A("LU", u0, u0 + sa))
-        gat("act", A("SG", 16 * sa, 2048), SW, A("LU", u0 + sa, u0 + 128))
-        mm(A("M6", 0, 136), A("ONB", 0, 128, p1=2), A("CR", p1=2), True, False)
-        mm(A("M6", 0, 136), A("STG", u1 + 128, u1 + 256), A("EN"), False, False)
-        mm(G(0, 17), A("IB"), A("ZB", 0, 136), True, False)
-        for k in range(16):
-            mm(A("M6", 1 + k, 136, 17), A("SG", k, 2048, 16), A("WS", 0, 8), False, False)
-        mm(A("M6", 0, 136), A("M3", m3, m3 + 128), A("EC"), False, True)
-        mm(G(1, 2), A("SG", 0, 2048, 16), A("WS", 9, 24, 2), False, False)
-        for k in range(1, 16):
-            mm(G(k, k + 2), A("SG", k, 2048, 16), A("WS", 8, 24), False, False)
-        for a, b in ((0, 16 * sa), (16 * sa, 8 * sa + 1024), (8 * sa + 1024, 2048)):
+            send(0, t + 1, blk("NG", t + 1), blk("NG", t))
+        for e, a, b in PAR["sg"]:
+            gat(e, A("SG", 16 * a, 16 * b), SW, A("LU", a, b))
+        tag[0] = "cd"
+        mm(G(0, 136), A("IB"), A("ZB", 0, 272), True, False)
+        mm(A("Z0", 0, 136), A("ONB", 0, 128, p1=2), A("CR", p1=2), False, False)
+        mm(A("Z0", 0, 136), A("STG", u1 + 128, u1 + 256), A("EN"), False, False)
+        for a, b in PAR["sm"]:
+            mm(A("Z0", 256, 392, 17, a, b), A("SG", 16 * a, 16 * b, 16), A("WS", 8, 16), False, False)
+            for k in range(16):
+                mm(G(k + 1, 136, 17, a, b), A("SG", 16 * a + k, 16 * b, 16), A("WS"), False, False)
+        mm(A("Z0", 0, 136), A("M3", m3, m3 + 128), A("EC"), False, True)
+        tag[0] = ""
+        vs = PAR["vs"]
+        for a, b in zip(vs[:-1], vs[1:]):
             scan(A("VS", a, b), A("RS0", 0, b - a), A("SG", a, b), OP.mult, OP.max)
-        mm(G(16, 17), A("VS", 15, 2048, 16), A("WS", 24, 32), False, True)
+        tag[0] = "v"
+        mm(A("W0", 0, 8), A("IB"), A("ZB", 0, 8), True, False)
+        for r in range(16):
+            a = 16 * (16 * (r % 8) + r // 8) + 15
+            mm(A("W0", 0, 8), A("BD", 15 - r, 143 - r), A("VS", a, a + 225, 32), False, False)
+        tag[0] = ""
+        if t > 0:
+            cp(jl, A("M3", m3 + 128, m3 + 136), "act")
         gat("act", A("OH"), A("OHW"), jl)
-        mm(A("J1", 0, 384), A("OH"), A("WX"), True, False)
+        tag[0] = "mk0"
+        mm(A("J1", 0, 384), A("IB"), A("ZB"), True, False)
+        tag[0] = "mk"
         for k in range(16):
-            mm(A("J1", k, 384, 16), A("SG", k, 2048, 16), A("WM"), False, k == 15)
-        scan(A("SCC", 0, 136), A("R17H"), A("M6", 0, 136), OP.add, OP.min)
-        scan(A("SC2"), A("R17H"), A("M6", 0, 136), OP.add, OP.min)
-        cp(A("NI"), A("SCC", 16, 136, 17))
-        gtt(A("ST"), A("SC2"), A("LS", 66, 75), A("SCC"), OP.is_equal)
-        ts(A("NA"), A("NI"), 2047, None, OP.bitwise_and)
-        tt(A("PR"), G(0, 17), A("ST", 0, 136), OP.mult)
+            mm(A("J1", k, 384, 16), A("SG", k, 2048, 16), A("WM"), False, False)
+        mm(A("J1", 0, 384), A("OH"), A("WX"), False, True)
+        tag[0] = ""
+        least = A("SCI", 32, 152, 17)
+        scan(A("SCI", 16, 152), A("R17H"), A("Z0", 0, 136), OP.add, OP.min)
+        scan(A("SC2", 16, 152), A("R17H"), A("Z0", 0, 136), OP.add, OP.min)
+        gtt(A("ST"), A("SC2"), A("LS", 96, 105), A("SCI", 15, 159), OP.is_lt)
+        ts(A("NA"), least, 2047, None, OP.bitwise_and)
+        tt(A("PR"), A("Z0", 256, 392), A("ST", 0, 136), OP.mult)
+        act(A("SN"), A("ST", 0, 136), bias=1.0, scale=-1.0)
         gtt(A("XN"), A("NA"), A("LS", 0, 8), A("MX"), OP.mult)
-        scan(A("SCS"), A("R17M"), A("PR"), OP.mult, OP.add)
+        scan(A("SCS"), A("SN"), A("PR"), OP.mult, OP.add)
         mm(A("M6", 0, 8), A("XN"), A("CM", 0, 8), True, True)
-        cp(A("LX", 0, 8), A("M6", 0, 8))
+        cp(A("LX", 0, 8), A("M6", 0, 8), ON["LX0"])
         gat("act", A("X"), SW, A("LX", 0, 8))
+        gtt(A("XF"), A("SCS"), A("LS", 48, 56), A("MX"), OP.mult)
+        mm(A("W0", 0, 8), A("XF"), A("CF"), False, True)
+        mm(A("Z1", 0, 128), A("WU"), A("X"), True, True)
         if t == 0:
-            cp(A("UI"), A("SCS", 16, 136, 17))
-            ts(A("UA"), A("UI"), 2047, None, OP.bitwise_and)
-            gtt(A("XO"), A("UA"), A("LS", 0, 8), A("MX"), OP.mult)
-            mm(A("W0", 0, 8), A("XO"), A("CM", 8, 16), True, True)
+            ts(A("UI"), A("W0", 0, 8), 1.0 / 8192, None, OP.mult)
+            ts(A("UA"), A("UI"), 255, None, OP.bitwise_and)
+            cp(A("LX", 8, 16), A("UA"))
         else:
-            gtt(A("XF"), A("SCS"), A("LS", 140, 148), A("MX"), OP.mult)
-            mm(A("W0", 0, 8), A("XF"), A("CF"), True, True)
-        mm(A("Z1", 0, 128), A("ONB", 0, 128, p1=1), A("C32", p1=1), True, False)
-        mm(A("Z1", 0, 128), A("WU"), A("X"), False, True)
+            ts(A("LX", 8, 16), A("W0", 0, 8), 1.0 / 8192, None, OP.mult)
+        act(A("U"), A("Z1", 0, 128), bias=C(36))
         mm(A("Z0", 0, 128), A("X"), A("I15"), True, True)
-        cp(A("LX", 8, 16), A("W0", 0, 8))
         act(A("XT"), A("Z0", 0, 128))
-        gat("dve", A("UP"), A("OT", 0, 256 if t == 0 else 15136), A("LX", 8, 16))
-        tt(A("N1"), A("Z1", 0, 128), A("UP"), OP.mult)
+        gtt(A("N1"), A("OT", 0, 256 if t == 0 else 15136), A("LX", 8, 16), A("U"), OP.mult)
         ts(A("N2"), A("N1"), 5, 2047, OP.arith_shift_right, OP.bitwise_and)
         ts(A("NL"), A("N2"), A("AC", 0, 1), None, OP.add)
-        mm(A("W1", 0, 128), A("XN"), A("IB"), True, True)
-        cp(A("NX"), A("W1", 0, 128))
-        if fu:
-            op("act", "gatm", (A("XB", 0, fu), A("X"), A("LS", 76, 76 + fu // 16), 0.0, C(8)), [A("X"), A("LS", 76, 140), C(8)],
-               [A("XB", 0, fu)], 60 + fu * GF * CY)
-        mm(A("J2", 0, 128), ng, A("IB"), True, False)
+        for a in range(0, 2048 - fu, 256):
+            b = min(2048 - fu, a + 256)
+            gat("act", A("XB", a, b), A("X", fu // 16, 128), A("LS", 114 + a // 16, 114 + b // 16), 0.0, C(8))
+        mm(A("J2", 0, 128), blk("NG", t % 4), A("IB"), True, False)
         mm(A("J2", 0, 128), A("I15"), A("X"), False, True)
         act(A("DX"), A("J2", 0, 128), AF.Abs)
         ts(A("TX"), A("DX"), 5.0, None, OP.is_gt)
         mm(A("J2", 128, 152), A("DX"), A("WD"), True, False)
         mm(A("J2", 128, 152), A("TX"), A("WT"), False, True)
-        ts(A("NH"), A("J2", 128, 152), -1.0, None, OP.mult)
-        tt(A("KM"), A("J1", 0, 384), blk("MK", 2 * t, 384), OP.max)
-        mm(A("M6", 0, 384), A("ONB", 0, 128, p1=1), A("KR", p1=1), True, False)
-        mm(A("M6", 0, 384), A("I2K"), A("KM"), False, True)
-        act(A("CQ"), A("M6", 0, 384))
-        scan(A("SQ"), A("RS0", 0, 384), A("CQ"), OP.mult, OP.max)
-        gtt(A("EQ"), A("SQ"), A("LS", 24, 48), A("CQ"), OP.is_equal)
+        for h in range(2):
+            act(blk("NH", h, 24), A("J2", 128, 152), scale=C(45 + h))
+        act(A("NH2"), A("J2", 128, 152), bias=C(37), scale=-1.0)
+        for l in range(3):
+            tt(blk("KM", l), blk("J1", l), blk("MK", 6 * t + l), OP.max)
+        scan(A("SQ", 16, 400), A("RS0", 0, 384), A("KM"), OP.mult, OP.max)
+        tag[0] = "eq"
+        mm(A("M7", 0, 384), A("IA"), A("SQ", 16, 400), True, False)
+        mm(A("M7", 0, 384, 16), A("IB"), A("SQ", 15, 399, 16), False, False)
+        mm(A("M7", 0, 384, 16), A("IB"), A("ONB", 0, 24), False, False)
+        for k in range(16):
+            mm(A("M7", k, 384, 16), A("IM"), A("SQ", 31, 400, 16), False, False)
+        mm(A("M7", 0, 384), A("NIB"), A("SQ", 15, 399), False, True)
+        tag[0] = ""
+        act(A("EQ"), A("M7", 0, 384), AF.Sign, C(33))
+        for l in range(3):
+            act(blk("DH", l), A("IB"), scale=A("KP", 8 + t, 9 + t))
+        tag[0] = "nk"
+        mm(A("M7", 0, 384), A("ONB", 0, 128), A("DH"), True, False)
+        for l in range(3):
+            mm(blk("M7", l), blk("EQ", l), blk("DH", 0), False, False)
+        tag[0] = "idu"
+        mm(A("M6", 0, 384), A("IB"), A("IDU"), True, False)
+        tag[0] = ""
         for e, a, b in PAR["eg"]:
-            if 16 * b <= fu:
-                gtt(A("E", 16 * a, 16 * b), A("EF"), A("NL", a, b), A("XB", 16 * a, 16 * b), OP.add)
+            if 16 * a >= fu:
+                gtt(A("E", 16 * a, 16 * b), A("EF"), A("NL", a, b), A("XB", 16 * a - fu, 16 * b - fu), OP.add)
             else:
                 gat(e, A("E", 16 * a, 16 * b), A("EF"), A("NL", a, b))
-        mm(A("J1", 0, 288), A("IB"), A("ZB"), True, False)
-        mm(A("J2", 0, 96), A("IB"), A("ZB", 0, 96), True, False)
-        jo = lambda b: A("J1", b, 288, 12) if b < 12 else A("J2", b - 12, 96, 4)
+        tag[0] = "hx"
+        mm(A("J1", 0, 384), A("IB"), A("ZB"), True, False)
+        jo = lambda b: A("J1", b, 384, 16)
         for b in range(16):
-            mm(jo(b), blk("REP", b), A("NH"), False, False)
-        mm(A("M6", 0, 384), A("I2K"), A("IDU"), True, False)
-        ch = PAR["ch"]
-        for c in range(len(ch) - 1):
-            a, b = ch[c], ch[c + 1]
-            z, w = A("Z%d" % (c % 2), 0, b - a), A("W%d" % (c % 2), 0, b - a)
-            if b <= fu:
-                z = A("E", a, b)
-            else:
-                mm(z, A("XT"), A("REP", a, b), True, False)
+            mm(jo(b), blk("REP", b % 8), blk("NH", b // 8, 24), False, False)
+        tag[0] = ""
+        ch, turned = PAR["ch"], PAR["turned"]
+
+        def spread(bank, a, b, src):
+            mm(A(bank, 0, b - a), src(a // 1024), half("REP", a // 1024, a % 1024, (b - 1) % 1024 + 1), True, False)
+        for c, (a, b, zb, wb) in enumerate(ch):
+            z, w = A(zb or "E", 0 if zb else a, b - a if zb else b), A(wb, 0, b - a)
+            if zb:
+                tag[0] = "zx%d" % c
+                spread(zb, a, b, lambda h: half("XT", h))
+                tag[0] = "ze%d" % c
                 mm(z, A("IB"), A("E", a, b), False, True)
+            tag[0] = "y%d" % c
             ts(A("Y", a, b), z, 0.0, 63.0, OP.max, OP.min)
-            mm(w, ng, A("REP", a, b), True, False)
+            tag[0] = "wg%d" % c
+            spread(wb, a, b, ng)
+            tag[0] = "wy%d" % c
             mm(w, A("IB"), A("Y", a, b), False, True)
+            tag[0] = "d%d" % c
             act(A("D", a, b), w, AF.Abs)
+            tag[0] = "t%d" % c
             ts(A("TT", a, b), A("D", a, b), 5.0, None, OP.is_gt)
-            for q in range(a // 128, b // 128):
-                mm(jo(q), blk("D", q), A("WD"), False, False)
-            for q in range(a // 128, b // 128):
-                mm(jo(q), blk("TT", q), A("WT"), False, q in (11, 15))
-            if b == 1536:
-                op("dve", "cpj", (0, 12, A("J1", 0, 288)), [A("J1", 0, 288)], [A("JS", 0, 288)], 288 * CY)
-        op("dve", "cpj", (12, 16, A("J2", 0, 96)), [A("J2", 0, 96)], [A("JS", 288, 384)], 96 * CY)
-        for l in range(3):
-            op("pe", "mmj", (blk("M6", l), l, A("I2K"), l == 2), [A("JS"), A("I2K")], [A("M6", 0, 384)], 128 * PCY)
+            qs = range(a // 128, b // 128)
+            if c < turned:
+                tag[0] = "sd%d" % c
+                for q in qs:
+                    mm(jo(q), blk("D", q), A("WD"), False, False)
+                tag[0] = "st%d" % c
+                for q in qs:
+                    mm(jo(q), blk("TT", q), A("WT"), False, c == turned - 1 and q == qs[-1])
+            else:
+                for l, src in ((0, "D"), (2, "D"), (1, "TT")):
+                    tag[0] = ("st%d" if l == 1 else "sd%d") % c
+                    for q in qs:
+                        mm(blk("M6", l), A("BD", 144 * l + 15 - q, 144 * l + 143 - q), blk(src, q), False,
+                           l == 1 and c == len(ch) - 1 and q == qs[-1])
+            if c == turned - 1:
+                tag[0] = "js"
+                cp(A("JS"), A("J1", 0, 384), ON["JS"])
+                tag[0] = "mmj"
+                for l in range(3):
+                    mm(blk("M6", l), blk("JS", l), A("I8K"), False, False)
+        tag[0] = "rn"
         mm(A("Z1", 0, 384), A("IB"), names, True, False)
-        mm(A("Z1", 0, 384), A("N2K"), A("EQ"), False, True)
-        act(A("RN"), A("Z1", 0, 384), AF.Relu)
-        mm(A("Z0", 0, 384), A("T3", 0, 128, p1=1), A("ONB", 0, 384, p1=1), True, False)
-        mm(A("Z0", 0, 384), A("CT", 128 * t, 128 * t + 128, p1=1), A("ONB", 0, 384, p1=1), False, False)
-        mm(A("Z0", 0, 384), A("I2K"), A("EQ"), False, True)
-        tt(newnames, A("Z0", 0, 384), A("RN"), OP.max)
+        for l in range(3):
+            mm(blk("Z1", l), blk("EQ", l), A("N1K"), False, l == 2)
+        tag[0] = ""
+        act(A("RN"), A("Z1", 0, 384), AF.Relu, C(34))
+        tag[0] = "nr"
+        mm(A("M7", 0, 384), A("IB"), A("RN"), False, True)
+        tag[0] = ""
         if not last:
-            for l in range(3):
-                mm(blk("Z1", l), blk("OK", 6 * t + 3 + l), A("IB"), True, True)
-            act(A("NK"), A("Z1", 0, 384))
-        w = "M7"
-        mm(G(0, 64), A("I2K"), A("TRI"), True, False)
+            act(A("NK"), A("M7", 0, 384))
+        cp(newnames, A("M7", 0, 384), ON["N16"])
+        ts(A("HI", 0, 8), least, 7, 15, OP.arith_shift_right, OP.bitwise_and)
+        ts(A("HI", 8, 16), least, 127, None, OP.bitwise_and)
+        act(A("LO"), A("HI", 8, 16))
+        for h in range(4):
+            gtt(blk("OHH", h, 64), A("HI", 0, 8), A("LS", 32 + 4 * h, 36 + 4 * h), blk("CH", h, 64), OP.is_equal)
         for q in range(8):
-            for h in range(2):
-                mm(A(w, 64 * q, 64 * q + 64, 1, 64 * h, 64 * h + 64), blk("BG", q, 64), blk("NX", h, 64), False, False)
-        mm(G(0, 64), A("NX"), A("NBG"), False, True)
-        if PAR["dd"] == "act":
-            act(A("TB"), G(0, 64), AF.Abs)
-            for q in range(8):
-                act(blk("TB", q, 64), blk("TB", q, 64), AF.Relu, 1.0, -1.0, A("MN", q, q + 1))
-            act(A("MN", 8, 16), A("MN", 0, 8), AF.Sign)
-        else:
-            for q in range(8):
-                op("dve", "red", (A("MN", q, q + 1), blk(w, q, 64), OP.min, True), [blk(w, q, 64)], [A("MN", q, q + 1)], 64 * CY)
-            ts(A("MN", 8, 16), A("MN", 0, 8), 0.0, None, OP.is_equal)
-        scan(A("SU"), A("RH"), A("M6", 0, 384), OP.add, OP.min)
-        gtt(A("PB"), A("SU"), A("LS", 48, 51), A("MC", m3, m3 + 48), OP.mult)
-        scan(A("P1"), A("R3"), A("PB"), OP.mult, OP.add)
-        ts(A("GO", 0, 8), A("P1", 2, 24, 3), 0.0, None, OP.is_lt)
-        cp(A("AB"), A("P1", 2, 48, 3))
-        if not last:
-            tt(A("GO", 8, 16), A("GO", 0, 8), A("MC", m3 + 112, m3 + 120), OP.mult)
-        ts(A("AL", 0, 16), A("AB"), 2047, None, OP.bitwise_and)
+            ts(blk("OHL", q), A("T3", 0, 128), A("LO", q, q + 1), None, OP.is_equal)
+        tag[0] = "mrk"
+        mm(A("Z0", 0, 128), A("IB"), A("ZB", 0, 128), True, False)
+        for q in range(8):
+            mm(A("Z0", 0, 128, 1, 32 * (q // 2), 32 * (q // 2) + 32), blk("OHH", q, 32), blk("OHL", q), False, False)
+        mm(A("Z0", 0, 128), A("IB"), A("MKS"), False, True)
+        tag[0] = ""
+        ts(A("MKS"), A("Z0", 0, 128), 1.0, A("KP", t, t + 1), OP.min, OP.mult)
+        dma("sp", "marks", A("MKS"), [A("MKS")], [A("S", 0, 2048, 1, 15, 16)])
+        act(A("D0", 3, 32, 4), A("MC", m3 + 128, m3 + 136))
+        scan(A("SU", 0, 384), A("RH"), A("M6", 0, 384), OP.add, OP.min)
+        gtt(A("PB"), A("SU"), A("LS", 110, 114), A("MC", m3 + 64, m3 + 128), OP.add)
+        scan(A("P1"), A("D0"), A("PB"), OP.max, OP.min)
+        ts(A("AL"), A("P1", 2, 64, 4), 2047, None, OP.bitwise_and)
+        tag[0] = "lab"
+        cp(A("LA", 0, 16), A("AL"), ON["lab"])
+        tag[0] = ""
         if not last:
             njl = A("LA", 16, 24)
-            tt(A("OB", u1 + 256, u1 + 264), A("GO", 8, 16), A("MC", m3 + 120, m3 + 128), OP.add)
-            cp(A("LA", 0, 16), A("AL", 0, 16))
-            cp(njl, A("OB", u1 + 256, u1 + 264))
-            gat("dve", A("OB", u1, u1 + 128), A("Y"), A("LA", 8, 16))
-            gat("dve", A("OB", u1 + 128, u1 + 256), A("NK"), njl)
-            send(2, t, [(blk("STG", t + 1, 264), blk("OB", t, 264))])
+            act(njl, A("P1", 3, 32, 4), AF.Abs)
+            gat(ON["yb"], A("OB", u1, u1 + 128), A("Y"), A("LA", 8, 16))
+            gat(ON["nm"], A("OB", u1 + 128, u1 + 256), A("NK"), njl)
+            send(2, t, blk("STG", t + 1, 256), blk("OB", t, 256))
         else:
-            cp(A("LA", 0, 16), A("AL", 0, 16))
             gat("act", A("OL"), A("Y"), A("LA", 8, 16))
-            send(2, t, [(A("SL"), A("OL"))])
+            send(2, t, A("SL"), A("OL"))
+        ts(A("GO"), A("P1", 2, 32, 4), 0.0, None, OP.is_lt)
         mm(A("W1", 0, 384), A("IB"), A("KM"), True, False)
-        mm(A("W1", 0, 384), A("N2K"), A("EQ"), False, True)
-        act(A("A2"), A("W1", 0, 384), AF.Relu)
-        mm(A("W0", 0, 384), A("I2K"), A("EQ"), True, False)
-        mm(A("W0", 0, 384), A("ONB", 0, 128, p1=1), A("K2", p1=1), False, False)
+        mm(A("W1", 0, 384), A("N1K"), A("EQ"), False, True)
+        act(A("A2"), A("W1", 0, 384), AF.Relu, C(34))
+        mm(A("W0", 0, 384), A("I1K"), A("EQ"), True, False)
         for k in range(16):
-            mm(A("W0", k, 384, 16), A("PM"), A("NH"), False, k == 15)
+            mm(A("W0", k, 384, 16), A("PM"), A("NH2"), False, k == 15)
         tt(newkeys, A("W0", 0, 384), A("A2"), OP.max)
-        ts(A("FF"), A("GO", 0, 8), -3.0, 1.0, OP.mult, OP.add)
-        gtt(A("PX", 24, 56), A("FF"), A("LS", 52, 54), A("MC", m3 + 48, m3 + 80), OP.mult)
+        gtt(A("PX"), A("GO"), A("LS", 108, 110), A("MC", m3 + 32, m3 + 64), OP.mult)
+        tt(A("PF"), A("PX"), A("MC", m3, m3 + 32), OP.add)
         if not last:
             for l in range(3):
                 mm(blk("W1", l), blk("OK", 6 * t + l), A("IB"), True, True)
             act(A("CK"), A("W1", 0, 384))
-            gat("dve", A("O3", m3, m3 + 128), A("CK"), njl)
-            tt(A("OC", m3 + 80, m3 + 112), A("PX", 24, 56), A("MC", m3 + 80, m3 + 112), OP.add)
+            gat(ON["O3"], A("O3", m3, m3 + 128), A("CK"), njl)
+            act(A("O3", m3 + 128, m3 + 136), A("P1", 3, 32, 4), AF.Abs)
             control(t + 1, "OC", m3)
-            send(3, t, [(blk("M3", t + 1), blk("O3", t))])
-            wc = 128 if t < RO - 2 else 112
-            send(4, t, [(A("MC", m3 + 128, m3 + 128 + wc), A("OC", m3, m3 + wc))], 300)
-            send(1, t, [(blk("MK", t + 1, 768), blk("OK", t, 768))], 1500)
-            act(A("AG"), A("GO", 0, 8))
-            mm(A("J1", 0, 8), A("BLK"), A("AG"), True, True)
+            send(3, t, blk("M3", t + 1, 136), blk("O3", t, 136))
+            send(1, t, blk("MK", t + 1, 768), blk("OK", t, 768))
+            send(4, t, blk("MC", t + 1, 136), blk("OC", t, 136))
+            mm(A("J1", 0, 8), A("BLK"), A("GO"), True, True)
             act(A("AC", 8, 16), A("J1", 0, 8), acc=A("AC", 4, 5))
             act(A("AC", 5, 6), A("AC", 4, 5), AF.Sign, C(13))
-            act(A("AC", 6, 7), A("AC", 4, 5), AF.Sign, C(22))
+            act(A("AC", 6, 7), A("AC", 4, 5), AF.Sign, C(20))
             act(A("AC", 7, 8), A("AC", 4, 5), bias=C(32))
             act(A("AC", 3, 4), A("AC", 5, 6), bias=A("AC", 7, 8), scale=-32.0)
             act(A("AC", 0, 1), A("AC", 6, 7), bias=A("AC", 3, 4), scale=-32.0)
+            gat("act", blk("S", t), A("Y"), A("LA", 0, 8))
+            cp(A("LU", 0, 128), A("STG", u1 + 384, u1 + 512))
+            cp(blk("S", RO + t), A("STG", u1 + 256, u1 + 384), ON["Sb"])
         else:
+            mm(A("W1", 0, 384), A("IB"), newnames, True, False)
             for l in range(3):
-                mm(blk("W1", l), blk("OK", 6 * t + 3 + l), A("IB"), True, False)
-                mm(blk("W1", l), blk("OK", 6 * t + l), A("I2K"), False, False)
-                mm(blk("W1", l), blk("OK", 6 * t + l), A("I2K"), False, True)
+                mm(blk("W1", l), blk("OK", 6 * t + l), A("I4K"), False, l == 2)
             act(A("YQ"), A("W1", 0, 384))
             dma("sp", "yq", A("YQ"), [A("YQ")], [])
-            tt(A("T4", 24, 48), A("PX", 24, 48), A("MC", m3 + 80, m3 + 104), OP.add)
-            gtt(A("PE2"), A("T4", 24, 48), A("LS", 0, 24), A("DG"), OP.mult)
+            cp(A("PI"), A("PF"))
+            ts(A("PJ"), A("PI"), 9, None, OP.arith_shift_right)
+            gtt(A("PE2"), A("PJ"), A("LS", 64, 88), A("DG"), OP.mult)
             mm(A("J1", 0, 384, p1=8), A("B8B"), A("PE2"), True, True)
             act(A("YP", p1=8), A("J1", 0, 384, p1=8))
             dma("act", "yp", A("YP", p1=8), [A("YP")], [])
-        ts(A("MN", 16, 24), A("NA"), -1.0, C(6), OP.mult, OP.add)
-        tt(A("MN", 24, 32), A("MN", 16, 24), A("MN", 8, 16), OP.mult)
-        tt(A("T2D"), A("MN", 24, 32), A("NA"), OP.add)
-        gtt(A("XD"), A("T2D"), A("LS", 0, 8), A("DG", 0, 128), OP.mult)
-        mm(A("J2", 0, 8), A("XD"), A("B8B"), True, True)
-        cp(A("LX", 16, 24), A("J2", 0, 8))
-        op("act", "gatm", (A("XM"), A("S"), A("LX", 16, 24), C(9), C(8)), [A("S"), A("LX", 16, 24), C(9), C(8)], [A("XM")],
-           60 + 128 * GF * CY)
-        for h in range(2):
-            op("dve", "sca", (A("S"), blk("LX", h, 4, 16), blk("XM", h, 64)), [blk("LX", h, 4, 16), blk("XM", h, 64)], [A("S")],
-               55 + 64 * PAR["sf"] * CY)
-        if not last:
-            gat("act", blk("S", t), A("Y"), A("LA", 0, 8))
-            cp(A("LU"), A("STG", u1 + 392, u1 + 528))
-            cp(blk("S", RO + t), A("STG", u1 + 264, u1 + 392))
-        else:
             gat("act", A("GP"), A("Y"), A("LA", 0, 8))
             dma("act", ("ys", 512, 640), A("GP"), [A("GP")], [])
             dma("sp", ("ys", 0, 512), A("S", 0, 512), [A("S", 0, 512)], [])
             dma("act", ("ys", 640, 1152), A("S", 640, 1152), [A("S", 640, 1152)], [])
-            dma("sp", "ym", "marks", [A("S", 1280, 1792)], [])
+            dma("sp", "ym", "marks2", [A("S", 1280, 1792)], [])
             dma("sp", ("ys", 1152, 1280), A("SL"), [A("SL")], [])
     return ops
 
 
 def deps_of(ops):
     hist = {}
+    adds = lambda o: o["k"] == "mm" and not o["a"][3] and not o["a"][4]
     for n, o in enumerate(ops):
         dp = {}
         acc = [(r, False) for r in o["rd"]] + [(w, True) for w in o["wr"]]
@@ -557,6 +591,8 @@ def deps_of(ops):
                 if m == n:
                     continue
                 oe = ops[m]["e"]
+                if adds(o) and adds(ops[m]) and bank:
+                    continue
                 if bank and oe != o["e"]:
                     dp[m] = True
                 elif (w or isw) and q[1] < r[2] and r[1] < q[2]:
@@ -565,44 +601,60 @@ def deps_of(ops):
                     dp[m] = dp.get(m, False)
         for r, isw in acc:
             h = hist.setdefault(r[0], [])
-            if isw:
+            if isw and not adds(o):
                 h[:] = [x for x in h if not (r[1] <= x[1][1] and x[1][2] <= r[2] and r[3] == 1 and cnt(r) == r[2] - r[1] and r[4] == 0 and r[5] == 128)]
             h.append((n, r, isw))
         o["dp"] = dp
 
 
-def place(ops, keys, before, after, gap, lead):
+def place(ops, keys, before, after):
     n = len(ops)
     left = [len(before[i]) for i in range(n)]
-    ready = list(lead)
+    ready = [0.0] * n
     start = [0.0] * n
-    busy = dict((e, []) for e in ENG)
-    todo = sorted((keys[i], i) for i in range(n) if left[i] == 0)
+    busy = dict((e, ([], [])) for e in ENG)
+    todo = sorted(((keys[i], i) for i in range(n) if left[i] == 0), reverse=True)
     while todo:
-        i = todo.pop(0)[1]
-        c, st, bz = ops[i]["c"], ready[i], busy[ops[i]["e"]]
-        lo, hi = 0, len(bz)
-        while lo < hi:
-            mid = (lo + hi) // 2
-            if bz[mid][1] <= st:
-                lo = mid + 1
-            else:
-                hi = mid
-        while lo < len(bz) and bz[lo][0] < st + c - 1e-6:
-            st = max(st, bz[lo][1])
+        i = todo.pop()[1]
+        c, st = ops[i]["c"], ready[i]
+        b0, b1 = busy[ops[i]["e"]]
+        lo = len(b0)
+        while lo and b1[lo - 1] > st:
+            lo -= 1
+        while lo < len(b0) and b0[lo] < st + c - 1e-6:
+            st = max(st, b1[lo])
             lo += 1
-        bz.insert(lo, (st, st + c))
+        b0.insert(lo, st)
+        b1.insert(lo, st + c)
         start[i] = st
         new = False
-        for j in after[i]:
-            ready[j] = max(ready[j], st + c + gap(i, j))
+        for j, gp in after[i]:
+            if ready[j] < st + c + gp:
+                ready[j] = st + c + gp
             left[j] -= 1
             if left[j] == 0:
                 todo.append((keys[j], j))
                 new = True
         if new:
-            todo.sort()
+            todo.sort(reverse=True)
     return start
+
+
+def replay(order, calls):
+    free, last = [0.0] * len(ENG), [-1] * len(ENG)
+    seen, why = [0.0] * len(calls), [-1] * len(calls)
+    for i in order:
+        e, c, lat, before = calls[i]
+        st, w = free[e], last[e]
+        for m in before:
+            if seen[m] > st:
+                st, w = seen[m], m
+        free[e] = st = st + c
+        last[e] = i
+        seen[i] = st + lat
+        why[i] = w
+    end = max(seen)
+    return end, seen.index(end), why
 
 
 def label(o):
@@ -611,53 +663,135 @@ def label(o):
 
 
 def kinds(ops):
-    seen, names, out, prev = {}, {}, [], None
+    seen, names, out, prev, run = {}, {}, [], None, 0.0
     for o in ops:
-        if o["st"] < 0:
-            out.append(-1)
-            continue
         key = (o["st"], o["e"], label(o))
-        if not (o["e"] == "pe" and prev == key):
+        run = run + o["c"] if o["e"] == "pe" and prev == key and run < 200.0 else 0.0
+        if not run:
             seen[key] = seen.get(key, 0) + 1
         prev = key
-        out.append(names.setdefault((key[1], key[2], seen[key]), len(names)))
-    return out
+        out.append(names.setdefault((o["st"] < 0, key[1], key[2], seen[key]), len(names)))
+    return out, len(names)
 
 
 def schedule(ops):
     deps_of(ops)
     n = len(ops)
-    pred = [list(o["dp"]) for o in ops]
+    pred, anc = [], []
+    for i, o in enumerate(ops):
+        far, keep = 0, []
+        for m in sorted(o["dp"], reverse=True):
+            if not far >> m & 1:
+                keep.append((m, o["dp"][m]))
+                far |= anc[m] | (1 << m if o["dp"][m] else 0)
+        pred.append(keep)
+        anc.append(far)
+    lat = [o.get("lat", 0.0) for o in ops]
     succ = [[] for _ in range(n)]
     for i in range(n):
-        for m in pred[i]:
-            succ[m].append(i)
-    lat = [o.get("lat", 0.0) for o in ops]
-    gap = lambda m, i: lat[m] + (PAR["hop"] if ops[i]["dp"][m] else 0.0)
+        for m, need in pred[i]:
+            succ[m].append((i, lat[m] + (PAR["hop"] if need else 0.0)))
     tail = [0.0] * n
     for i in range(n - 1, -1, -1):
-        tail[i] = ops[i]["c"] + max([gap(i, j) + tail[j] for j in succ[i]] + [lat[i]])
-    early = [PAR["early"].get(o["e"] + ":" + label(o), 0.0) for o in ops]
-    keys = [-tail[i] - early[i] for i in range(n)]
-    best = None
+        tail[i] = ops[i]["c"] + max([gp + tail[j] for j, gp in succ[i]] + [lat[i]])
+    kind, nk = kinds(ops)
     rs = np.random.RandomState(PAR["seed"])
-    for it in range(PAR["iters"]):
-        st = place(ops, keys, pred, succ, gap, [0.0] * n)
-        total = max(st[i] + ops[i]["c"] + lat[i] for i in range(n))
-        if best is None or total < best[0]:
-            best = (total, st)
-        back = place(ops, [-(st[i] + ops[i]["c"] + lat[i]) for i in range(n)], succ, pred, lambda j, i: gap(i, j), lat)
-        noise = rs.uniform(0.0, PAR["noise"], n)
-        keys = [float(-(back[i] + ops[i]["c"]) + noise[i] - early[i]) for i in range(n)]
-    total, st = best
-    if PAR["off"]:
-        kind = kinds(ops)
-        keys = [st[i] if kind[i] < 0 else 4000.0 + 17000.0 * ops[i]["st"] + 10.0 * PAR["off"][kind[i]] + 1e-3 * i for i in range(n)]
-        st = place(ops, keys, pred, succ, gap, [0.0] * n)
-        total = max(st[i] + ops[i]["c"] + lat[i] for i in range(n))
+
+    same = {}
     for i in range(n):
-        ops[i]["t"] = st[i]
-    return sorted(range(n), key=lambda i: (st[i], i)), total
+        same.setdefault((kind[i], ops[i]["st"]), []).append(i)
+    up = [[m for m, _ in pred[i]] for i in range(n)]
+    down = [[j for j, _ in succ[i]] for i in range(n)]
+
+    cases = [[(ENG.index(o["e"]), o["c"] * (1.0 if "lat" in o else scale), o.get("lat", 0.0) + hop + (far if o["k"] == "send" else 0.0),
+               [m for m, need in pred[i] if need]) for i, o in enumerate(ops)] for scale, hop, far in PAR["cases"]]
+
+    def judge(order):
+        rp = [replay(order, c) for c in cases]
+        return sum(r[0] for r in rp) / len(rp), order, rp
+
+    def swap(order, xa, xb, ahead):
+        lo, hi = order.index(xa[0]), order.index(xb[-1])
+        if lo > hi:
+            return
+        seg = order[lo:hi + 1]
+        need, took = set(xb if ahead else xa), set()
+        for i in (reversed(seg) if ahead else seg):
+            if i in need:
+                took.add(i)
+                need.update(up[i] if ahead else down[i])
+        if any(i in took for i in (xa if ahead else xb)):
+            return
+        a, b = [i for i in seg if i in took], [i for i in seg if i not in took]
+        order[lo:hi + 1] = a + b if ahead else b + a
+    st = place(ops, [-x for x in tail], pred, succ)
+    groups, queue = {}, dict((e, []) for e in ENG)
+    for i in range(n):
+        groups.setdefault((ops[i]["st"], ops[i]["e"], ops[i]["tag"] or label(ops[i])), []).append(i)
+    for t in range(RO):
+        for e in ENG:
+            for word in ORDER[e].split():
+                name, k = (word.split("*") + ["1"])[:2]
+                g = groups.get((t, e, name), [])
+                queue[e] += g[:int(k)]
+                del g[:int(k)]
+    for i in sorted((i for i in range(n) if ops[i]["st"] < 0), key=lambda i: -st[i]):
+        q = queue[ops[i]["e"]]
+        q.insert(([k for k, j in enumerate(q) if st[j] > st[i] - PAR["lead"]] + [len(q)])[0], i)
+    listed, out, order, end = set(i for e in ENG for i in queue[e]), set(), [], [0.0] * n
+    free = dict((e, 0.0) for e in ENG)
+
+    def can(i):
+        return all(m in out or (m not in listed and can(m)) for m in up[i])
+
+    def put(i):
+        for m in sorted(up[i]):
+            if m not in out:
+                put(m)
+        end[i] = free[ops[i]["e"]] = max([free[ops[i]["e"]]] + [end[m] + lat[m] + PAR["hop"] for m in up[i]]) + ops[i]["c"]
+        out.add(i)
+        order.append(i)
+    while any(queue.values()):
+        able = [e for e in ENG if queue[e] and can(queue[e][0])]
+        if not able:
+            PAR.setdefault("stuck", []).append([(e, ops[queue[e][0]]["st"], ops[queue[e][0]]["tag"] or label(ops[queue[e][0]])) for e in ENG if queue[e]])
+            able = [e for e in ENG if queue[e]][:1]
+        i = queue[min(able, key=lambda e: max([free[e]] + [end[m] + lat[m] for m in up[queue[e][0]]]))].pop(0)
+        if i not in out:
+            put(i)
+    for i in range(n):
+        if i not in out:
+            put(i)
+    now = best = judge(order)
+    for it in range(PAR["iters"]):
+        _, i, why = now[2][rs.randint(len(now[2]))]
+        held, then = [], {}
+        while why[i] >= 0:
+            if why[i] not in ops[i]["dp"] and kind[why[i]] != kind[i]:
+                held.append((why[i], i))
+            then[why[i]] = i
+            i = why[i]
+        if not held:
+            continue
+        a, b = held[rs.randint(len(held))]
+        ahead = rs.rand() < 0.5
+        for _ in range(rs.randint(4) * rs.randint(6)):
+            if ahead and why[a] >= 0 and ops[why[a]]["e"] == ops[a]["e"]:
+                a = why[a]
+            elif not ahead and b in then and ops[then[b]]["e"] == ops[b]["e"]:
+                b = then[b]
+        order = list(now[1])
+        d = ops[a]["st"] - ops[b]["st"]
+        steps = range(RO) if min(ops[a]["st"], ops[b]["st"]) >= 0 and rs.rand() < 0.85 else [ops[b]["st"]]
+        for t in steps:
+            if (kind[a], t + d) in same and (kind[b], t) in same:
+                swap(order, same[(kind[a], t + d)], same[(kind[b], t)], ahead)
+        new = judge(order)
+        if new[0] <= now[0] + PAR["warm"] * (1.0 - it / PAR["iters"]) * rs.rand():
+            now = new
+            if new[0] < best[0]:
+                best = new
+    return best[1], [r[0] for r in best[2]]
 
 
 def plan():
@@ -720,15 +854,17 @@ def rank_program(g, core, T, topo):
         if not isinstance(x, tuple):
             return x
         if len(x) == 7:
-            return T["M7"][:, :, x[6][0]:x[6][1]]
-        if x[0] == "M7":
-            return T["M7"][x[4]:x[5], x[1] // 64, x[1] % 64:x[1] % 64 + x[2] - x[1]]
+            return T[x[0]][x[4]:x[5], :, x[6][0]:x[6][1]:x[6][2]]
+        if x[0] == "Z0":
+            return T["Z0"][x[4]:x[5], x[1] // 256, x[1] % 256:(x[2] - 1) % 256 + 1:x[3]]
         if x[3] == 1:
             return T[x[0]][x[4]:x[5], x[1]:x[2]]
         return T[x[0]][x[4]:x[5], x[1]:x[2]:x[3]]
 
     def ext(x):
         if x == "marks":
+            return T["S"][15::16, 0:2048]
+        if x == "marks2":
             return T["S"][15::16, 1280:1792]
         if isinstance(x, str):
             return T[x][:]
@@ -746,7 +882,7 @@ def rank_program(g, core, T, topo):
         for s, v in o["w"]:
             wait(q, s, v)
         if k == "send":
-            g.remote_dma(ap(a[2][0][0]), ap(a[2][0][1]), T.sem[o["sem"]], T.sem["sent"], pid, rid, mask)
+            g.remote_dma(ap(a[0]), ap(a[1]), T.sem[o["sem"]], T.sem["sent"], pid, rid, mask)
             nsent += nout
             ends.append(o["sig"])
             continue
@@ -756,8 +892,6 @@ def rank_program(g, core, T, topo):
             continue
         if k == "cp":
             r = q.tensor_copy(ap(a[0]), ap(a[1]))
-        elif k == "cpj":
-            r = q.tensor_copy(T["JS"][:, :, a[0]:a[1]], ap(a[2]))
         elif k == "tt":
             r = q.tensor_tensor(ap(a[0]), ap(a[1]), ap(a[2]), a[3])
         elif k == "ts":
@@ -769,17 +903,11 @@ def rank_program(g, core, T, topo):
             r = q.tensor_tensor_scan(ap(a[0]), ap(a[1]), ap(a[2]), 0.0, a[3], a[4])
         elif k == "ms":
             r = q.memset(ap(a[0]), a[1])
-        elif k == "red":
-            r = q.tensor_reduce(ap(a[0]), ap(a[1]), AxisListType.X, a[2], apply_absolute_value=a[3])
-        elif k == "gatm":
-            r = q.activation(ap(a[0]), ap(a[1]).indirect(ap(a[2])), AF.Identity, ap(a[3]), ap(a[4]))
         elif k == "gat":
             w = ap(a[1]).indirect(ap(a[2]))
-            r = q.tensor_copy(ap(a[0]), w) if o["e"] == "dve" else q.activation(ap(a[0]), w, AF.Identity)
+            r = q.tensor_copy(ap(a[0]), w) if o["e"] == "dve" else q.activation(ap(a[0]), w, AF.Identity, ap(a[3]), ap(a[4]))
         elif k == "gtt":
             r = q.tensor_tensor(ap(a[0]), ap(a[1]).indirect(ap(a[2])), ap(a[3]), a[4])
-        elif k == "sca":
-            r = q.tensor_copy(ap(a[0]).indirect(ap(a[1])), ap(a[2]))
         elif k == "act":
             if a[5] is None:
                 r = q.activation(ap(a[0]), ap(a[1]), a[2], ap(a[3]), ap(a[4]))
@@ -787,8 +915,6 @@ def rank_program(g, core, T, topo):
                 r = q.activation(ap(a[0]), ap(a[1]), a[2], ap(a[3]), ap(a[4]), accum_out=ap(a[5]))
         elif k == "mm":
             r = q.matmul(ap(a[0]), ap(a[1]), ap(a[2]), a[3], a[4])
-        elif k == "mmj":
-            r = q.matmul(ap(a[0]), T["JS"][:, 8 * a[1]:8 * a[1] + 8, :], ap(a[2]), False, a[3])
         elif k == "iota":
             if SB[a[0][0]][1] == I32:
                 r = q.iota(ap(a[0]), a[1], a[2], a[3])

import numpy as np
from concourse.mybir import AluOpType as OP, ActivationFunctionType as AF

RO = 5
F32, BF, F16, I32, U16 = "float32", "bfloat16", "float16", "int32", "uint16"
SB = {
    "S": (2048, BF), "EF": (2672, BF), "OT": (15136, BF), "GL": (128, BF), "RM": (8, BF),
    "QN": (384, I32), "QK": (384, I32), "TU": (128, I32), "MKS": (128, BF),
    "STG": (5 * 256, F16), "SL": (128, BF), "M3": (5 * 136, F16), "MC": (5 * 136, F32), "MK": (5 * 768, F16), "NG": (4 * 128, BF),
    "OB": (4 * 256, F16), "OL": (128, BF), "O3": (4 * 136, F16), "OC": (4 * 136, F32), "OK": (5 * 768, F16),
    "YQ": (384, F32), "YP": (384, F32), "GP": (128, BF),
    "CI": (16, I32), "CC": (48, F32), "IB": (128, BF), "I15": (128, BF), "NIB": (128, BF), "I8K": (128, BF), "I4K": (128, BF),
    "I1K": (128, BF), "N1K": (128, BF), "IA": (128, F16), "IM": (128, F16), "REP": (1024, BF), "BLK": (128, BF), "MX": (128, BF),
    "CM": (16, BF), "CF": (8, F32), "B8": (8, F32), "BX": (32, F32), "DG": (384, BF), "PM": (128, BF), "WU": (128, BF),
    "WS": (16, BF), "WM": (24, BF), "WX": (384, BF), "EC": (136, BF), "EN": (136, BF), "CR": (136, BF), "ONB": (136, BF),
    "R17H": (136, BF), "RS0": (512, BF), "RH": (384, BF), "IDU": (384, F16), "OHW": (384, BF),
    "WD": (24, BF), "WT": (24, BF), "ZB": (384, BF), "BD": (432, BF), "JS": (384, F16), "B8B": (8, BF), "P24": (32, BF), "ID4": (32, F32), "R4": (32, F32),
    "LI": (88, I32), "LS": (192, U16), "XB": (1024, BF), "T1": (512, BF), "T3": (144, BF), "T4": (48, F32), "TI": (48, I32),
    "CH": (256, BF), "KP": (16, F32), "DH": (384, F16), "D0": (64, F32),
    "TUB": (128, BF), "LU": (136, U16), "SG": (2048, BF), "VS": (2048, BF), "E": (2048, BF), "Y": (2048, BF), "D": (2048, BF),
    "TT": (2048, BF), "SCI": (160, I32), "SC2": (160, F32), "ST": (144, F32), "SN": (136, F32), "PR": (136, F32), "SCS": (136, F32), "UI": (8, I32),
    "NA": (8, I32), "UA": (8, I32), "XN": (128, F16), "XF": (128, F32), "LX": (16, U16), "X": (128, BF), "XT": (128, BF),
    "UB": (128, F32), "U": (128, F32), "N1": (128, I32), "N2": (128, I32), "NL": (128, U16), "AC": (16, F32),
    "DX": (128, BF), "TX": (128, BF), "NH": (48, F16), "NH2": (24, F16), "SU": (512, F32), "PB": (64, F32), "P1": (64, I32),
    "GO": (8, BF), "LA": (24, U16), "AL": (16, I32), "OH": (128, BF), "KM": (384, F16), "SQ": (400, F16), "EQ": (384, BF), "KH": (384, F16),
    "A2": (384, F16), "RN": (384, F16), "NK": (384, F32), "CK": (384, F32), "PF": (32, F32), "PX": (32, F32), "MM": (64, I32),
    "EQ4": (32, F32), "E5": (32, F32), "MI": (16, I32), "HI": (16, I32), "LO": (8, F32), "OHH": (256, BF), "OHL": (1024, BF),
    "PI": (32, I32), "PJ": (32, I32), "PE2": (384, BF),
}
PACK = {}
for _n in list(SB):
    _w, _d = SB[_n]
    if _w <= 64 and _n != "RM":
        _o = SB.get("small_" + _d, (0, _d))[0]
        PACK[_n] = ("small_" + _d, _o)
        SB["small_" + _d] = (_o + (_w + 15) // 16 * 16, _d)
SCRATCH = {}
for _n in SB:
    if _n not in PACK:
        SCRATCH[_n] = ("sbuf", [128, SB[_n][0]], SB[_n][1])
BANKS = ["Z0", "Z1", "W0", "W1", "J1", "J2", "M6", "M7"]
for _n in BANKS:
    SCRATCH[_n] = ("psum", [128, 2, 256] if _n == "Z0" else [128, 512], F32)
ENG = ["pe", "dve", "act", "pool", "sp"]
NDMA = 40
SEMAPHORES = ["c_" + e for e in ENG[:4]] + ["d%d" % i for i in range(NDMA)] + ["sent"] + \
    ["r%d_%d" % (m, t) for m in range(5) for t in range(5)]

PAR = {"cy": 0.95, "pcy": 0.5, "hop": 180.0, "rlat": 1200.0, "dlat": 2200.0, "issue": 500.0, "gf": 1.56, "bw": 100.0, "fix": 0.0,
       "sg": [("dve", 0, 32), ("dve", 32, 64), ("act", 64, 96), ("act", 96, 128)], "sm": [(0, 32), (64, 96), (32, 64), (96, 128)],
       "vs": [0, 512, 1024, 1536, 1792, 2048],
       "eg": [("dve", 64, 80), ("dve", 80, 96), ("dve", 96, 112), ("dve", 112, 128), ("act", 0, 16), ("act", 16, 48), ("act", 48, 64)],
       "ch": [(1024, 1536, "", "W1"), (0, 256, "Z0", "W0"), (256, 768, "Z1", "J2"), (768, 1024, "Z0", "W1"), (1536, 1792, "", "W0"),
              (1792, 2048, "", "J2")],
       "seed": 0, "iters": 35000, "warm": 120.0, "fu": 1024,
       "lead": 2000.0, "turned": 4,
       "cases": [(1.09, 100.0, 0.0), (0.88, 250.0, 300.0)],
       "on": {"N16": "dve", "JS": "dve", "O3": "dve", "LX0": "act", "LX1": "dve", "yb": "act", "nm": "dve", "Sb": "dve", "lab": "act"}}


ORDER = {
    "dve": "SG SG VS VS VS VS SCI SC2 NA ST XN PR VS HI HI SCS KM XF KM KM UI UA LX SQ N1 TX OHL*2 N2 OHL*3 NL OHL*3 E E OHH y0 y1 E y2 "
           "y3 t0 E y4 t1 OHH y5 t2 t3 OHH js t4 t5 OHH SU PB MKS P1 AL GO OB OK OK PX PF MM O3 EQ4 OC MM MI LU S PI PJ PE2",
    "act": "SG SG LU OH DH*3 SN LX LO X XB U XT DX XB XB NH NH NH2 E E E XB d0 EQ d1 d2 d3 d4 d5 RN D0 NK A2 LA lab OB OL O3 CK S GP ys AC*2 E5 OC*3 AC*4 OC*2",
    "pe": "cd*3 mk0 cd*69 mk*17 J2 M6 v*17 Z1 W0 Z0 J2 wg0 wg1 zx1 zx2 J2*2 idu eq*20 wg2 hx*9 ze1 hx*8 wy0 ze2 wy1 zx3 ze3 sd0*4 wy2 wg3 wy3 st0*4 "
          "rn*4 sd1*2 wg4 wy4 st1*2 wg5 wy5 sd2*4 st2*4 sd3*2 st3*2 sd4*4 sd5*4 st4*2 mmj*3 st5*2 mrk*10 nk*4 nr W1*2 W0*17 J1 W1*4",
    "pool": "NG STG SL M3 MK MC", "sp": "S"}


def A(n, a=0, b=None, s=1, p0=0, p1=128):
    if b is None:
        b = 512 if n in BANKS else (384 if n == "JS" else SB[n][0])
    if n in PACK:
        return (PACK[n][0], a + PACK[n][1], b + PACK[n][1], s, p0, p1)
    return (n, a, b, s, p0, p1)


def G(a, b, s=1, p0=0, p1=128):
    return ("Z0", a, 256 + b, 2, p0, p1, (a, b, s))


def cnt(x):
    if len(x) == 7:
        return 2 * ((x[6][1] - x[6][0] + x[6][2] - 1) // x[6][2])
    return (x[2] - x[1] + x[3] - 1) // x[3]


def two(x):
    return x[0] == "JS" or (x[0] in SB and SB[x[0]][1] in (BF, F16, U16))


def build():
    ops = []
    now, tag = [-1], [""]
    CY, PCY, GF, ON = PAR["cy"], PAR["pcy"], PAR["gf"], PAR["on"]

    def op(eng, kind, args, rd, wr, cost, **kw):
        d = {"e": eng, "k": kind, "a": args, "rd": [r for r in rd if isinstance(r, tuple)], "wr": wr,
             "c": cost + (PAR["fix"] if eng in ("dve", "act") else 0.0), "st": now[0], "tag": tag[0]}
        d.update(kw)
        ops.append(d)
        return d

    def vc(n, *aps):
        f = 0.5 if all(two(x) for x in aps) else 1.0
        return max(64.0, n * f) * CY

    def act(o, i, f=AF.Identity, bias=0.0, scale=1.0, acc=None):
        op("act", "act", (o, i, f, bias, scale, acc), [i, bias, scale], [o] + ([acc] if acc else []), max(64.0, cnt(o)) * CY)

    def cp(o, i, e="dve"):
        if e == "act":
            act(o, i)
        else:
            op("dve", "cp", (o, i), [i], [o], vc(cnt(o), o, i))

    def tt(o, a, b, f):
        k = 1 if (a[0] in BANKS or b[0] in BANKS) else 2
        op("dve", "tt", (o, a, b, f), [a, b], [o], vc(cnt(o) * k, o, a, b))

    def ts(o, a, s1, s2, f0, f1=None):
        op("dve", "ts", (o, a, s1, s2, f0, f1), [a, s1, s2], [o], vc(cnt(o), o, a))

    def scan(o, d0, d1, f0, f1):
        op("dve", "scan", (o, d0, d1, f0, f1), [d0, d1], [o], vc(cnt(o), o, d0, d1))

    def ms(o, v):
        op("dve", "ms", (o, v), [], [o], vc(cnt(o), o))

    def gat(e, o, w, l, bias=0.0, scale=1.0):
        op(e, "gat", (o, w, l, bias, scale), [w, l, bias, scale], [o], 60 + cnt(o) * GF * CY)

    def gtt(o, w, l, b, f):
        op("dve", "gtt", (o, w, l, b, f), [w, l, b], [o], 55 + cnt(o) * GF * CY)

    def mm(o, l, r, st, sp):
        f = 4 if SB.get(l[0], (0, 0))[1] == F32 else 1
        op("pe", "mm", (o, l, r, st, sp), [l, r], [o], max(min(64, cnt(l)), cnt(r)) * f * PCY)

    def iota(o, pat, base, cm):
        op("pool", "iota", (o, pat, base, cm), [], [o], 130 + 2 * cnt(o) * CY)

    def asel(o, i, pat, f, base, cm):
        op("pool", "asel", (o, i, pat, f, 0.0, base, cm), [i], [o], 170 + 2 * cnt(o) * CY)

    nd = [0]

    def dma(e, o, i, rd, wr, extra=0.0):
        op(e, "dma", (o, i), rd, wr, 60.0, lat=PAR["dlat"] + extra, sem="d%d" % nd[0])
        nd[0] += 1

    def send(m, t, dst, src):
        op("pool", "send", (dst, src), [src], [dst], PAR["issue"] + cnt(dst) * (256 if two(dst) else 512) / PAR["bw"],
           lat=PAR["rlat"], sem="r%d_%d" % (m, t))

    def C(j):
        return A("CC", j, j + 1)

    def blk(n, j, w=128, o=0):
        return A(n, o + w * j, o + w * j + w)

    def half(n, h, a=0, b=None):
        return A(n, a, b, 1, 64 * h, 64 * h + 64)

    for q in range(8):
        dma("act" if q % 2 else "sp", A("TU", 16 * q, 16 * q + 16, p1=24), ("tu", q), [], [A("TU", 16 * q, 16 * q + 16)])
    dma("act", A("QN"), "qn", [], [A("QN")], 300)
    dma("sp", A("S", 0, 1792), "st0", [], [A("S", 0, 1792)], 1200)
    dma("act", A("QK"), "qk", [], [A("QK")], 1500)
    dma("sp", A("GL"), "gl", [], [A("GL")], 1500)
    dma("sp", A("OT", 0, 256), "ot", [], [A("OT", 0, 256)], 1700)
    dma("sp", A("RM", 0, 1), "rm", [], [A("RM")], 1700)
    dma("sp", A("EF", 0, 2048), "ef", [], [A("EF", 0, 2048)], 2800)
    dma("sp", A("EF", 2048, 2672), ("ef", 0, 624), [], [A("EF", 2048, 2672)], 3200)
    ms(A("S", 1792, 2048), 0.0)
    dma("sp", A("MKS"), "marks", [A("S")], [A("MKS")])
    for a, b in ((256, 256), (512, 512), (1024, 1024), (2048, 2048), (4096, 4096), (8192, 4096), (12288, 2848)):
        dma("sp", A("OT", a, a + b), A("OT", 0, b), [A("OT", 0, b)], [A("OT", a, a + b)], 1.5 * b)

    BIG = 2.0 ** 24
    iota(A("CI", 0, 1), [[0, 1]], 0, 1)
    iota(A("TI", 0, 24), [[1, 24]], 0, 0)
    iota(A("ID4"), [[16, 8], [128, 4]], 0, 0)
    ms(A("ONB"), 1.0)
    ms(A("P24"), 512.0)
    asel(A("P24"), A("P24"), [[1, 8], [8, 4]], OP.is_equal, 0, -1)
    asel(A("IB"), A("ONB", 0, 128), [[-1, 128]], OP.is_equal, 0, 1)
    iota(A("T1"), [[0, 32], [1, 16]], 0, 0)
    iota(A("T3"), [[1, 144]], 0, 0)
    iota(A("REP"), [[1, 64], [0, 16]], 0, 0)
    iota(A("CH"), [[0, 4], [-16, 2], [1, 32]], 0, 0)
    for j, (sh, m) in enumerate(((0, 15), (4, 7), (0, 1), (1, 7), (0, 7), (3, 15), (2, 3), (0, 3), (0, 63))):
        ts(A("CI", 1 + j, 2 + j), A("CI", 0, 1), sh, m, OP.arith_shift_right, OP.bitwise_and)
    cp(A("CC", 0, 7), A("CI", 0, 7))
    cp(A("CC", 22, 25), A("CI", 7, 10))
    act(A("ID4"), A("ID4"), bias=C(1))
    ms(A("ID4", 3, 32, 4), 2.0 ** 20)
    ms(A("R4"), 0.0)
    ms(A("R4", 0, 32, 4), 2 * BIG)
    for a, pat, base in ((0, [[1, 32]], 0), (32, [[1, 8], [0, 2]], 0), (48, [[17, 16]], 16), (64, [[1, 3], [4, 8]], 0)):
        iota(A("LI", a, a + int(np.prod([x[1] for x in pat]))), pat, base, 0)
    cp(A("LS", 0, 88), A("LI"))
    cp(A("LS", 114, 178), A("T3", 0, 64))
    ts(C(25), C(22), 4.0, 3.0, OP.mult, OP.add)
    ts(A("LS", 106, 108), A("TI", 0, 2), 16.0, C(25), OP.mult, OP.add)
    ts(A("LS", 108, 110), A("TI", 0, 2), 4.0, C(22), OP.mult, OP.add)
    ts(C(11), C(5), 16.0, None, OP.mult)
    ts(C(26), C(1), 8.0, C(11), OP.is_ge, OP.add)
    ts(A("LS", 88, 96), A("TI", 0, 8), 2.0, C(26), OP.mult, OP.add)
    ts(A("T4", 0, 9), A("TI", 0, 9), 16.0, C(1), OP.mult, OP.add)
    ts(A("TI", 32, 41), A("T4", 0, 9), 1.0 / 17, -0.47, OP.mult, OP.add)
    ts(A("T4", 16, 25), A("TI", 32, 41), 17.0, None, OP.mult)
    tt(A("T4", 0, 9), A("T4", 0, 9), A("T4", 16, 25), OP.not_equal)
    ts(A("T4", 16, 25), A("T4", 16, 25), 32.0, 152.0, OP.add, OP.min)
    tt(A("LS", 96, 105), A("T4", 0, 9), A("T4", 16, 25), OP.mult)
    ms(A("SC2"), -2.0 ** 30)
    ms(A("SCI"), 0)
    ms(C(38), 15.0)
    act(C(27), C(22), bias=C(38), scale=16.0)
    act(C(28), C(23), bias=C(27), scale=128.0)
    ts(C(39), C(23), 2.0, -384.0, OP.is_ge, OP.mult)
    ts(C(39), C(39), 128.0, C(28), OP.add, OP.add)
    ts(A("LS", 110, 112), A("TI", 0, 2), 64.0, C(28), OP.mult, OP.add)
    ts(A("LS", 112, 114), A("TI", 0, 2), 64.0, C(39), OP.mult, OP.add)
    act(C(3), C(3), bias=C(2), scale=8.0)
    act(C(5), C(6), bias=C(11))
    act(C(7), C(1), scale=37.0)
    ts(C(8), C(1), 15.0, None, OP.not_equal)
    ts(C(9), C(1), 15.0, None, OP.is_equal)
    ts(C(12), C(1), 0.5, C(8), OP.add, OP.mult)
    ts(C(14), C(1), 3.0, -2048.0, OP.is_lt, OP.mult)
    ts(C(15), C(0), 1.0, 2048.0, OP.is_equal, OP.mult)
    ts(C(16), C(0), BIG - 2048, -BIG, OP.mult, OP.add)
    act(C(21), C(1), scale=128.0)
    for j, v in ((13, -63.5), (20, -127.5), (33, -0.5), (34, -1024.0), (35, BIG), (36, 32.0), (37, 1024.0), (40, 2.0 ** 27)):
        ms(C(j), v)
    ts(C(32), C(1), 37.0, -64.0, OP.mult, OP.add)
    ts(C(41), C(1), -1.0, 2.5, OP.mult, OP.add)
    act(A("KP", 0, 5), A("T3", 0, 5), AF.Abs, C(41))
    ts(A("KP", 0, 5), A("KP", 0, 5), 2.5, None, OP.not_equal)
    act(C(42), C(0), scale=0.5)
    act(A("KP", 8, 13), A("T3", 0, 5), bias=C(42), scale=64.0)
    ts(A("CC", 17, 20), A("TI", 0, 3), C(1), None, OP.is_equal)
    ts(A("CC", 29, 32), A("CC", 17, 20), 2047.0, C(14), OP.mult, OP.add)
    ts(A("B8"), A("TI", 0, 8), C(2), None, OP.is_equal)
    act(A("BX", 0, 8), A("B8"), scale=C(9))
    act(A("BX", 8, 16), A("B8"), scale=C(12))
    act(A("BX", 16, 24), A("B8"), scale=C(8))
    act(A("WS", 0, 8), A("BX", 0, 8), scale=2.0 ** 26)
    act(A("WS", 8, 16), A("BX", 8, 16), scale=2.0)
    for l in range(3):
        act(blk("WM", l, 8), A("BX", 0, 8), scale=1024.0)
    ts(A("CM", 0, 8), A("TI", 0, 8), C(4), None, OP.is_equal)
    act(A("CF"), A("CM", 0, 8), scale=8192.0)
    ts(A("MX"), A("T1", 0, 128), C(3), None, OP.is_equal)
    ts(A("DG"), A("T1", 0, 384), C(1), None, OP.is_equal)
    act(A("RS0"), A("T1"), AF.Sign)
    act(A("RH"), A("RS0", 0, 384), bias=C(40), scale=-2.0 ** 27)
    ts(A("REP"), A("REP"), C(24), None, OP.is_equal)
    asel(A("EN"), A("ONB"), [[-16, 8], [-1, 17]], OP.is_equal, 1, 1)
    ms(A("EN", 0, 136, 17), 0.0)
    act(A("EC"), A("EN"), scale=32768.0)
    asel(A("EN", 0, 136, 17), A("ONB", 0, 8), [[-16, 8]], OP.is_equal, 0, 1)
    iota(A("CR"), [[0, 8], [1, 17]], 0, 0)
    ts(A("CR", p1=2), A("CR", p1=2), A("CC", 15, 16, p1=2), A("CC", 16, 17, p1=2), OP.mult, OP.add)
    ms(A("CR", 0, 136, 17), 244.0 * 32768)
    ms(A("R17H"), 0.0)
    ms(A("R17H", 0, 136, 17), 2.0 ** 27)
    ms(A("ZB"), 0.0)
    ms(A("SQ", 0, 16), 0.0)
    ms(A("SU", 384, 512), 0.0)
    ms(A("D0"), -2 * BIG)
    ms(A("D0", 0, 64, 4), 2 * BIG)
    asel(A("BLK"), A("ONB", 0, 128), [[-16, 8], [0, 16]], OP.is_ge, 0, 1)
    asel(A("BLK"), A("BLK"), [[16, 8], [0, 16]], OP.is_ge, 15, -1)
    for n, v in (("I15", C(8)), ("NIB", -1.0), ("I8K", 8192.0), ("I4K", 4096.0), ("I1K", 1024.0), ("N1K", -1024.0), ("IA", 1026.0),
                 ("IM", -1025.0)):
        act(A(n), A("IB"), scale=v)
    for l in range(3):
        act(blk("OHW", l), A("ONB", 0, 128), scale=C(17 + l))
        act(blk("WX", l), A("BLK"), scale=C(29 + l))
        act(blk("IDU", l), A("T3", 0, 128), bias=C(21))
    ts(A("PM"), A("T3", 0, 128), C(5), -1.0, OP.is_equal, OP.mult)
    act(C(43), C(2), bias=C(38), scale=16.0)
    act(C(44), C(8), scale=8192.0)
    ts(C(45), C(0), 64.0, -1.0, OP.is_lt, OP.mult)
    ts(C(46), C(0), 64.0, -1.0, OP.is_ge, OP.mult)
    ts(A("BD", 0, 144), A("T3"), C(43), C(44), OP.is_equal, OP.mult)
    act(A("BD", 144, 288), A("BD", 0, 144), scale=16.0)
    ts(A("BD", 288, 432), A("BD", 0, 144), A("RM", 0, 1), None, OP.mult)
    ts(A("WU"), A("BLK"), C(12), 2.0, OP.mult, OP.mult)
    ms(A("WD", 8, 16), 0.0)
    ms(A("WT"), 0.0)
    act(A("WD", 0, 8), A("BX", 16, 24))
    ts(A("WD", 16, 24), A("B8"), A("RM", 0, 1), None, OP.mult)
    act(A("WT", 8, 16), A("BX", 16, 24), scale=16.0)
    act(A("AC", 0, 1), C(7))
    act(A("B8B"), A("B8"))

    def control(t, n, o):
        scan(A("MM", 0, 32), A("R4"), A("PF"), OP.add, OP.min)
        if t == 0:
            ts(A("AL", 0, 8), A("MM", 3, 32, 4), 511, None, OP.bitwise_and)
            cp(A("LU", 128, 136), A("AL", 0, 8))
        gtt(A("EQ4"), A("MM", 0, 32), A("LS", 106, 108), A("PF"), OP.is_equal)
        act(A("E5"), A("EQ4"), scale=512.0)
        act(A(n, o + 32, o + 64), A("EQ4"), scale=-1536.0)
        for h in range(2):
            act(A(n, o + 64 + 32 * h, o + 96 + 32 * h), A("EQ4"), bias=C(35), scale=4096.0 - BIG)
        tt(A(n, o, o + 32), A("PF"), A("E5"), OP.add)
        scan(A("MM", 32, 64), A("R4"), A(n, o, o + 32), OP.add, OP.min)
        ts(A("MI"), A("MM", 3, 64, 4), 511, None, OP.bitwise_and)
        act(A(n, o + 128, o + 136), A("MI", 0, 8), scale=-1.0)
        act(A(n, o + 67, o + 96, 4), A("MI", 8, 16))

    cp(A("TUB", p1=24), A("TU", p1=24))
    mm(A("M6", 0, 32), A("TUB", p1=24), A("P24", p1=24), True, True)
    tt(A("PF"), A("ID4"), A("M6", 0, 32), OP.add)
    control(0, "MC", 0)
    gat("dve", A("LU", 0, 128), A("QN"), A("LU", 128, 136))
    gat("act", A("M3", 0, 128), A("QK"), A("LU", 128, 136))
    gat("act", A("STG", 128, 256), A("QN"), A("LU", 128, 136))
    cp(A("KH"), A("QK"), "act")
    for l in range(3):
        mm(blk("J2", l), blk("KH", l), A("IB"), True, True)
    cp(blk("MK", 0, 384), A("J2", 0, 384), "act")
    cp(blk("MK", 1, 384), A("QN"), "act")
    gat("act", A("GP"), A("GL"), A("LS", 88, 96))
    mm(A("J1", 0, 128), A("GP"), A("NIB"), True, True)
    act(A("NG", 0, 128), A("J1", 0, 128))

    SW = A("S", 0, 1792)
    fu = PAR["fu"]
    for t in range(RO):
        last = t == RO - 1
        now[0] = t
        u1, m3 = 256 * t, 136 * t
        ng = lambda h: half("NG", h, 128 * (t % 4), 128 * (t % 4) + 128)
        jl = A("LU", 128, 136)
        keys, names = blk("MK", 2 * t, 384), blk("MK", 2 * t + 1, 384)
        newkeys, newnames = blk("OK", 2 * t, 384), blk("OK", 2 * t + 1, 384)
        if t < 3:
            send(0, t + 1, blk("NG", t + 1), blk("NG", t))
        for e, a, b in PAR["sg"]:
            gat(e, A("SG", 16 * a, 16 * b), SW, A("LU", a, b))
        tag[0] = "cd"
        mm(G(0, 136), A("IB"), A("ZB", 0, 272), True, False)
        mm(A("Z0", 0, 136), A("ONB", 0, 128, p1=2), A("CR", p1=2), False, False)
        mm(A("Z0", 0, 136), A("STG", u1 + 128, u1 + 256), A("EN"), False, False)
        for a, b in PAR["sm"]:
            mm(A("Z0", 256, 392, 17, a, b), A("SG", 16 * a, 16 * b, 16), A("WS", 8, 16), False, False)
            for k in range(16):
                mm(G(k + 1, 136, 17, a, b), A("SG", 16 * a + k, 16 * b, 16), A("WS"), False, False)
        mm(A("Z0", 0, 136), A("M3", m3, m3 + 128), A("EC"), False, True)
        tag[0] = ""
        vs = PAR["vs"]
        for a, b in zip(vs[:-1], vs[1:]):
            scan(A("VS", a, b), A("RS0", 0, b - a), A("SG", a, b), OP.mult, OP.max)
        tag[0] = "v"
        mm(A("W0", 0, 8), A("IB"), A("ZB", 0, 8), True, False)
        for r in range(16):
            a = 16 * (16 * (r % 8) + r // 8) + 15
            mm(A("W0", 0, 8), A("BD", 15 - r, 143 - r), A("VS", a, a + 225, 32), False, False)
        tag[0] = ""
        if t > 0:
            cp(jl, A("M3", m3 + 128, m3 + 136), "act")
        gat("act", A("OH"), A("OHW"), jl)
        tag[0] = "mk0"
        mm(A("J1", 0, 384), A("IB"), A("ZB"), True, False)
        tag[0] = "mk"
        for k in range(16):
            mm(A("J1", k, 384, 16), A("SG", k, 2048, 16), A("WM"), False, False)
        mm(A("J1", 0, 384), A("OH"), A("WX"), False, True)
        tag[0] = ""
        least = A("SCI", 32, 152, 17)
        scan(A("SCI", 16, 152), A("R17H"), A("Z0", 0, 136), OP.add, OP.min)
        scan(A("SC2", 16, 152), A("R17H"), A("Z0", 0, 136), OP.add, OP.min)
        gtt(A("ST"), A("SC2"), A("LS", 96, 105), A("SCI", 15, 159), OP.is_lt)
        ts(A("NA"), least, 2047, None, OP.bitwise_and)
        tt(A("PR"), A("Z0", 256, 392), A("ST", 0, 136), OP.mult)
        act(A("SN"), A("ST", 0, 136), bias=1.0, scale=-1.0)
        gtt(A("XN"), A("NA"), A("LS", 0, 8), A("MX"), OP.mult)
        scan(A("SCS"), A("SN"), A("PR"), OP.mult, OP.add)
        mm(A("M6", 0, 8), A("XN"), A("CM", 0, 8), True, True)
        cp(A("LX", 0, 8), A("M6", 0, 8), ON["LX0"])
        gat("act", A("X"), SW, A("LX", 0, 8))
        gtt(A("XF"), A("SCS"), A("LS", 48, 56), A("MX"), OP.mult)
        mm(A("W0", 0, 8), A("XF"), A("CF"), False, True)
        mm(A("Z1", 0, 128), A("WU"), A("X"), True, True)
        if t == 0:
            ts(A("UI"), A("W0", 0, 8), 1.0 / 8192, None, OP.mult)
            ts(A("UA"), A("UI"), 255, None, OP.bitwise_and)
            cp(A("LX", 8, 16), A("UA"))
        else:
            ts(A("LX", 8, 16), A("W0", 0, 8), 1.0 / 8192, None, OP.mult)
        act(A("U"), A("Z1", 0, 128), bias=C(36))
        mm(A("Z0", 0, 128), A("X"), A("I15"), True, True)
        act(A("XT"), A("Z0", 0, 128))
        gtt(A("N1"), A("OT", 0, 256 if t == 0 else 15136), A("LX", 8, 16), A("U"), OP.mult)
        ts(A("N2"), A("N1"), 5, 2047, OP.arith_shift_right, OP.bitwise_and)
        ts(A("NL"), A("N2"), A("AC", 0, 1), None, OP.add)
        for a in range(0, 2048 - fu, 256):
            b = min(2048 - fu, a + 256)
            gat("act", A("XB", a, b), A("X", fu // 16, 128), A("LS", 114 + a // 16, 114 + b // 16), 0.0, C(8))
        mm(A("J2", 0, 128), blk("NG", t % 4), A("IB"), True, False)
        mm(A("J2", 0, 128), A("I15"), A("X"), False, True)
        act(A("DX"), A("J2", 0, 128), AF.Abs)
        ts(A("TX"), A("DX"), 5.0, None, OP.is_gt)
        mm(A("J2", 128, 152), A("DX"), A("WD"), True, False)
        mm(A("J2", 128, 152), A("TX"), A("WT"), False, True)
        for h in range(2):
            act(blk("NH", h, 24), A("J2", 128, 152), scale=C(45 + h))
        act(A("NH2"), A("J2", 128, 152), bias=C(37), scale=-1.0)
        for l in range(3):
            tt(blk("KM", l), blk("J1", l), blk("MK", 6 * t + l), OP.max)
        scan(A("SQ", 16, 400), A("RS0", 0, 384), A("KM"), OP.mult, OP.max)
        tag[0] = "eq"
        mm(A("M7", 0, 384), A("IA"), A("SQ", 16, 400), True, False)
        mm(A("M7", 0, 384, 16), A("IB"), A("SQ", 15, 399, 16), False, False)
        mm(A("M7", 0, 384, 16), A("IB"), A("ONB", 0, 24), False, False)
        for k in range(16):
            mm(A("M7", k, 384, 16), A("IM"), A("SQ", 31, 400, 16), False, False)
        mm(A("M7", 0, 384), A("NIB"), A("SQ", 15, 399), False, True)
        tag[0] = ""
        act(A("EQ"), A("M7", 0, 384), AF.Sign, C(33))
        for l in range(3):
            act(blk("DH", l), A("IB"), scale=A("KP", 8 + t, 9 + t))
        tag[0] = "nk"
        mm(A("M7", 0, 384), A("ONB", 0, 128), A("DH"), True, False)
        for l in range(3):
            mm(blk("M7", l), blk("EQ", l), blk("DH", 0), False, False)
        tag[0] = "idu"
        mm(A("M6", 0, 384), A("IB"), A("IDU"), True, False)
        tag[0] = ""
        for e, a, b in PAR["eg"]:
            if 16 * a >= fu:
                gtt(A("E", 16 * a, 16 * b), A("EF"), A("NL", a, b), A("XB", 16 * a - fu, 16 * b - fu), OP.add)
            else:
                gat(e, A("E", 16 * a, 16 * b), A("EF"), A("NL", a, b))
        tag[0] = "hx"
        mm(A("J1", 0, 384), A("IB"), A("ZB"), True, False)
        jo = lambda b: A("J1", b, 384, 16)
        for b in range(16):
            mm(jo(b), blk("REP", b % 8), blk("NH", b // 8, 24), False, False)
        tag[0] = ""
        ch, turned = PAR["ch"], PAR["turned"]

        def spread(bank, a, b, src):
            mm(A(bank, 0, b - a), src(a // 1024), half("REP", a // 1024, a % 1024, (b - 1) % 1024 + 1), True, False)
        for c, (a, b, zb, wb) in enumerate(ch):
            z, w = A(zb or "E", 0 if zb else a, b - a if zb else b), A(wb, 0, b - a)
            if zb:
                tag[0] = "zx%d" % c
                spread(zb, a, b, lambda h: half("XT", h))
                tag[0] = "ze%d" % c
                mm(z, A("IB"), A("E", a, b), False, True)
            tag[0] = "y%d" % c
            ts(A("Y", a, b), z, 0.0, 63.0, OP.max, OP.min)
            tag[0] = "wg%d" % c
            spread(wb, a, b, ng)
            tag[0] = "wy%d" % c
            mm(w, A("IB"), A("Y", a, b), False, True)
            tag[0] = "d%d" % c
            act(A("D", a, b), w, AF.Abs)
            tag[0] = "t%d" % c
            ts(A("TT", a, b), A("D", a, b), 5.0, None, OP.is_gt)
            qs = range(a // 128, b // 128)
            if c < turned:
                tag[0] = "sd%d" % c
                for q in qs:
                    mm(jo(q), blk("D", q), A("WD"), False, False)
                tag[0] = "st%d" % c
                for q in qs:
                    mm(jo(q), blk("TT", q), A("WT"), False, c == turned - 1 and q == qs[-1])
            else:
                for l, src in ((0, "D"), (2, "D"), (1, "TT")):
                    tag[0] = ("st%d" if l == 1 else "sd%d") % c
                    for q in qs:
                        mm(blk("M6", l), A("BD", 144 * l + 15 - q, 144 * l + 143 - q), blk(src, q), False,
                           l == 1 and c == len(ch) - 1 and q == qs[-1])
            if c == turned - 1:
                tag[0] = "js"
                cp(A("JS"), A("J1", 0, 384), ON["JS"])
                tag[0] = "mmj"
                for l in range(3):
                    mm(blk("M6", l), blk("JS", l), A("I8K"), False, False)
        tag[0] = "rn"
        mm(A("Z1", 0, 384), A("IB"), names, True, False)
        for l in range(3):
            mm(blk("Z1", l), blk("EQ", l), A("N1K"), False, l == 2)
        tag[0] = ""
        act(A("RN"), A("Z1", 0, 384), AF.Relu, C(34))
        tag[0] = "nr"
        mm(A("M7", 0, 384), A("IB"), A("RN"), False, True)
        tag[0] = ""
        if not last:
            act(A("NK"), A("M7", 0, 384))
        cp(newnames, A("M7", 0, 384), ON["N16"])
        ts(A("HI", 0, 8), least, 7, 15, OP.arith_shift_right, OP.bitwise_and)
        ts(A("HI", 8, 16), least, 127, None, OP.bitwise_and)
        act(A("LO"), A("HI", 8, 16))
        for h in range(4):
            gtt(blk("OHH", h, 64), A("HI", 0, 8), A("LS", 32 + 4 * h, 36 + 4 * h), blk("CH", h, 64), OP.is_equal)
        for q in range(8):
            ts(blk("OHL", q), A("T3", 0, 128), A("LO", q, q + 1), None, OP.is_equal)
        tag[0] = "mrk"
        mm(A("Z0", 0, 128), A("IB"), A("ZB", 0, 128), True, False)
        for q in range(8):
            mm(A("Z0", 0, 128, 1, 32 * (q // 2), 32 * (q // 2) + 32), blk("OHH", q, 32), blk("OHL", q), False, False)
        mm(A("Z0", 0, 128), A("IB"), A("MKS"), False, True)
        tag[0] = ""
        ts(A("MKS"), A("Z0", 0, 128), 1.0, A("KP", t, t + 1), OP.min, OP.mult)
        dma("sp", "marks", A("MKS"), [A("MKS")], [A("S", 0, 2048, 1, 15, 16)])
        act(A("D0", 3, 32, 4), A("MC", m3 + 128, m3 + 136))
        scan(A("SU", 0, 384), A("RH"), A("M6", 0, 384), OP.add, OP.min)
        gtt(A("PB"), A("SU"), A("LS", 110, 114), A("MC", m3 + 64, m3 + 128), OP.add)
        scan(A("P1"), A("D0"), A("PB"), OP.max, OP.min)
        ts(A("AL"), A("P1", 2, 64, 4), 2047, None, OP.bitwise_and)
        tag[0] = "lab"
        cp(A("LA", 0, 16), A("AL"), ON["lab"])
        tag[0] = ""
        if not last:
            njl = A("LA", 16, 24)
            act(njl, A("P1", 3, 32, 4), AF.Abs)
            gat(ON["yb"], A("OB", u1, u1 + 128), A("Y"), A("LA", 8, 16))
            gat(ON["nm"], A("OB", u1 + 128, u1 + 256), A("NK"), njl)
            send(2, t, blk("STG", t + 1, 256), blk("OB", t, 256))
        else:
            gat("act", A("OL"), A("Y"), A("LA", 8, 16))
            send(2, t, A("SL"), A("OL"))
        ts(A("GO"), A("P1", 2, 32, 4), 0.0, None, OP.is_lt)
        mm(A("W1", 0, 384), A("IB"), A("KM"), True, False)
        mm(A("W1", 0, 384), A("N1K"), A("EQ"), False, True)
        act(A("A2"), A("W1", 0, 384), AF.Relu, C(34))
        mm(A("W0", 0, 384), A("I1K"), A("EQ"), True, False)
        for k in range(16):
            mm(A("W0", k, 384, 16), A("PM"), A("NH2"), False, k == 15)
        tt(newkeys, A("W0", 0, 384), A("A2"), OP.max)
        gtt(A("PX"), A("GO"), A("LS", 108, 110), A("MC", m3 + 32, m3 + 64), OP.mult)
        tt(A("PF"), A("PX"), A("MC", m3, m3 + 32), OP.add)
        if not last:
            for l in range(3):
                mm(blk("W1", l), blk("OK", 6 * t + l), A("IB"), True, True)
            act(A("CK"), A("W1", 0, 384))
            gat(ON["O3"], A("O3", m3, m3 + 128), A("CK"), njl)
            act(A("O3", m3 + 128, m3 + 136), A("P1", 3, 32, 4), AF.Abs)
            control(t + 1, "OC", m3)
            send(3, t, blk("M3", t + 1, 136), blk("O3", t, 136))
            send(1, t, blk("MK", t + 1, 768), blk("OK", t, 768))
            send(4, t, blk("MC", t + 1, 136), blk("OC", t, 136))
            mm(A("J1", 0, 8), A("BLK"), A("GO"), True, True)
            act(A("AC", 8, 16), A("J1", 0, 8), acc=A("AC", 4, 5))
            act(A("AC", 5, 6), A("AC", 4, 5), AF.Sign, C(13))
            act(A("AC", 6, 7), A("AC", 4, 5), AF.Sign, C(20))
            act(A("AC", 7, 8), A("AC", 4, 5), bias=C(32))
            act(A("AC", 3, 4), A("AC", 5, 6), bias=A("AC", 7, 8), scale=-32.0)
            act(A("AC", 0, 1), A("AC", 6, 7), bias=A("AC", 3, 4), scale=-32.0)
            gat("act", blk("S", t), A("Y"), A("LA", 0, 8))
            cp(A("LU", 0, 128), A("STG", u1 + 384, u1 + 512))
            cp(blk("S", RO + t), A("STG", u1 + 256, u1 + 384), ON["Sb"])
        else:
            mm(A("W1", 0, 384), A("IB"), newnames, True, False)
            for l in range(3):
                mm(blk("W1", l), blk("OK", 6 * t + l), A("I4K"), False, l == 2)
            act(A("YQ"), A("W1", 0, 384))
            dma("sp", "yq", A("YQ"), [A("YQ")], [])
            cp(A("PI"), A("PF"))
            ts(A("PJ"), A("PI"), 9, None, OP.arith_shift_right)
            gtt(A("PE2"), A("PJ"), A("LS", 64, 88), A("DG"), OP.mult)
            mm(A("J1", 0, 384, p1=8), A("B8B"), A("PE2"), True, True)
            act(A("YP", p1=8), A("J1", 0, 384, p1=8))
            dma("act", "yp", A("YP", p1=8), [A("YP")], [])
            gat("act", A("GP"), A("Y"), A("LA", 0, 8))
            dma("act", ("ys", 512, 640), A("GP"), [A("GP")], [])
            dma("sp", ("ys", 0, 512), A("S", 0, 512), [A("S", 0, 512)], [])
            dma("act", ("ys", 640, 1152), A("S", 640, 1152), [A("S", 640, 1152)], [])
            dma("sp", "ym", "marks2", [A("S", 1280, 1792)], [])
            dma("sp", ("ys", 1152, 1280), A("SL"), [A("SL")], [])
    return ops


def deps_of(ops):
    hist = {}
    adds = lambda o: o["k"] == "mm" and not o["a"][3] and not o["a"][4]
    for n, o in enumerate(ops):
        dp = {}
        acc = [(r, False) for r in o["rd"]] + [(w, True) for w in o["wr"]]
        for r, isw in acc:
            bank = r[0] in BANKS
            for m, q, w in hist.get(r[0], []):
                if m == n:
                    continue
                oe = ops[m]["e"]
                if adds(o) and adds(ops[m]) and bank:
                    continue
                if bank and oe != o["e"]:
                    dp[m] = True
                elif (w or isw) and q[1] < r[2] and r[1] < q[2]:
                    dp[m] = dp.get(m, False) or not (oe == "pe" and o["e"] == "pe")
                elif bank and oe == "pe":
                    dp[m] = dp.get(m, False)
        for r, isw in acc:
            h = hist.setdefault(r[0], [])
            if isw and not adds(o):
                h[:] = [x for x in h if not (r[1] <= x[1][1] and x[1][2] <= r[2] and r[3] == 1 and cnt(r) == r[2] - r[1] and r[4] == 0 and r[5] == 128)]
            h.append((n, r, isw))
        o["dp"] = dp


def place(ops, keys, before, after):
    n = len(ops)
    left = [len(before[i]) for i in range(n)]
    ready = [0.0] * n
    start = [0.0] * n
    busy = dict((e, ([], [])) for e in ENG)
    todo = sorted(((keys[i], i) for i in range(n) if left[i] == 0), reverse=True)
    while todo:
        i = todo.pop()[1]
        c, st = ops[i]["c"], ready[i]
        b0, b1 = busy[ops[i]["e"]]
        lo = len(b0)
        while lo and b1[lo - 1] > st:
            lo -= 1
        while lo < len(b0) and b0[lo] < st + c - 1e-6:
            st = max(st, b1[lo])
            lo += 1
        b0.insert(lo, st)
        b1.insert(lo, st + c)
        start[i] = st
        new = False
        for j, gp in after[i]:
            if ready[j] < st + c + gp:
                ready[j] = st + c + gp
            left[j] -= 1
            if left[j] == 0:
                todo.append((keys[j], j))
                new = True
        if new:
            todo.sort(reverse=True)
    return start


def replay(order, calls):
    free, last = [0.0] * len(ENG), [-1] * len(ENG)
    seen, why = [0.0] * len(calls), [-1] * len(calls)
    for i in order:
        e, c, lat, before = calls[i]
        st, w = free[e], last[e]
        for m in before:
            if seen[m] > st:
                st, w = seen[m], m
        free[e] = st = st + c
        last[e] = i
        seen[i] = st + lat
        why[i] = w
    end = max(seen)
    return end, seen.index(end), why


def label(o):
    x = (o["wr"] + o["rd"])[0]
    return ([k for k, v in PACK.items() if v[0] == x[0] and v[1] <= x[1] < v[1] + SB[k][0]] + [x[0]])[0]


def kinds(ops):
    seen, names, out, prev, run = {}, {}, [], None, 0.0
    for o in ops:
        key = (o["st"], o["e"], label(o))
        run = run + o["c"] if o["e"] == "pe" and prev == key and run < 200.0 else 0.0
        if not run:
            seen[key] = seen.get(key, 0) + 1
        prev = key
        out.append(names.setdefault((o["st"] < 0, key[1], key[2], seen[key]), len(names)))
    return out, len(names)


def schedule(ops):
    deps_of(ops)
    n = len(ops)
    pred, anc = [], []
    for i, o in enumerate(ops):
        far, keep = 0, []
        for m in sorted(o["dp"], reverse=True):
            if not far >> m & 1:
                keep.append((m, o["dp"][m]))
                far |= anc[m] | (1 << m if o["dp"][m] else 0)
        pred.append(keep)
        anc.append(far)
    lat = [o.get("lat", 0.0) for o in ops]
    succ = [[] for _ in range(n)]
    for i in range(n):
        for m, need in pred[i]:
            succ[m].append((i, lat[m] + (PAR["hop"] if need else 0.0)))
    tail = [0.0] * n
    for i in range(n - 1, -1, -1):
        tail[i] = ops[i]["c"] + max([gp + tail[j] for j, gp in succ[i]] + [lat[i]])
    kind, nk = kinds(ops)
    rs = np.random.RandomState(PAR["seed"])

    same = {}
    for i in range(n):
        same.setdefault((kind[i], ops[i]["st"]), []).append(i)
    up = [[m for m, _ in pred[i]] for i in range(n)]
    down = [[j for j, _ in succ[i]] for i in range(n)]

    cases = [[(ENG.index(o["e"]), o["c"] * (1.0 if "lat" in o else scale), o.get("lat", 0.0) + hop + (far if o["k"] == "send" else 0.0),
               [m for m, need in pred[i] if need]) for i, o in enumerate(ops)] for scale, hop, far in PAR["cases"]]

    def judge(order):
        rp = [replay(order, c) for c in cases]
        return sum(r[0] for r in rp) / len(rp), order, rp

    def swap(order, xa, xb, ahead):
        lo, hi = order.index(xa[0]), order.index(xb[-1])
        if lo > hi:
            return
        seg = order[lo:hi + 1]
        need, took = set(xb if ahead else xa), set()
        for i in (reversed(seg) if ahead else seg):
            if i in need:
                took.add(i)
                need.update(up[i] if ahead else down[i])
        if any(i in took for i in (xa if ahead else xb)):
            return
        a, b = [i for i in seg if i in took], [i for i in seg if i not in took]
        order[lo:hi + 1] = a + b if ahead else b + a
    st = place(ops, [-x for x in tail], pred, succ)
    groups, queue = {}, dict((e, []) for e in ENG)
    for i in range(n):
        groups.setdefault((ops[i]["st"], ops[i]["e"], ops[i]["tag"] or label(ops[i])), []).append(i)
    for t in range(RO):
        for e in ENG:
            for word in ORDER[e].split():
                name, k = (word.split("*") + ["1"])[:2]
                g = groups.get((t, e, name), [])
                queue[e] += g[:int(k)]
                del g[:int(k)]
    for i in sorted((i for i in range(n) if ops[i]["st"] < 0), key=lambda i: -st[i]):
        q = queue[ops[i]["e"]]
        q.insert(([k for k, j in enumerate(q) if st[j] > st[i] - PAR["lead"]] + [len(q)])[0], i)
    listed, out, order, end = set(i for e in ENG for i in queue[e]), set(), [], [0.0] * n
    free = dict((e, 0.0) for e in ENG)

    def can(i):
        return all(m in out or (m not in listed and can(m)) for m in up[i])

    def put(i):
        for m in sorted(up[i]):
            if m not in out:
                put(m)
        end[i] = free[ops[i]["e"]] = max([free[ops[i]["e"]]] + [end[m] + lat[m] + PAR["hop"] for m in up[i]]) + ops[i]["c"]
        out.add(i)
        order.append(i)
    while any(queue.values()):
        able = [e for e in ENG if queue[e] and can(queue[e][0])]
        if not able:
            PAR.setdefault("stuck", []).append([(e, ops[queue[e][0]]["st"], ops[queue[e][0]]["tag"] or label(ops[queue[e][0]])) for e in ENG if queue[e]])
            able = [e for e in ENG if queue[e]][:1]
        i = queue[min(able, key=lambda e: max([free[e]] + [end[m] + lat[m] for m in up[queue[e][0]]]))].pop(0)
        if i not in out:
            put(i)
    for i in range(n):
        if i not in out:
            put(i)
    now = best = judge(order)
    for it in range(PAR["iters"]):
        _, i, why = now[2][rs.randint(len(now[2]))]
        held, then = [], {}
        while why[i] >= 0:
            if why[i] not in ops[i]["dp"] and kind[why[i]] != kind[i]:
                held.append((why[i], i))
            then[why[i]] = i
            i = why[i]
        if not held:
            continue
        a, b = held[rs.randint(len(held))]
        ahead = rs.rand() < 0.5
        for _ in range(rs.randint(4) * rs.randint(6)):
            if ahead and why[a] >= 0 and ops[why[a]]["e"] == ops[a]["e"]:
                a = why[a]
            elif not ahead and b in then and ops[then[b]]["e"] == ops[b]["e"]:
                b = then[b]
        order = list(now[1])
        d = ops[a]["st"] - ops[b]["st"]
        steps = range(RO) if min(ops[a]["st"], ops[b]["st"]) >= 0 and rs.rand() < 0.85 else [ops[b]["st"]]
        for t in steps:
            if (kind[a], t + d) in same and (kind[b], t) in same:
                swap(order, same[(kind[a], t + d)], same[(kind[b], t)], ahead)
        new = judge(order)
        if new[0] <= now[0] + PAR["warm"] * (1.0 - it / PAR["iters"]) * rs.rand():
            now = new
            if new[0] < best[0]:
                best = new
    return best[1], [r[0] for r in best[2]]


def plan():
    ops = build()
    order, total = schedule(ops)
    count = dict((e, 0) for e in ENG)
    known = dict((e, {}) for e in ENG)
    for i in order:
        o = ops[i]
        e = o["e"]
        waits = {}
        for m, need in o["dp"].items():
            if need:
                s, v = ops[m]["sig"]
                if known[e].get(s, 0) < v:
                    waits[s] = max(waits.get(s, 0), v)
        src = dict(((ops[m]["sig"]), m) for m in o["dp"])
        keep = []
        for s, v in waits.items():
            if not any(s2 != s and ops[src[(s2, v2)]]["kn"].get(s, 0) >= v for s2, v2 in waits.items()):
                keep.append((s, v))
        for s, v in waits.items():
            for s2, v2 in ops[src[(s, v)]]["kn"].items():
                known[e][s2] = max(known[e].get(s2, 0), v2)
            known[e][s] = max(known[e].get(s, 0), v)
        o["w"] = keep
        if o["k"] == "send":
            o["sig"] = (o["sem"], 8)
            o["kn"] = {}
        elif o["k"] == "dma":
            o["sig"] = (o["sem"], 16)
            o["kn"] = dict(known[e])
        else:
            count[e] += 1
            o["sig"] = ("c_" + e, count[e])
            o["kn"] = dict(known[e])
    return ops, order, total, count


PLAN = []


def rank_program(g, core, T, topo):
    rank = T.rank_of(core)
    if rank is None:
        return
    if not PLAN:
        PLAN.append(plan())
    ops, order, total, count = PLAN[0]
    nxt = T.cores[(rank + 1) % len(T.cores)]
    rid, pid = topo.addr(nxt, core)
    mask, nout = topo.mask(core, nxt), len(topo.engines(core, nxt))
    nin = len(topo.engines(T.cores[rank - 1], core))

    def wait(q, s, v):
        q.wait_ge(T.sem[s], nin if s[0] == "r" else v)
    Q = {"pe": g.tensor, "dve": g.vector, "act": g.scalar, "pool": g, "sp": g.sync}

    def ap(x):
        if not isinstance(x, tuple):
            return x
        if len(x) == 7:
            return T[x[0]][x[4]:x[5], :, x[6][0]:x[6][1]:x[6][2]]
        if x[0] == "Z0":
            return T["Z0"][x[4]:x[5], x[1] // 256, x[1] % 256:(x[2] - 1) % 256 + 1:x[3]]
        if x[3] == 1:
            return T[x[0]][x[4]:x[5], x[1]:x[2]]
        return T[x[0]][x[4]:x[5], x[1]:x[2]:x[3]]

    def ext(x):
        if x == "marks":
            return T["S"][15::16, 0:2048]
        if x == "marks2":
            return T["S"][15::16, 1280:1792]
        if isinstance(x, str):
            return T[x][:]
        if len(x) == 2:
            return T[x[0]][x[1]]
        if len(x) == 3:
            return T[x[0]][:, x[1]:x[2]]
        return ap(x)

    nsent = 0
    ends = []
    for i in order:
        o = ops[i]
        q, k, a = Q[o["e"]], o["k"], o["a"]
        for s, v in o["w"]:
            wait(q, s, v)
        if k == "send":
            g.remote_dma(ap(a[0]), ap(a[1]), T.sem[o["sem"]], T.sem["sent"], pid, rid, mask)
            nsent += nout
            ends.append(o["sig"])
            continue
        if k == "dma":
            q.dma_start(ext(a[0]), ext(a[1])).then_inc(T.sem[o["sem"]], 16)
            ends.append(o["sig"])
            continue
        if k == "cp":
            r = q.tensor_copy(ap(a[0]), ap(a[1]))
        elif k == "tt":
            r = q.tensor_tensor(ap(a[0]), ap(a[1]), ap(a[2]), a[3])
        elif k == "ts":
            if a[5] is None:
                r = q.tensor_scalar(ap(a[0]), ap(a[1]), ap(a[2]), None, a[4])
            else:
                r = q.tensor_scalar(ap(a[0]), ap(a[1]), ap(a[2]), ap(a[3]), a[4], a[5])
        elif k == "scan":
            r = q.tensor_tensor_scan(ap(a[0]), ap(a[1]), ap(a[2]), 0.0, a[3], a[4])
        elif k == "ms":
            r = q.memset(ap(a[0]), a[1])
        elif k == "gat":
            w = ap(a[1]).indirect(ap(a[2]))
            r = q.tensor_copy(ap(a[0]), w) if o["e"] == "dve" else q.activation(ap(a[0]), w, AF.Identity, ap(a[3]), ap(a[4]))
        elif k == "gtt":
            r = q.tensor_tensor(ap(a[0]), ap(a[1]).indirect(ap(a[2])), ap(a[3]), a[4])
        elif k == "act":
            if a[5] is None:
                r = q.activation(ap(a[0]), ap(a[1]), a[2], ap(a[3]), ap(a[4]))
            else:
                r = q.activation(ap(a[0]), ap(a[1]), a[2], ap(a[3]), ap(a[4]), accum_out=ap(a[5]))
        elif k == "mm":
            r = q.matmul(ap(a[0]), ap(a[1]), ap(a[2]), a[3], a[4])
        elif k == "iota":
            if SB[a[0][0]][1] == I32:
                r = q.iota(ap(a[0]), a[1], a[2], a[3])
            else:
                r = q.iota(ap(a[0]), a[1], a[2], a[3], allow_small_or_imprecise_dtypes=True)
        elif k == "asel":
            r = q.affine_select(ap(a[0]), ap(a[1]), a[2], a[3], a[4], a[5], a[6])
        r.then_inc(T.sem[o["sig"][0]], 1)
    for s, v in ends:
        wait(g, s, v)
    g.wait_ge(T.sem["sent"], nsent)
    for e in ENG[:4]:
        g.wait_ge(T.sem["c_" + e], count[e])
